import numpy as np, ml_dtypes
CORES = [24,25,26,27,28,29,30,31]
N = 8
BF = ml_dtypes.bfloat16
def gentries(a):
    return np.ascontiguousarray(a.reshape(8, 16, -1).transpose(0, 2, 1)).reshape(8, -1)
def gtable(e):
    e = np.asarray(e); return np.ascontiguousarray(e.reshape(8, -1, 16).transpose(0, 2, 1)).reshape(128, -1).astype(np.int32)
W, L, C, VIS, SLOT, Q = 4096, 3072, 192, 3, 128, 11
GM = 255 * L
def cuts(rng, tot, k):
    return np.diff(np.concatenate([[0], np.sort(rng.integers(0, tot + 1, k - 1)), [tot]]))
def some(rng, tot, k):
    n = np.zeros(C, np.int64); n[rng.permutation(C)[:k]] = cuts(rng, tot, k)
    return n
def pack(x, o, n, gt):
    return {"aud": np.ascontiguousarray(x.reshape(N, 128, W)).astype(np.float32).astype(BF), "spots": np.stack([gtable(a) for a in o]),
            "lens": np.ascontiguousarray(n).astype(np.int32), "gua": np.ascontiguousarray(gt.reshape(N, 128, C)).astype(np.int32)}
def contrast(rng, sizes):
    st = rng.choice(np.array(sizes), (N, 8, 1, 1)); tot = rng.integers(13 * L // 16, 15 * L // 16, (N, 8))
    for g in range(8):
        q = int(rng.integers(0, N)); st[q, g] = sizes[-1]; st[(q + 1) % N, g] = sizes[0]; tot[(q + 1) % N, g] = L
    return st, tot
def parts(rng):
    st, tot = contrast(rng, [0.45, 0.6, 0.8, 1.0])
    x = (255 * st * (0.25 + 0.75 * rng.random((N, 8, 1, W))) * (0.5 + 0.5 * rng.random((N, 8, 16, W)))).astype(np.int64)
    o = rng.integers(0, W, (N, 8, L))
    n = np.stack([np.stack([cuts(rng, int(tot[r, g]), C) for g in range(8)]) for r in range(N)])
    gt = 84 * (n[:, :, None] - 2 + 5 * rng.random((N, 8, 1, C))) * (0.85 + 0.3 * rng.random((N, 8, 16, C)))
    return x, o, n, np.minimum(np.maximum(gt, 0).astype(np.int64), GM)
def exact(rng, xg, o, n, R, S, low=False):
    tot = int(np.add.reduce(n)); end = np.add.accumulate(n); beg = end - n; own = np.repeat(np.arange(C), n)
    cs = np.concatenate([np.zeros((16, 1), np.int64), np.add.accumulate(xg[:, o[:tot]], axis=1)], axis=1)
    who = rng.permutation(C)
    if low: who = who[np.argsort(n[who], kind="stable")]
    short = np.zeros(C, bool); short[who[:S]] = True
    pool = np.nonzero(~short[own])[0]; cut = np.bincount(own[rng.permutation(pool)[:R]], minlength=C)
    coin = rng.random(C) < 0.5; pr = np.argsort(rng.random((16, C)), axis=0); lift = rng.choice(np.array([1, 40, GM]), C)
    hold = cs[:, end - cut] - cs[:, beg]; full = cs[:, end] - cs[:, beg]
    v = hold + lift * (coin & (pr < Q - 1)); u = np.where(pr < Q, full + 1, np.where(coin, 0, full + 1))
    return np.minimum(np.where(short, u, v), GM)
def hunger(rng, x, o, n, gt, g):
    for r in range(N):
        pr = np.argsort(rng.random((16, C)), axis=0); u = rng.integers(1, 512, (1, C)); k = rng.integers(Q, 17, C)
        o[r, g] = rng.integers(0, W, L); n[r, g] = 0
        if r % 2 == 0:
            c = int(rng.integers(0, C)); n[r, g, c] = L; k[c] = 0
        if r % 4 == 3: k[rng.permutation(C)[int(rng.integers(1, 4)):]] = Q - 1
        gt[r, g] = u * (pr < k)
def filled(rng, x, o, n, gt, g):
    xv = x[:, g]
    for r in range(N):
        bl = r + N * rng.permutation(W // N); pr = np.argsort(rng.random((16, C)), axis=0)
        o[r, g] = bl[rng.integers(0, W // N, L)]; n[r, g] = 0; gt[r, g] = 0
        if r % 4 == 0:
            top = rng.integers(200, 256, (16, W // N))
            for p in range(N): xv[p][:, bl] = top if p == r else top >> 2
            who = np.sort(rng.permutation(C)[:7]); n[r, g, who[1:]] = L // 8 + rng.integers(0, 16, 6)
            n[r, g, who[0]] = L - int(np.add.reduce(n[r, g]))
            end = np.add.accumulate(n[r, g])
            cs = np.concatenate([np.zeros((16, 1), np.int64), np.add.accumulate(xv[r][:, o[r, g]], axis=1)], axis=1)
            full = cs[:, end] - cs[:, end - n[r, g]]
            for j in range(6):
                c = int(who[j + 1])
                gt[r, g][:, c] = np.where(pr[:, c] < Q, full[:, c] + 1, 0) if j % 2 == 0 else np.where(pr[:, c] < Q - 1, GM, full[:, c])
        if r % 4 == 1:
            xv[:, :, bl] = 255; n[r, g, 0] = L
            gt[r, g] = (pr < Q) * rng.integers(0, 300, (1, C)); gt[r, g][:, 0] = GM
        if r % 4 == 2:
            xv[:, :, bl] = 0; xv[(r + VIS - 1) % N][:, bl] = 255
            c = int(rng.integers(0, C)); n[r, g, c] = L // 2; gt[r, g][:, c] = 255
        if r % 4 == 3:
            n[r, g] = cuts(rng, L, C); gt[r, g] = GM
def few(rng, x, o, n, gt, g):
    xv = x[:, g]; sh = int(rng.integers(0, 4))
    for r in range(N):
        v = (r + sh) % 4; u = r + N * rng.permutation(W // N)[:3]; low = rng.integers(1, 64, (16, 3)); pr = np.argsort(rng.random(16))
        xv[:, :, u] = low; goal = np.add.reduce(low[:, :v], axis=1); a, b = rng.permutation(C)[:2]
        if v: xv[(r + 1) % N][:, u[0]] = goal
        n[r, g] = 0; n[r, g, a] = v; o[r, g, :v] = u[:v]
        gt[r, g] = 0; gt[r, g][:, a] = goal; gt[r, g][:, b] = pr < Q
def setup_inputs(rng):
    return pack(*parts(rng))
def setup_inputs_spread(rng):
    st, tot = contrast(rng, [0.25, 0.5, 1.0])
    x = np.minimum((st * np.exp2(8 * rng.random((N, 8, 1, W))) * (0.25 + 0.75 * rng.random((N, 8, 16, W)))).astype(np.int64), 255)
    o = rng.integers(0, W, (N, 8, L)); n = np.zeros((N, 8, C), np.int64)
    for r in range(N):
        for g in range(8):
            k = int(tot[r, g]); c = np.sort((k * rng.random(C - 1) ** 3).astype(np.int64))
            n[r, g] = np.diff(np.concatenate([[0], c, [k]]))
    m = n[:, :, None]; e = rng.random((N, 8, 1, C))
    gt = np.where(m > 0, 17 * m * np.exp2(-3 + 3.7 * e), np.exp2(8 * e) - 1) * (0.7 + 0.6 * rng.random((N, 8, 16, C)))
    gt = np.where(rng.random((N, 8, 1, C)) < 0.0625, np.exp2(20 * rng.random((N, 8, 16, C))), gt)
    return pack(x, o, n, np.minimum(gt.astype(np.int64), GM))
def setup_inputs_ends(rng):
    x = 255 * ((rng.random((N, 8, 1, W)) < 0.6) ^ (rng.random((N, 8, 16, W)) < 0.05)).astype(np.int64)
    o = np.zeros((N, 8, L), np.int64); n = np.zeros((N, 8, C), np.int64); gt = np.zeros((N, 8, 16, C), np.int64)
    for r in range(N):
        vs = rng.permutation(5)
        for g in range(8):
            one = int(rng.integers(0, 2)); lone = (r + g) % 2 == 0
            x[r, g, :, 0] = 255 if lone else 255 * one; x[r, g, :, W - 1] = 255 if lone else 255 * (1 - one)
            pr = np.argsort(rng.random((16, C)), axis=0); live = rng.random(C) < 0.3; live[C - C // 16:] = False
            k = rng.integers(0, Q, C); k[C - C // 16:] = rng.integers(Q, 17, C // 16)
            ends = rng.choice(np.array([0, W - 1]), L)
            if lone: o[r, g] = ends
            else:
                o[r, g] = np.where(rng.random(L) < 0.8, ends, rng.integers(0, W, L)); s = np.argsort(rng.random(C) - 0.5 * live)[:3 * C // 10]
                n[r, g, s] = cuts(rng, 7 * L // 8, len(s))
            j = rng.integers(1, 4, C) if lone else 1 + (rng.random(C) * (n[r, g] + 1)).astype(np.int64)
            gt[r, g] = np.where(live, 255 * j, GM * (pr < k))
            if lone:
                c = int(rng.choice(np.array([0, C // 2 + 1, C - 1]))); v = int(vs[g // 2])
                if r == N - 1 and g == 7: c = C - 1; v = 0
                if r == 0 and g == 0: v = 1
                n[r, g, c] = L; h = pr[:, c]
                gt[r, g, :, c] = (GM * (h >= 0), (GM - 255) * (h >= 0), GM * (h < Q - 1), GM * (h < Q), 255 * (h >= 0))[v]
    return pack(x, o, n, np.minimum(gt, GM))
def setup_inputs_corners(rng):
    assert SLOT + 4 <= C
    x, o, n, gt = parts(rng)
    cases = [(SLOT, SLOT, L), (SLOT + 1, SLOT + 1, L - SLOT), (SLOT - 1, SLOT, L - SLOT), (1, 1, L), (0, C, L), (-1, 0, 0), (SLOT, 1, L), (3 * SLOT, SLOT + 1, L - SLOT + 1)]
    for r in range(0, N, 2):
        sh = int(rng.integers(0, 8)); q = r + 1
        for g in range(8):
            d, e, tot = cases[(g + sh) % 8]; s = int(rng.integers(0, C // 8))
            if d < 0: n[r, g] = some(rng, L, C - C // 8); gt[r, g] = exact(rng, x[r, g], o[r, g], n[r, g], L, C // 8, True)
            else: n[r, g] = cuts(rng, 15 * L // 16, C); gt[r, g] = exact(rng, x[r, g], o[r, g], n[r, g], s + d, s)
            k = 0 if e == 0 or e == C else int(rng.integers(0, 4))
            n[q, g] = cuts(rng, tot, C); gt[q, g] = exact(rng, x[q, g], o[q, g], n[q, g], k, e + k)
    return pack(x, o, n, gt)
def setup_inputs_crowd(rng):
    x, o, n, gt = parts(rng)
    for r in range(N):
        w = W - N + r
        for g in range(8):
            role = (g - r) % 8; o[r, g] = w
            if role in (1, 3): o[r, g, int(rng.integers(0, L))] = int(rng.integers(4, W - N))
            if role in (6, 7): o[r, g] = rng.choice(np.array([0, 1, 2, 3, w]), L)
            if role in (4, 5):
                n[r, g] = 0; c = int(rng.integers(0, C)); n[r, g, c] = L
                x[r, g, :, w] = 0; x[(r + 1) % N, g, :, w] = 255
                gt[r, g] = 255 * rng.integers(0, 2, (1, C)); gt[r, g, :, c] = 255 + (role == 5)
                continue
            n[r, g] = cuts(rng, L, C) if role < 2 else some(rng, L, C - C // 4) if role < 4 else cuts(rng, 7 * L // 8, C)
            R, S = ((0, C), (0, C - 1), (L, C // 4), (L - 1, C // 4), (0, 0), (0, 0), (C // 4, C // 4), (C // 8 + SLOT, C // 8))[role]
            gt[r, g] = exact(rng, x[r, g], o[r, g], n[r, g], R, S, role in (2, 3))
    two = rng.permutation(8)[:2]
    hunger(rng, x, o, n, gt, int(two[0])); filled(rng, x, o, n, gt, int(two[1]))
    return pack(x, o, n, gt)
def setup_inputs_calm(rng):
    x = np.repeat(rng.integers(100, 256, (1, 8, 16, W)), N, axis=0); base = x[0].copy()
    o = rng.integers(0, W, (N, 8, L)); n = np.zeros((N, 8, C), np.int64); gt = np.zeros((N, 8, 16, C), np.int64)
    for r in range(N):
        for g in range(8):
            bl = r + N * rng.permutation(W // N); R = rng.integers(0, 4, N); S = rng.integers(0, 4, N); R[1] = g % 4; S[1] = (g // 4 + r) % 4
            tau = np.concatenate([np.repeat(np.arange(N), R), np.repeat(np.arange(N), S)]); m = len(tau); h = int(np.add.reduce(R)); rel = np.arange(m) < h
            sc = rng.permutation(C)[:m]; a = bl[:m]; b = bl[m:m + h]; rest = bl[m + h:]
            pr = np.argsort(rng.random((16, m)), axis=0); xv = x[:, g]; xv[:, :, b] = 1
            for p in range(N):
                late = (p - r) % N >= tau
                xv[p][:, a] = base[g][:, a] - (pr < Q - (late == rel))
            tot = 3 * L // 4; nb = cuts(rng, tot, C); nm = rest[rng.integers(0, len(rest), tot)]; end = np.add.accumulate(nb); beg = end - nb
            cs = np.concatenate([np.zeros((16, 1), np.int64), np.add.accumulate(base[g][:, nm], axis=1)], axis=1); full = cs[:, end] - cs[:, beg]
            gt[r, g] = full + ((rng.random(C) < 0.5) & (np.argsort(rng.random((16, C)), axis=0) < Q - 1)); gt[r, g][:, sc] = full[:, sc] + base[g][:, a]
            names = np.concatenate([nm, a, b]); camp = np.concatenate([np.repeat(np.arange(C), nb), sc, sc[:h]])
            o[r, g, :len(names)] = names[np.argsort(camp, kind="stable")]; n[r, g] = np.bincount(camp, minlength=C)
    few(rng, x, o, n, gt, int(rng.integers(0, 8)))
    return pack(x, o, n, gt)
def check_inputs(d):
    bad = []
    for k, lo, hi in (("aud", 0, 255), ("spots", 0, W - 1), ("lens", 0, L), ("gua", 0, GM)):
        a = np.asarray(d[k]).astype(np.float64)
        if not np.all((a >= lo) & (a <= hi)): bad.append("range of " + k)
    a = np.asarray(d["aud"]).astype(np.float64)
    if np.any(a != np.floor(a)): bad.append("whole numbers in aud")
    if np.max(np.add.reduce(np.asarray(d["lens"]).astype(np.int64), axis=2)) > L: bad.append("sum of lens in a group")
    return bad
def reference(aud, spots, lens, gua):
    x = aud.astype(np.float32).astype(np.int64).reshape(N, 8, 16, W); gt = gua.astype(np.int64).reshape(N, 8, 16, C)
    nm = np.stack([gentries(a) for a in spots]).astype(np.int64); ln = lens.astype(np.int64)
    for t in range(VIS):
        kept, sent = {}, {}
        for r in range(N):
            p = (r + t) % N
            for g in range(8):
                k = ln[r, g]; tot = int(np.add.reduce(k)); o = nm[r, g, :tot]; own = np.repeat(np.arange(C), k)
                end = np.add.accumulate(k); beg = end - k
                cs = np.concatenate([np.zeros((16, 1), np.int64), np.add.accumulate(x[p, g][:, o], axis=1)], axis=1)
                before = cs[:, :tot] - cs[:, beg[own]]; full = cs[:, end] - cs[:, beg]
                need = np.add.reduce((before < gt[r, g][:, own]).astype(np.int64), axis=0) >= Q
                short = np.nonzero(np.add.reduce((full < gt[r, g]).astype(np.int64), axis=0) >= Q)[0]
                rel = o[~need]; a = min(len(rel), len(short))
                more = np.full(C, -1, np.int64); more[short[:a]] = rel[:a]
                kept[r, g] = (o[need], own[need], more, short[a:]); sent[r, g] = rel[a:a + SLOT]
        new, nl = np.full((N, 8, L), -1, np.int64), np.zeros((N, 8, C), np.int64)
        for r in range(N):
            for g in range(8):
                o, own, more, rest = kept[r, g]; come = sent[(r - 1) % N, g]; a = min(len(come), len(rest))
                more[rest[:a]] = come[:a]; c = np.nonzero(more >= 0)[0]
                camp = np.concatenate([own, c]); w = np.argsort(camp, kind="stable")[:L]
                new[r, g, :len(w)] = np.concatenate([o, more[c]])[w]; nl[r, g] = np.bincount(camp[w], minlength=C)
        nm, ln = new, nl
    return {"yo": np.stack([gtable(a) for a in nm]).astype(np.float32), "yn": ln.astype(np.float32)}

@@ -1,0 +1,653 @@
+from concourse.mybir import AluOpType as A, AxisListType, ActivationFunctionType as AF
+
+W, L, C = 4096, 3072, 192
+BIG = 16384.0
+XB = 8 + L
+ZN = XB + 3 * C
+NULLC = ZN + 7
+TB = ZN + 8
+NREL = 320
+NTW = TB + 6 * NREL
+
+F_T = dict(pc=8, g16=8, sc=8, g15=8, p16=8, s15=8, s8k=8, s8z=8, e1=8, sm15=8, i143=144, j16=128, blk=128, blks=128, trl=128,
+           trg=128, p15=128, rep=128, mk=384, md=384, md8=192, ones=320, l8f=208, b8=208, bd1=208, bd2=192, cd=16, len=16,
+           t1=24, t2=24, t3=24, dum=24, negg=192, sg=192, stc=24, sv=24, c3=16, ks=16, kd=192, k0=24, k1=24, k2=24,
+           ts=48, tp=48, cap=48, kq=48, mx=48, ns=48, nsc=48, pa=24, pb=16, th0=192, th1=192, u1=192, ff=24, yy=24, rx2=24,
+           ro=24, cr=16, zo=24, oo=24, vv=24, ee=384, v1=320, v2=320, rr=8, rm=24, isin=16, aw=8, t4=24, sv0=16, sm4k=8, idh=128,
+           gi0=16, g1=16, xo=16, gg=192, gn=192, gd=192, en0=16, ea=16, ms0=8, ms1=8, ms2=8, vrep=384, msk=384, jd=192, jadj=192,
+           npad=224, tt=416, lq=16, tot=8, el=192, ynr=192, ta=192, tb=192, z16=16, bb=24)
+H_T = dict(big=144, hp=128, hn=128, trlh=128, trgh=128, nid=128, ss=16, zb=208, km=208, m512=192, gz=192, hl=384, fd=200, cx=200,
+           h1=208, h2=208, fa=384, fs=192, cs=16, b15=24)
+U_T = dict(so=192, kb=16, sto=16, ex=24, pd=16, ou=24, rp=24, gi=16, xu=16, eb=16, eau=16, fo=192, tg=16)
+I_T = dict(pi=8, pj=8, l8=192, sp=192, gu=192, hli=384, bi=208, kbi=16, exi=24, rpi=24, bbi=24, nn=192)
+
+
+def _alloc(d):
+    pos, at = {}, 0
+    for k, n in d.items():
+        pos[k] = (at, n)
+        at += (n + 15) // 16 * 16
+    return pos, at
+
+
+POOL = {}
+SCRATCH = {}
+for _n, _d, _t in (("pf", F_T, "float32"), ("ph", H_T, "bfloat16"), ("pu", U_T, "uint16"), ("pi32", I_T, "int32")):
+    _p, _w = _alloc(_d)
+    SCRATCH[_n] = ("sbuf", [128, _w], _t)
+    for _k, _v in _p.items():
+        POOL[_k] = (_n, _v[0], _v[1])
+for _t in range(3):
+    SCRATCH["au%d" % _t] = ("sbuf", [128, W + 16], "bfloat16")
+    SCRATCH["yy%d" % _t] = ("sbuf", [128, C + L], "float32")
+    SCRATCH["mi%d" % _t] = ("sbuf", [128, 4], "float32")
+for _t in range(2):
+    SCRATCH["xx%d" % _t] = ("sbuf", [128, L + 2 * C], "float32")
+    SCRATCH["fl%d" % _t] = ("sbuf", [128, L], "bfloat16")
+SCRATCH["mm"] = ("sbuf", [128, L + C], "bfloat16")
+SCRATCH["on"] = ("sbuf", [128, L], "bfloat16")
+SCRATCH["selt"] = ("sbuf", [128, 2048], "bfloat16")
+SCRATCH["nt"] = ("sbuf", [128, NTW], "float32")
+SCRATCH["wr"] = ("sbuf", [128, 2 * NREL + L + 2 * C], "float32")
+for _t in range(8):
+    SCRATCH["ps%d" % _t] = ("psum", [128, 512], "float32")
+
+SEMAPHORES = (["qv", "qa", "qp", "qg", "sent", "dl", "dsp", "dg", "da0", "da1", "do", "dn", "ra1", "ra2"]
+              + ["rr%d" % t for t in range(3)] + ["rm%d" % t for t in range(3)])
+
+GCH = 512
+SCH = 1024
+DVE_G = {0: (0, 1, 2), 1: (), 2: ()}
+FIN_V = (0, 1, 2)
+LAG_SAME, LAG_CROSS = 50.0, 90.0
+PLAN = {}
+
+
+def _ops(g, T, topo, core):
+    ops, tag = [], [0]
+    V, S, P = g.vector, g.scalar, g.tensor
+    N = len(T.cores)
+    r = T.rank_of(core)
+
+    def X(name, a=0, b=None, st=1, p=128):
+        if name in POOL:
+            buf, o, n = POOL[name]
+        else:
+            buf, o, n = name, 0, SCRATCH[name][1][1]
+        b = n if b is None else b
+        ap = T[buf][0:p, o + a:o + b:st] if st != 1 else T[buf][0:p, o + a:o + b]
+        return (ap, [(buf, o + a, o + b)], (b - a + st - 1) // st, SCRATCH[buf][2], SCRATCH[buf][0])
+
+    def IND(win, off):
+        return (win[0].indirect(off[0]), win[1] + off[1], 16 * off[2], win[3], "ind", win[1], off[1])
+
+    def add(q, emit, rd, wr, cost, lat=0.0, sem=None, cnt=1):
+        ops.append((q, emit, rd, wr, cost, lat, sem, cnt, tag[0]))
+
+    def split(out, ins):
+        rd = []
+        for i in ins:
+            if isinstance(i, tuple):
+                rd += i[1]
+        if out[4] == "ind":
+            return rd + out[6], out[5]
+        return rd, out[1]
+
+    def vcost(out, ins, two=False):
+        n = out[2]
+        if out[4] == "ind":
+            return 50 + 3.8 * n
+        if ins and ins[0][4] == "ind":
+            return 50 + 1.56 * n
+        f = 2.0 if two else (0.5 if all(x[3] == "bfloat16" for x in [out] + ins) else 1.0)
+        return 20 + max(64, f * n)
+
+    def ap(x):
+        return x[0] if isinstance(x, tuple) else x
+
+    def cp(out, i):
+        rd, wr = split(out, [i])
+        add("v", lambda: V.tensor_copy(out[0], i[0]), rd, wr, vcost(out, [i]))
+
+    def tt(out, a, b, op):
+        rd, wr = split(out, [a, b])
+        add("v", lambda: V.tensor_tensor(out[0], a[0], b[0], op), rd, wr,
+            vcost(out, [a, b], a[4] != "psum" and b[4] != "psum"))
+
+    def ts(out, a, s1, op0, s2=None, op1=None):
+        rd, wr = split(out, [a, s1, s2])
+        if op1 is None:
+            add("v", lambda: V.tensor_scalar(out[0], a[0], ap(s1), None, op0), rd, wr, vcost(out, [a]))
+        else:
+            add("v", lambda: V.tensor_scalar(out[0], a[0], ap(s1), ap(s2), op0, op1), rd, wr, vcost(out, [a]))
+
+    def scan(out, d0, d1, init, op0, op1):
+        rd, wr = split(out, [d0, d1, init])
+        add("v", lambda: V.tensor_tensor_scan(out[0], d0[0], d1[0], ap(init), op0, op1), rd, wr, vcost(out, [d0, d1]))
+
+    def ms(out, c):
+        add("v", lambda: V.memset(out[0], c), [], out[1], vcost(out, []))
+
+    def tr(out, i):
+        add("v", lambda: V.transpose(out[0], i[0]), i[1], out[1], vcost(out, [i]))
+
+    def act(out, i, fn=AF.Identity, bias=0.0, scale=1.0):
+        rd, wr = split(out, [i, bias, scale])
+        c = 65 + 1.56 * out[2] if i[4] == "ind" else 60 + max(64, out[2])
+        add("a", lambda: S.activation(out[0], i[0], fn, bias=ap(bias), scale=ap(scale)), rd, wr, c)
+
+    def gat(eng, out, i):
+        if eng == "v":
+            cp(out, i)
+        else:
+            act(out, i)
+
+    def mm(groups):
+        rd, wr, c = [], [], 60.0
+        for out, l in groups:
+            wr += out[1]
+            for a, b in l:
+                rd += a[1] + b[1]
+                c += 0.5 * max(64, b[2]) * (4 if b[3] == "float32" else 1)
+
+        def emit():
+            ins = None
+            for out, l in groups:
+                for k, (a, b) in enumerate(l):
+                    ins = P.matmul(out[0], a[0], b[0], k == 0, k == len(l) - 1)
+            return ins
+        add("p", emit, rd, wr, c)
+
+    def iota(out, pat, base, cm):
+        if out[3] == "int32":
+            add("g", lambda: g.iota(out[0], pat, base, cm), [], out[1], 130 + 2 * out[2])
+        else:
+            add("g", lambda: g.iota(out[0], pat, base, cm, allow_small_or_imprecise_dtypes=True), [], out[1], 130 + 2 * out[2])
+
+    def fill(out, c):
+        iota(out, [[0, out[2]]], c, 0)
+
+    def asel(out, i, pat, op, base, cm):
+        add("g", lambda: g.affine_select(out[0], i[0], pat, op, 0.0, base, cm), i[1], out[1], 170 + 2 * out[2])
+
+    def dma(q, out, i, rd, wr, sem, nbytes, extra=0.0):
+        e = g.sync if q == "s" else g.scalar
+        add(q, lambda: e.dma_start(out, i), rd, wr, 60.0, 1700 + extra + nbytes / 300.0, sem, 16)
+
+    def remote(dst_rank, out, i, sem, nbytes, extra=0.0):
+        d = T.cores[dst_rank % N]
+        rid, pid, _ = topo.addr(d)
+        m = topo.mask(core, d)
+        k = len(topo.engines(core, d))
+        add("g", lambda: g.remote_dma(out[0], i[0], T.sem[sem], T.sem.sent, pid, rid, m), i[1], out[1], 400.0,
+            1800 + extra + nbytes / 250.0, sem, k)
+
+    def diag(out, src):
+        scan(out, X("mk", 0, src[2]), src, 0.0, A.add, A.min)
+
+    def D16(name, n):
+        return X(name, 15, n, 16)
+
+    def sel(s):
+        return X("big", 15 - s, 143 - s)
+
+    def count(out, name, a, b):
+        mm([(out, [(sel(s), X(name, a + s, b, 16)) for s in range(16)])])
+
+    col = lambda n: X(n, 0, 1)
+
+    dma("s", T.pi32[0:8, POOL["l8"][1]:POOL["l8"][1] + C], T.lens[:], [], X("l8")[1], "dl", 6144)
+    dma("s", X("sp")[0], T.spots[:], [], X("sp")[1], "dsp", 98304)
+    dma("a", X("au0", 0, W // 2)[0], T.aud[:, 0:W // 2], [], X("au0", 0, W // 2)[1], "da0", 524288, 500)
+    dma("s", X("gu")[0], T.gua[:], [], X("gu")[1], "dg", 98304, 300)
+    dma("a", X("au0", W // 2, W)[0], T.aud[:, W // 2:W], [], X("au0", W // 2, W)[1], "da1", 524288, 2300)
+    remote(r - 1, X("au1", 0, W), X("au0", 0, W), "ra1", 1 << 20, 1500)
+    remote(r - 2, X("au2", 0, W), X("au0", 0, W), "ra2", 1 << 20, 5500)
+
+    iota(X("pi", 0, 1), [[0, 1]], 0, 1)
+    iota(X("i143"), [[1, 144]], 0, 0)
+    iota(X("j16"), [[16, 8], [0, 16]], 0, 0)
+    iota(X("md"), [[0, 24], [1, 16]], 0, 0)
+    cp(col("pc"), X("pi", 0, 1))
+    ts(X("pj", 0, 1), X("pi", 0, 1), 15, A.bitwise_and)
+    cp(col("sc"), X("pj", 0, 1))
+    ts(X("rep"), X("j16"), 0.0625, A.mult, col("pc"), A.is_equal)
+    tt(col("g16"), col("pc"), col("sc"), A.subtract)
+    ts(X("mk"), X("md"), col("sc"), A.is_equal, 16777216.0, A.mult)
+    ms(X("l8f"), 0.0)
+    ms(X("mm"), 1.0)
+    ms(X("zb"), 0.0)
+    ts(X("big"), X("i143"), -15.0, A.add, col("g16"), A.is_equal)
+    ts(X("blk"), X("j16"), col("g16"), A.is_equal)
+    act(X("blks"), X("blk"), scale=1.0 / 16777216.0)
+    act(X("hp"), X("blk"), scale=0.5)
+    act(X("hn"), X("blk"), scale=-0.5)
+    asel(X("trl"), X("blk"), [[1, 128]], A.is_gt, 0, -1)
+    asel(X("trg"), X("blk"), [[-1, 128]], A.is_ge, 0, 1)
+    act(X("trlh"), X("trl"))
+    act(X("trgh"), X("trg"))
+    asel(X("p15"), X("blk"), [[-16, 8], [0, 16]], A.is_equal, -15, 1)
+    asel(X("idh"), X("blk"), [[-1, 128]], A.is_equal, 0, 1)
+    act(X("nid"), X("idh"), scale=-BIG)
+    act(col("s8k"), col("sc"), scale=8192.0)
+    act(col("s8z"), col("sc"), scale=-8192.0, bias=-4096.0)
+    act(col("g15"), col("g16"), scale=-BIG, bias=BIG)
+    act(col("sm15"), col("sc"), bias=-15.0)
+    act(col("sm4k"), col("sc"), scale=-4096.0)
+    act(X("md8"), X("md", 0, C), scale=8192.0)
+    act(X("m512"), X("md", 0, C), scale=512.0)
+    act(X("ones"), X("md", 0, NREL), bias=1.0, scale=0.0)
+    for k in range(6):
+        fill(X("on", 512 * k, 512 * k + 512), 1)
+    for h in range(4):
+        asel(X("selt", 512 * h, 512 * h + 512), X("on", 0, 512), [[1, 4], [16, 8], [0, 16]], A.is_equal, 4 * h, -1)
+    iota(X("jd"), [[16, C]], 0, 1)
+    ts(X("cd", 0, 12), X("jd", 0, 12), col("g16"), A.subtract)
+    iota(X("exi"), [[1, 24]], 0, 0)
+    cp(X("ex"), X("exi"))
+    act(X("dum", 0, 12), X("cd", 0, 12), bias=float(L))
+    act(X("dum", 12, 24), X("cd", 0, 12), bias=float(L + C))
+    act(X("c3", 0, 12), X("cd", 0, 12), scale=3.0)
+    for t in range(3):
+        fill(X("au%d" % t, W, W + 16), 0)
+    act(X("xx0", L, L + 2 * C), X("md"), scale=0.0)
+    fill(X("xx1", L, L + 2 * C), 0)
+    for t in range(3):
+        fill(X("wr", NREL * t, NREL * t + NREL), 0)
+    fill(X("nt", 0, 8), 0)
+    fill(X("nt", XB, ZN), 0)
+    fill(X("nt", ZN, ZN + 1), W)
+    fill(X("nt", ZN + 1, TB), -1)
+    for nm, a, b in (("fd", 192, 200), ("cx", 0, 1), ("cr", 0, 1), ("cs", 0, 1), ("z16", 0, 16), ("cap", 12, 24),
+                     ("npad", 0, 16), ("npad", 208, 224)):
+        fill(X(nm, a, b), 0)
+
+    cp(X("so"), X("sp"))
+    cp(X("l8f", 1, 193, p=8), X("l8", p=8))
+    scan(X("b8", p=8), X("l8f", p=8), X("zb", p=8), 0.0, A.add, A.add)
+    mm([(X("ps6", 0, 208), [(X("rep", p=8), X("b8", p=8))])])
+    diag(X("bd1"), X("ps6", 0, 208))
+    diag(X("bd2"), X("ps6", 1, 193))
+    st, ln, cd = D16("bd1", C), X("len", 0, 12), X("cd", 0, 12)
+    tt(ln, D16("bd2", C), st, A.subtract)
+    ts(X("t1", 0, 12), ln, 1.0, A.is_lt, BIG, A.mult)
+    tt(X("t2", 0, 12), X("t1", 0, 12), st, A.add)
+    tt(X("t3", 0, 12), X("t2", 0, 12), X("dum", 0, 12), A.min)
+    cp(X("sto", 0, 12), X("t3", 0, 12))
+    cp(IND(X("mm"), X("sto", 0, 12)), X("zb", 0, C))
+    ts(X("negg"), X("gu"), -1.0, A.mult)
+    for t in range(3):
+        act(X("yy%d" % t, 0, C), X("negg"))
+    cp(X("bi"), X("ps6", 0, 208))
+    ts(X("bi"), X("bi"), 15, A.bitwise_and)
+    ts(X("km"), X("bi"), col("sc"), A.is_gt)
+    cp(X("kbi", 0, 13), D16("bd1", 208))
+    ts(X("kbi", 0, 13), X("kbi", 0, 13), 4, A.logical_shift_right)
+    cp(X("kb", 0, 13), X("kbi", 0, 13))
+    act(X("gz"), X("negg"), AF.Sign, bias=-0.5, scale=-1.0)
+    count(X("ps2", 0, 12), "gz", 0, C)
+    ts(X("t1", 0, 12), X("ps2", 0, 12), 5.0, A.is_gt)
+    act(X("t4", 0, 12), ln, scale=0.5, bias=col("sm4k"))
+    tt(X("ks", 0, 12), X("t1", 0, 12), X("t4", 0, 12), A.add)
+    act(X("stc", 0, 12), st, bias=191.0)
+    act(X("stc", 12, 24), cd, scale=1.0 / 8192.0)
+    act(X("sv", 0, 12), cd, scale=16387.0, bias=16384.0 + XB - 1)
+    act(X("t4", 12, 24), cd, scale=16384.0, bias=8192.0 + 7)
+    tt(X("sv", 12, 24), X("t4", 12, 24), st, A.add)
+    act(X("sv0", 0, 12), st, bias=7.0)
+    for u in range(2):
+        act(X("ts", 24 + 12 * u, 36 + 12 * u), ln)
+        act(X("rm", 12 * u, 12 * u + 12), st, scale=-1.0, bias=float(L))
+    tag[0] = 1
+    cp(X("ta"), X("sp"))
+    act(X("hl", 0, C), X("ta"))
+    act(X("tb"), X("hl", 0, C), scale=-1.0)
+    mm([(X("ps7", 0, C), [(X("idh"), X("ta")), (X("idh"), X("tb"))])])
+    act(X("hl", C, 2 * C), X("ps7", 0, C))
+    for s in range(16):
+        pb, o = "ps%d" % (6 + (s // 2) % 2), C * (s % 2)
+        if s % 2 == 0:
+            mm([(X(pb, C * u, C * u + C), [(X("selt", 128 * (s + u), 128 * (s + u) + 128), X("hl", 0, C)),
+                                           (X("selt", 128 * (s + u), 128 * (s + u) + 128), X("hl", C, 2 * C))]) for u in range(2)])
+        act(X("nt", 8 + s, 8 + L, 16), X(pb, o, o + C))
+
+    def wide(t):
+        xx, yy, fl, au = "xx%d" % (t % 2), "yy%d" % t, "fl%d" % (t % 2), "au%d" % t
+        for k in range(L // GCH):
+            gat("v" if k in DVE_G[t] else "a", X(xx, GCH * k, GCH * k + GCH),
+                IND(X(au), X("so", GCH // 16 * k, GCH // 16 * (k + 1))))
+        act(X("sg"), IND(X(xx, 0, L + C), X("sto", 0, 12)))
+        tt(IND(X(xx, 0, L + C), X("sto", 0, 12)), X("sg"), X("negg"), A.add)
+        for k in range(L // SCH):
+            a, b = SCH * k, SCH * k + SCH
+            scan(X(yy, C + a, C + b), X("mm", a, b), X(xx, a, b), 0.0 if k == 0 else X(yy, C + a - 1, C + a), A.mult, A.add)
+            act(X(fl, a, b), X(yy, C + a, C + b), AF.Sign, bias=-0.5, scale=-1.0)
+            count(X("ps0", a // 16, b // 16), fl, a, b)
+        act(X("fd", 0, C), X("ps0", 0, C), AF.Sign, bias=-5.0)
+        scan(X("cx", 1, 193), X("fd", 0, C), X("zb", 0, C), 0.0, A.add, A.add)
+        act(X("h1"), IND(X("cx", 0, 193), X("kb", 0, 13)))
+        tt(X("h2"), IND(X("fd", 0, 193), X("kb", 0, 13)), X("km"), A.mult)
+        mm([(X("ps1", 0, C), [(X("hp"), X("m512")), (X("hp"), X("h2", 1, 193)), (X("hn"), X("h2", 0, C)),
+                              (X("hp"), X("h1", 1, 193)), (X("hn"), X("h1", 0, C))])])
+        diag(X("kd"), X("ps1", 0, C))
+        for u in range(2):
+            tt(X("k%d" % t, 12 * u, 12 * u + 12), D16("kd", C), X("ks", 0, 12), A.add)
+
+    def visit(t):
+        yy, au, mi = "yy%d" % t, "au%d" % t, "mi%d" % t
+        rel, inn = TB + 2 * NREL * t, TB + 2 * NREL * t + NREL
+        n, y, m = X("ts", 24, 36), X("cap", 12, 24), X("cap", 24, 36)
+        ro, rx, s = X("ro", 12, 24), X("ro", 0, 12), X("ss", 0, 12)
+        tt(X("pa"), X("ts", 24, 48), X("stc"), A.add)
+        ts(X("pb", 0, 12), X("pa", 12, 24), 8192.0, A.mult)
+        tt(X("pb", 0, 12), X("pa", 0, 12), X("pb", 0, 12), A.min)
+        cp(X("pd", 0, 12), X("pb", 0, 12))
+        yd = IND(X(yy), X("pd", 0, 12))
+        act(X("fa", C, 2 * C), yd, AF.Sign, bias=-0.5, scale=-1.0)
+        if t > 0:
+            act(X("th0"), yd, scale=-1.0)
+        tt(X("cap", 24, 48), X("ts", 24, 48), X("k%d" % t), A.min)
+        if t == 0:
+            count(X("ps2", 0, 12), "fa", C, 2 * C)
+            ts(s, X("ps2", 0, 12), 5.0, A.is_gt)
+        elif t == 1:
+            count(X("ps2", 0, 12), "fa", C, 2 * C)
+            ts(X("ff", 0, 12), X("ps2", 0, 12), 5.0, A.is_gt)
+            tt(y, X("ts", 12, 24), X("ff", 0, 12), A.mult)
+        else:
+            tt(X("ea", 0, 12), X("en0", 0, 12), X("ts", 12, 24), A.mult)
+            ts(X("eau", 0, 12), X("ea", 0, 12), float(W), A.add)
+            tt(X("u1"), IND(X(au), X("eau", 0, 12)), X("th0"), A.subtract)
+            act(X("fa", 0, C), X("u1"), AF.Sign, bias=-0.5, scale=-1.0)
+            act(X("th1"), X("u1"), scale=-1.0)
+            count(X("ps2", 0, 24), "fa", 0, 2 * C)
+            ts(X("ff"), X("ps2", 0, 24), 5.0, A.is_gt)
+            tt(X("yy"), X("ts", 0, 24), X("ff"), A.mult)
+            tt(X("ts", 12, 24), X("ts", 0, 12), X("ts", 12, 24), A.add)
+            tt(y, X("yy", 0, 12), X("yy", 12, 24), A.add)
+        a0 = 12 if t == 0 else 0
+        tt(X("ro", a0, 24), X("ts", 12 + a0, 36), X("cap", 12 + a0, 36), A.subtract)
+        scan(X("cr", 1, 13), ro, X("z16", 0, 12) if t == 0 else rx, 0.0, A.add, A.add)
+        mm([(X("ps3", 12 * u, 12 * u + 12), [(X("trl"), X("cr", 1, 13)), (X("trg"), X("cr", 0, 12))]) for u in range(2)]
+           + [(X("ps3", 24, 25), [(X("blk"), X("cr", 12, 13))])])
+        ts(X("zo", a0, 24), X("ro", a0, 24), 1.0, A.is_lt, BIG, A.mult)
+        q = 16 * (24 - a0)
+        if t > 0:
+            tt(X("zo", 0, 12), X("zo", 0, 12), ro, A.add)
+            tt(X("vv"), X("cap", 12, 36), X("sv"), A.add)
+            act(X("ee"), IND(X("vv"), X("ex")))
+        else:
+            tt(X("vv", 0, 12), m, X("sv0", 0, 12), A.add)
+            act(X("ee", 0, q), IND(X("vv", 0, 12), X("ex", 0, 12)))
+        tt(X("oo", a0, 24), X("ps3", a0, 24), X("zo", a0, 24), A.add)
+        tt(X("oo", a0, 24), X("oo", a0, 24), X("dum", a0, 24), A.min)
+        cp(X("ou", a0, 24), X("oo", a0, 24))
+        w0 = NREL * (2 - t)
+        tt(IND(X("wr", w0, w0 + L + 2 * C), X("ou", a0, 24)), X("ee", 0, q), X("mk", 0, q), A.mult)
+        mm([(X("ps5", 0, NREL), [(X("blks"), X("wr", w0, w0 + NREL))])])
+        act(col("rr"), X("ps3", 24, 25))
+        act(X("rr", 1, 2), X("ps3", 24, 25), scale=-0.5, bias=NREL / 2.0)
+        tt(X("kq", 24, 48), X("ps3", 0, 24), X("rm"), A.add)
+        scan(X("v1"), X("ps5", 0, NREL), X("ones"), 0.0, A.max, A.add)
+        diag(X("v2"), X("v1"))
+        if t == 0:
+            ts(X("rp", 0, 20), D16("v2", NREL), float(NULLC), A.min)
+        else:
+            cp(X("rpi", 0, 20), D16("v2", NREL))
+            ts(X("rpi", 0, 20), X("rpi", 0, 20), 8191, A.bitwise_and)
+            ts(X("rp", 0, 20), X("rpi", 0, 20), float(NULLC), A.min)
+        act(X("nt", rel, rel + NREL), IND(X("nt", 0, TB), X("rp", 0, 20)))
+        remote(r + 1, X("nt", inn, inn + NREL), X("nt", rel, rel + NREL), "rr%d" % t, 163840)
+        if t > 0:
+            tt(X("fs"), IND(X(au), X("eb", 0, 12)), X("th0" if t == 1 else "th1"), A.is_lt)
+            count(X("ps2", 32, 44), "fs", 0, C)
+            ts(s, X("ps2", 32, 44), 10.5, A.is_gt)
+        scan(X("cs", 1, 13), s, X("z16", 0, 12), 0.0, A.add, A.add)
+        c12 = X("cs", 12, 13)
+        mm([(X("ps4", 256, 257), [(X("blk"), X("cr", 12, 13)), (X("hn"), c12), (X("hn"), c12)]),
+            (X("ps4", 257, 258), [(X("hp"), c12)])])
+        mo = "ms%d" % t
+        ts(X(mo, 0, 2), X("ps4", 256, 258), 0.0, A.max, 128.0, A.min)
+        remote(r + 1, X(mi, 0, 2), X(mo, 0, 2), "rm%d" % t, 1024)
+        pre = [(X("trlh"), X("cs", 1, 13)), (X("trgh"), X("cs", 0, 12))]
+        mm([(X("ps4", 12 * u, 12 * u + 12), pre) for u in range(a0 // 12, 4)] + [(X("ps4", 48, 60), pre + [(X("nid"), s)])])
+        sg = X("ps4", 12, 24)
+        ts(X("isin", 0, 12), sg, col("rr"), A.is_ge, 2.0, A.mult)
+        tt(X("kq", 12, 24), X("kq", 36, 48), m, A.subtract)
+        if t > 0:
+            tt(X("kq", 0, 12), X("kq", 12, 24), y, A.subtract)
+            tt(X("xo", 0, 12), y, X("c3", 0, 12), A.add)
+            cp(X("xu", 0, 12), X("xo", 0, 12))
+        tt(X("aw", 0, 2), X(mi, 0, 2), X("rr", 0, 2), A.add)
+        ts(X("mx", a0, 48), X("ps4", a0, 48), col("aw"), A.min)
+        ts(X("cap", a0, a0 + 12), X("ps4", 48, 60), BIG, A.add, col("aw"), A.is_lt)
+        tt(X("tp", a0, 48), X("kq", a0, 48), X("mx", a0, 48), A.subtract)
+        tt(X("ts", a0, 48), X("tp", a0, 48), X("cap", a0, 48), A.min)
+        ts(X("ts", a0, 48), X("ts", a0, 48), 0.0, A.max)
+        if t < 2:
+            act(X("rm"), X("tp", 24, 48), AF.Relu)
+        else:
+            ts(X("rm"), X("tp", 24, 48), 0.0, A.max)
+        ts(X("g1", 0, 12), X("isin", 0, 12), X("aw", 1, 2), A.mult, float(rel - ZN), A.add)
+        tt(X("g1", 0, 12), X("g1", 0, 12), sg, A.add)
+        tt(X("g1", 0, 12), X("g1", 0, 12), X("ts", a0, a0 + 12), A.mult)
+        cp(X("gi", 0, 12), X("g1", 0, 12))
+        gw = IND(X("nt", ZN, inn + NREL), X("gi", 0, 12))
+        if t < 2:
+            tt(X("gn"), gw, X("md8"), A.add)
+            diag(X("gd"), X("gn"))
+            ts(X("eb", 0, 12), D16("gd", C), col("s8k"), A.subtract)
+        if t == 0:
+            act(X("en0", 0, 12), D16("gd", C), bias=col("s8z"))
+            act(X("nt", XB, ZN, 3), gw)
+        else:
+            act(X("gg"), gw)
+            cp(IND(X("nt", XB, ZN), X("xu", 0, 12)), X("gg"))
+
+    def final_static():
+        iota(X("vrep", 0, C), [[16387, C]], 16384 + XB - 1, 0)
+        iota(X("el"), [[16384, C]], 8192 + 7, 0)
+        mm([(X("ps7", 0, C), [(X("idh"), X("el")), (X("rep", p=8), X("b8", 0, C, p=8))])])
+        act(X("vrep", C, 2 * C), X("ps7", 0, C))
+        iota(X("ta"), [[1, 16], [32, 6], [224, 2]], 0, 0)
+        iota(X("tb"), [[0, 16], [0, 6], [-416, 2]], 208, 0)
+        ts(X("pj", 1, 2), X("pi", 0, 1), 4, A.logical_shift_right, 1, A.bitwise_and)
+        cp(col("e1"), X("pj", 1, 2))
+        act(X("tb"), X("tb"), scale=col("e1"))
+        mm([(X("ps7", 0, C), [(X("idh"), X("ta")), (X("idh"), X("tb")), (X("idh"), X("md8"))])])
+        diag(X("ta"), X("ps7", 0, C))
+        ts(X("tg", 0, 12), D16("ta", C), col("s8k"), A.subtract)
+
+    def final():
+        n = X("ts", 24, 36)
+        ts(X("bb", 12, 24), X("rm", 0, 12), -1.0, A.mult, float(L), A.add)
+        tt(X("bb", 0, 12), X("bb", 12, 24), n, A.add)
+        cp(X("bbi"), X("bb"))
+        ts(X("bbi"), X("bbi"), 15, A.bitwise_and)
+        cp(X("b15"), X("bbi"))
+        mm([(X("ps6", s, 384, 16), [(X("selt", 128 * s, 128 * s + 128), X("b15"))]) for s in range(16)])
+        tt(X("ts", 12, 24), X("ts", 0, 12), X("ts", 12, 24), A.add)
+        ts(X("zo"), X("ts", 12, 36), 1.0, A.is_lt, BIG, A.mult)
+        tt(X("oo"), X("bb"), X("zo"), A.add)
+        tt(X("oo"), X("oo"), X("dum"), A.min)
+        cp(X("ou"), X("oo"))
+        ts(X("msk"), X("ps6", 0, 384), col("sc"), A.is_le)
+        tt(IND(X("xx1"), X("ou")), X("vrep"), X("msk"), A.mult)
+        scan(X("yy1", C, C + L), X("xx1", 0, L), X("on"), 0.0, A.max, A.add)
+        lq = X("lq", 0, 12)
+        tt(lq, n, X("ts", 12, 24), A.add)
+        mm([(X("ps3", 0, 12), [(X("blk"), lq)])])
+        add("v", lambda: V.tensor_reduce(col("tot")[0], X("ps3", 0, 12)[0], AxisListType.X, A.add),
+            X("ps3", 0, 12)[1], col("tot")[1], 114.0)
+        act(X("tot", 1, 2), col("tot"), scale=-BIG, bias=col("g15"))
+        act(X("jadj"), X("jd"), AF.Relu, scale=BIG, bias=X("tot", 1, 2))
+        act(X("ps7", 0, C), X("jadj"), bias=col("sm15"))
+        tt(X("el"), IND(lq, X("ex", 0, 12)), X("mk", 0, C), A.mult)
+        mm([(X("ps4", 0, C), [(X("blks"), X("el"))])])
+        act(X("ynr"), X("ps4", 0, C))
+        o = POOL["ynr"][1]
+        dma("s", T.yn[:], T.pf[0:128:16, o:o + C], X("ynr")[1], [], "dn", 6144)
+        mm([(X("ps5", 0, C), [(X("blk"), X("ones", 0, C)), (X("p15"), X("yy1", C - 1, C - 1 + L, 16))])])
+        tt(X("nn"), X("ps5", 0, C), X("yy1", C + 15, C + L, 16), A.max)
+        ts(X("nn"), X("nn"), 8191, A.bitwise_and)
+        tt(X("npad", 16, 208), X("nn"), X("ps7", 0, C), A.add)
+        tr(X("tt", 0, C), X("npad", 16, 208))
+        tr(X("tt", C, C + 224), X("npad"))
+        ts(X("fo"), IND(X("tt"), X("tg", 0, 12)), float(NULLC), A.min)
+        h = L // 2
+        for k in range(2):
+            gat("va"[k], X("xx0", h * k, h * k + h), IND(X("nt", 0, TB), X("fo", h // 16 * k, h // 16 * (k + 1))))
+        dma("s", T.yo[:], T.xx0[0:128:16, 0:L], X("xx0", 0, L)[1], [], "do", 98304)
+
+    for k, (f, t) in enumerate(((wide, 0), (wide, 1), (visit, 0), (wide, 2), (final_static, 0), (visit, 1), (visit, 2), (final, 0))):
+        tag[0] = 2 + k
+        if f is final or f is final_static:
+            f()
+        else:
+            f(t)
+    return ops
+
+
+def _deps(ops):
+    hist, deps = {}, []
+    for i, o in enumerate(ops):
+        d = {}
+        for regs, w in ((o[2], False), (o[3], True)):
+            for buf, a, b in regs:
+                ps = SCRATCH[buf][0] == "psum"
+                for j, a2, b2, w2 in hist.get(buf, []):
+                    over = a < b2 and a2 < b
+                    if over and (w or w2) and not (w and w2 and buf == "nt" and o[8] == 1 and ops[j][8] == 1):
+                        d[j] = True
+                    elif (over and (w or w2)) or (ps and ops[j][0] != o[0]):
+                        d.setdefault(j, False)
+        for regs, w in ((o[2], False), (o[3], True)):
+            for buf, a, b in regs:
+                hist.setdefault(buf, []).append((i, a, b, w))
+        deps.append(d)
+    return deps
+
+
+def _place(ops, edges, order, rel):
+    n = len(ops)
+    fin, busy = [0.0] * n, {}
+    for i in order:
+        c, t = ops[i][4], rel[i]
+        for j, lag in edges[i]:
+            t = max(t, fin[j] + lag)
+        lst = busy.setdefault(ops[i][0], [(1e18, 1e18)])
+        k = 0
+        for k, (a, b) in enumerate(lst):
+            if t + c <= a:
+                break
+            if b > t:
+                t = b
+        lst.insert(k, (t, t + c))
+        fin[i] = t + c
+    return fin
+
+
+def _schedule(ops, tries=1200):
+    deps = _deps(ops)
+    n = len(ops)
+    fw, bw = [[] for _ in ops], [[] for _ in ops]
+    for i in range(n):
+        for j, raw in deps[i].items():
+            lag = (LAG_SAME if raw else 0.0) if (ops[j][0] == ops[i][0] and ops[j][6] is None) else ops[j][5] + LAG_CROSS
+            fw[i].append((j, lag))
+            bw[j].append((i, lag))
+    zero, tail = [0.0] * n, [o[5] for o in ops]
+    best, cur, seed, warm = None, None, 12345, max(1, tries // 10)
+    for it in range(tries):
+        rank = [0.0] * n
+        if it < warm:
+            fac = []
+            for _ in range(10):
+                seed = (seed * 1103515245 + 12345) % 2147483648
+                fac.append(0.05 + 2.0 * (seed / 2147483648.0) ** 2)
+            for i in range(n - 1, -1, -1):
+                seed = (seed * 1103515245 + 12345) % 2147483648
+                rank[i] += ((ops[i][4] + 70) * (1.0 + 0.3 * seed / 2147483648.0) + ops[i][5]) * fac[ops[i][8]]
+                for j in deps[i]:
+                    rank[j] = max(rank[j], rank[i] + 1e-3)
+        else:
+            rnd = []
+            for _ in range(6):
+                seed = (seed * 1103515245 + 12345) % 2147483648
+                rnd.append(seed / 2147483648.0)
+            mid, wid, sh, tg = rnd[0] * cur[0], 500 + 6000 * rnd[1], (rnd[2] - 0.5) * 8000, int(rnd[3] * 10)
+            rank = [-1e9] * n
+            for i in range(n - 1, -1, -1):
+                hit = abs(cur[1][i] - mid) < wid and (ops[i][8] == tg or (rnd[4] < 0.3 and (i * 7 + it) % 5 == 0))
+                rank[i] = max(rank[i], -cur[1][i] + (sh if hit else 0.0))
+                for j in deps[i]:
+                    rank[j] = max(rank[j], rank[i] + 1e-3)
+        order = sorted(range(n), key=lambda k: (-rank[k], k))
+        for _ in range(4 if it < warm else 2):
+            fin = _place(ops, fw, order, zero)
+            span = max(fin[i] + tail[i] for i in range(n))
+            got = (span, [fin[i] - ops[i][4] for i in range(n)])
+            if best is None or span < best[0]:
+                best = got
+            if it < warm:
+                cur = best
+            elif span < cur[0] + 400.0 * (1.0 - it / tries):
+                cur = got
+            back = _place(ops, bw, sorted(range(n), key=lambda k: (-fin[k] - tail[k], -k)), tail)
+            order = sorted(range(n), key=lambda k: (-back[k], k))
+    order = sorted(range(n), key=lambda k: (best[1][k], k))
+    need, waits, know, seen, pos, cnt = set(), {}, {}, {}, {}, {}
+    for i in order:
+        q = ops[i][0]
+        kn = know.setdefault(q, set())
+        w = []
+        for j in sorted(deps[i], key=lambda k: -best[1][k]):
+            if j in kn or (ops[j][0] == q and ops[j][6] is None and not deps[i][j]):
+                continue
+            w.append(j)
+            need.add(j)
+            kn |= seen[j]
+        waits[i] = w
+        s = set() if (q == "g" and ops[i][6]) else set(kn)
+        s.add(i)
+        if ops[i][6] is None:
+            s |= pos.get(q, set())
+            pos[q] = s
+        seen[i] = s
+    val = {}
+    for i in order:
+        if ops[i][6] is None and i in need:
+            cnt[ops[i][0]] = cnt.get(ops[i][0], 0) + 1
+            val[i] = cnt[ops[i][0]]
+    return dict(order=order, waits=waits, val=val, cnt=cnt, need=need, span=best[0], start=best[1])
+
+
+def rank_program(g, core, T, topo):
+    if T.rank_of(core) is None:
+        return
+    ops = _ops(g, T, topo, core)
+    if "p" not in PLAN:
+        PLAN["p"] = _schedule(ops)
+    p = PLAN["p"]
+    Q = dict(v=g.vector, a=g.scalar, p=g.tensor, g=g, s=g.sync)
+    sent = 0
+    for i in p["order"]:
+        q, emit, sem, k = ops[i][0], ops[i][1], ops[i][6], ops[i][7]
+        top = {}
+        for j in p["waits"][i]:
+            name, v = (ops[j][6], ops[j][7]) if ops[j][6] else ("q" + ops[j][0], p["val"][j])
+            top[name] = max(top.get(name, 0), v)
+        for name, v in top.items():
+            Q[q].wait_ge(T.sem[name], v)
+        ins = emit()
+        if sem is None:
+            if i in p["val"]:
+                ins.then_inc(T.sem["q" + q], 1)
+        elif q == "g":
+            sent += k
+        else:
+            ins.then_inc(T.sem[sem], 16)
+    g.wait_ge(T.sem.sent, sent)
+    for i in p["order"]:
+        if ops[i][6] and i not in p["need"]:
+            g.sync.wait_ge(T.sem[ops[i][6]], ops[i][7])

@@ -13,10 +13,10 @@ F_T = dict(pc=8, g16=8, sc=8, g15=8, p16=8, s15=8, s8k=8, s8z=8, e1=8, sm15=8, i
            trg=128, p15=128, rep=128, mk=384, md=384, md8=192, ones=320, l8f=208, b8=208, bd1=208, bd2=192, cd=16, len=16,
            t1=24, t2=24, t3=24, dum=24, negg=192, sg=192, stc=24, sv=24, c3=16, ks=16, kd=192, k0=24, k1=24, k2=24,
            ts=48, tp=48, cap=48, kq=48, mx=48, ns=48, nsc=48, pa=24, pb=16, th0=192, th1=192, u1=192, ff=24, yy=24, rx2=24,
-           ro=24, cr=16, zo=24, oo=24, vv=24, ee=384, v1=320, v2=320, rr=8, rm=24, isin=16, aw=8, t4=24, sv0=16, sm4k=8, idh=128,
+           ro=24, cr=16, zo=24, oo=24, vv=24, ee=384, v1=320, v2=320, rr=8, rm=24, isin=16, aw=8, t4=24, sv0=16, sm4k=8, idh=128, sh=8,
            gi0=16, g1=16, xo=16, gg=192, gn=192, gd=192, en0=16, ea=16, ms0=8, ms1=8, ms2=8, vrep=384, msk=384, jd=192, jadj=192,
            npad=224, tt=416, lq=16, tot=8, el=192, ynr=192, ta=192, tb=192, z16=16, bb=24)
-H_T = dict(big=144, hp=128, hn=128, trlh=128, trgh=128, nid=128, ss=16, zb=208, km=208, m512=192, gz=192, hl=384, fd=200, cx=200,
+H_T = dict(big=144, hp=128, hn=128, trlh=128, trgh=128, nid=128, ss=16, idb=128, aa=192, ab=192, lh=24, zb=208, km=208, m512=192, gz=192, hl=384, fd=200, cx=200,
            h1=208, h2=208, fa=384, fs=192, cs=16, b15=24)
 U_T = dict(so=192, kb=16, sto=16, ex=24, pd=16, ou=24, rp=24, gi=16, xu=16, eb=16, eau=16, fo=192, tg=16)
 I_T = dict(pi=8, pj=8, l8=192, sp=192, gu=192, hli=384, bi=208, kbi=16, exi=24, rpi=24, bbi=24, nn=192)
@@ -52,14 +52,16 @@ SCRATCH["wr"] = ("sbuf", [128, 2 * NREL + L + 2 * C], "float32")
 for _t in range(8):
     SCRATCH["ps%d" % _t] = ("psum", [128, 512], "float32")
 
-SEMAPHORES = (["qv", "qa", "qp", "qg", "sent", "dl", "dsp", "dg", "da0", "da1", "do", "dn", "ra1", "ra2"]
+SEMAPHORES = (["qv", "qa", "qp", "qg", "sent", "dl", "dsp", "dg", "da0", "da1", "do", "dn", "ra1", "ra2", "rb1", "dh0", "dh1", "dh2"]
               + ["rr%d" % t for t in range(3)] + ["rm%d" % t for t in range(3)])
 
 GCH = 512
 SCH = 1024
-DVE_G = {0: (0, 1, 2), 1: (), 2: ()}
+DVE_G = {0: (0, 1, 2), 1: (0, 1, 2, 3), 2: ()}
 FIN_V = (0, 1, 2)
-LAG_SAME, LAG_CROSS = 50.0, 90.0
+LAG_SAME, LAG_CROSS = 60.0, 140.0
+MV = 1088
+OPT = dict(k=0, zo=0, fs=0, gn=0, late=4500, pe=0.62, af=90)
 PLAN = {}
 
 
@@ -133,7 +135,7 @@ def _ops(g, T, topo, core):
 
     def act(out, i, fn=AF.Identity, bias=0.0, scale=1.0):
         rd, wr = split(out, [i, bias, scale])
-        c = 65 + 1.56 * out[2] if i[4] == "ind" else 60 + max(64, out[2])
+        c = 65 + 1.56 * out[2] if i[4] == "ind" else OPT["af"] + max(64, out[2])
         add("a", lambda: S.activation(out[0], i[0], fn, bias=ap(bias), scale=ap(scale)), rd, wr, c)
 
     def gat(eng, out, i):
@@ -142,19 +144,19 @@ def _ops(g, T, topo, core):
         else:
             act(out, i)
 
-    def mm(groups):
+    def mm(groups, start=True, stop=True):
         rd, wr, c = [], [], 60.0
         for out, l in groups:
             wr += out[1]
             for a, b in l:
                 rd += a[1] + b[1]
-                c += 0.5 * max(64, b[2]) * (4 if b[3] == "float32" else 1)
+                c += OPT["pe"] * max(64, b[2]) * (4 if b[3] == "float32" else 1)
 
         def emit():
             ins = None
             for out, l in groups:
                 for k, (a, b) in enumerate(l):
-                    ins = P.matmul(out[0], a[0], b[0], k == 0, k == len(l) - 1)
+                    ins = P.matmul(out[0], a[0], b[0], start and k == 0, stop and k == len(l) - 1)
             return ins
         add("p", emit, rd, wr, c)
 
@@ -180,7 +182,7 @@ def _ops(g, T, topo, core):
         m = topo.mask(core, d)
         k = len(topo.engines(core, d))
         add("g", lambda: g.remote_dma(out[0], i[0], T.sem[sem], T.sem.sent, pid, rid, m), i[1], out[1], 400.0,
-            1800 + extra + nbytes / 250.0, sem, k)
+            2400 + extra + nbytes / 250.0, sem, k)
 
     def diag(out, src):
         scan(out, X("mk", 0, src[2]), src, 0.0, A.add, A.min)
@@ -201,8 +203,9 @@ def _ops(g, T, topo, core):
     dma("a", X("au0", 0, W // 2)[0], T.aud[:, 0:W // 2], [], X("au0", 0, W // 2)[1], "da0", 524288, 500)
     dma("s", X("gu")[0], T.gua[:], [], X("gu")[1], "dg", 98304, 300)
     dma("a", X("au0", W // 2, W)[0], T.aud[:, W // 2:W], [], X("au0", W // 2, W)[1], "da1", 524288, 2300)
-    remote(r - 1, X("au1", 0, W), X("au0", 0, W), "ra1", 1 << 20, 1500)
-    remote(r - 2, X("au2", 0, W), X("au0", 0, W), "ra2", 1 << 20, 5500)
+    remote(r - 1, X("au1", 0, W // 2), X("au0", 0, W // 2), "ra1", 1 << 19, OPT["late"] + 2300)
+    remote(r - 1, X("au1", W // 2, W), X("au0", W // 2, W), "rb1", 1 << 19, OPT["late"])
+    remote(r - 2, X("au2", 0, W), X("au0", 0, W), "ra2", 1 << 20, OPT["late"] + 5000)
 
     iota(X("pi", 0, 1), [[0, 1]], 0, 1)
     iota(X("i143"), [[1, 144]], 0, 0)
@@ -215,7 +218,10 @@ def _ops(g, T, topo, core):
     tt(col("g16"), col("pc"), col("sc"), A.subtract)
     ts(X("mk"), X("md"), col("sc"), A.is_equal, 16777216.0, A.mult)
     ms(X("l8f"), 0.0)
-    ms(X("mm"), 1.0)
+    ms(X("mm", 0, MV), 1.0)
+    for a in range(MV, L + C, MV):
+        b = min(a + MV, L + C)
+        act(X("mm", a, b), X("mm", 0, b - a))
     ms(X("zb"), 0.0)
     ts(X("big"), X("i143"), -15.0, A.add, col("g16"), A.is_equal)
     ts(X("blk"), X("j16"), col("g16"), A.is_equal)
@@ -233,10 +239,13 @@ def _ops(g, T, topo, core):
     act(col("s8z"), col("sc"), scale=-8192.0, bias=-4096.0)
     act(col("g15"), col("g16"), scale=-BIG, bias=BIG)
     act(col("sm15"), col("sc"), bias=-15.0)
+    act(col("sh"), col("sc"), bias=0.5)
+    if OPT["fs"]:
+        act(X("idb"), X("idh"))
     act(col("sm4k"), col("sc"), scale=-4096.0)
-    act(X("md8"), X("md", 0, C), scale=8192.0)
-    act(X("m512"), X("md", 0, C), scale=512.0)
-    act(X("ones"), X("md", 0, NREL), bias=1.0, scale=0.0)
+    iota(X("md8"), [[0, 12], [8192, 16]], 0, 0)
+    iota(X("m512"), [[0, 12], [512, 16]], 0, 0)
+    fill(X("ones"), 1)
     for k in range(6):
         fill(X("on", 512 * k, 512 * k + 512), 1)
     for h in range(4):
@@ -250,8 +259,8 @@ def _ops(g, T, topo, core):
     act(X("c3", 0, 12), X("cd", 0, 12), scale=3.0)
     for t in range(3):
         fill(X("au%d" % t, W, W + 16), 0)
-    act(X("xx0", L, L + 2 * C), X("md"), scale=0.0)
-    fill(X("xx1", L, L + 2 * C), 0)
+    fill(X("xx0", L, L + C), 0)
+    fill(X("xx1", L, L + C), 0)
     for t in range(3):
         fill(X("wr", NREL * t, NREL * t + NREL), 0)
     fill(X("nt", 0, 8), 0)
@@ -277,7 +286,8 @@ def _ops(g, T, topo, core):
     cp(IND(X("mm"), X("sto", 0, 12)), X("zb", 0, C))
     ts(X("negg"), X("gu"), -1.0, A.mult)
     for t in range(3):
-        act(X("yy%d" % t, 0, C), X("negg"))
+        h = X("yy%d" % t, 0, C)
+        dma("s", h[0], X("negg")[0], X("negg")[1], h[1], "dh%d" % t, 98304, 1500)
     cp(X("bi"), X("ps6", 0, 208))
     ts(X("bi"), X("bi"), 15, A.bitwise_and)
     ts(X("km"), X("bi"), col("sc"), A.is_gt)
@@ -330,8 +340,11 @@ def _ops(g, T, topo, core):
         mm([(X("ps1", 0, C), [(X("hp"), X("m512")), (X("hp"), X("h2", 1, 193)), (X("hn"), X("h2", 0, C)),
                               (X("hp"), X("h1", 1, 193)), (X("hn"), X("h1", 0, C))])])
         diag(X("kd"), X("ps1", 0, C))
-        for u in range(2):
-            tt(X("k%d" % t, 12 * u, 12 * u + 12), D16("kd", C), X("ks", 0, 12), A.add)
+        tt(X("k%d" % t, 0, 12), D16("kd", C), X("ks", 0, 12), A.add)
+        if OPT["k"] and t > 0:
+            act(X("k%d" % t, 12, 24), X("k%d" % t, 0, 12))
+        else:
+            tt(X("k%d" % t, 12, 24), D16("kd", C), X("ks", 0, 12), A.add)
 
     def visit(t):
         yy, au, mi = "yy%d" % t, "au%d" % t, "mi%d" % t
@@ -345,7 +358,7 @@ def _ops(g, T, topo, core):
         yd = IND(X(yy), X("pd", 0, 12))
         act(X("fa", C, 2 * C), yd, AF.Sign, bias=-0.5, scale=-1.0)
         if t > 0:
-            act(X("th0"), yd, scale=-1.0)
+            act(X("th0"), yd, scale=1.0 if OPT["fs"] else -1.0)
         tt(X("cap", 24, 48), X("ts", 24, 48), X("k%d" % t), A.min)
         if t == 0:
             count(X("ps2", 0, 12), "fa", C, 2 * C)
@@ -357,9 +370,14 @@ def _ops(g, T, topo, core):
         else:
             tt(X("ea", 0, 12), X("en0", 0, 12), X("ts", 12, 24), A.mult)
             ts(X("eau", 0, 12), X("ea", 0, 12), float(W), A.add)
-            tt(X("u1"), IND(X(au), X("eau", 0, 12)), X("th0"), A.subtract)
-            act(X("fa", 0, C), X("u1"), AF.Sign, bias=-0.5, scale=-1.0)
-            act(X("th1"), X("u1"), scale=-1.0)
+            if OPT["fs"]:
+                act(X("aa"), IND(X(au), X("eau", 0, 12)))
+                mm([(X("ps6", 0, C), [(X("idh"), X("th0")), (X("idb"), X("aa"))])])
+                act(X("fa", 0, C), X("ps6", 0, C), AF.Sign, bias=-0.5, scale=-1.0)
+            else:
+                tt(X("u1"), IND(X(au), X("eau", 0, 12)), X("th0"), A.subtract)
+                act(X("fa", 0, C), X("u1"), AF.Sign, bias=-0.5, scale=-1.0)
+                act(X("th1"), X("u1"), scale=-1.0)
             count(X("ps2", 0, 24), "fa", 0, 2 * C)
             ts(X("ff"), X("ps2", 0, 24), 5.0, A.is_gt)
             tt(X("yy"), X("ts", 0, 24), X("ff"), A.mult)
@@ -370,7 +388,10 @@ def _ops(g, T, topo, core):
         scan(X("cr", 1, 13), ro, X("z16", 0, 12) if t == 0 else rx, 0.0, A.add, A.add)
         mm([(X("ps3", 12 * u, 12 * u + 12), [(X("trl"), X("cr", 1, 13)), (X("trg"), X("cr", 0, 12))]) for u in range(2)]
            + [(X("ps3", 24, 25), [(X("blk"), X("cr", 12, 13))])])
-        ts(X("zo", a0, 24), X("ro", a0, 24), 1.0, A.is_lt, BIG, A.mult)
+        if OPT["zo"]:
+            act(X("zo", a0, 24), X("ro", a0, 24), AF.Relu, scale=-BIG, bias=BIG)
+        else:
+            ts(X("zo", a0, 24), X("ro", a0, 24), 1.0, A.is_lt, BIG, A.mult)
         q = 16 * (24 - a0)
         if t > 0:
             tt(X("zo", 0, 12), X("zo", 0, 12), ro, A.add)
@@ -398,7 +419,13 @@ def _ops(g, T, topo, core):
             ts(X("rp", 0, 20), X("rpi", 0, 20), float(NULLC), A.min)
         act(X("nt", rel, rel + NREL), IND(X("nt", 0, TB), X("rp", 0, 20)))
         remote(r + 1, X("nt", inn, inn + NREL), X("nt", rel, rel + NREL), "rr%d" % t, 163840)
-        if t > 0:
+        if t > 0 and OPT["fs"]:
+            act(X("ab"), IND(X(au), X("eb", 0, 12)))
+            mm([(X("ps6", 0, C), [(X("idh"), X("th0"))] + ([(X("idb"), X("aa"))] if t == 2 else []) + [(X("idb"), X("ab"))])])
+            act(X("fs"), X("ps6", 0, C), AF.Sign, bias=-0.5, scale=-1.0)
+            count(X("ps2", 32, 44), "fs", 0, C)
+            ts(s, X("ps2", 32, 44), 5.0, A.is_gt)
+        elif t > 0:
             tt(X("fs"), IND(X(au), X("eb", 0, 12)), X("th0" if t == 1 else "th1"), A.is_lt)
             count(X("ps2", 32, 44), "fs", 0, C)
             ts(s, X("ps2", 32, 44), 10.5, A.is_gt)
@@ -426,16 +453,19 @@ def _ops(g, T, topo, core):
         ts(X("ts", a0, 48), X("ts", a0, 48), 0.0, A.max)
         if t < 2:
             act(X("rm"), X("tp", 24, 48), AF.Relu)
-        else:
-            ts(X("rm"), X("tp", 24, 48), 0.0, A.max)
         ts(X("g1", 0, 12), X("isin", 0, 12), X("aw", 1, 2), A.mult, float(rel - ZN), A.add)
         tt(X("g1", 0, 12), X("g1", 0, 12), sg, A.add)
         tt(X("g1", 0, 12), X("g1", 0, 12), X("ts", a0, a0 + 12), A.mult)
         cp(X("gi", 0, 12), X("g1", 0, 12))
         gw = IND(X("nt", ZN, inn + NREL), X("gi", 0, 12))
         if t < 2:
-            tt(X("gn"), gw, X("md8"), A.add)
-            diag(X("gd"), X("gn"))
+            if OPT["gn"]:
+                act(X("gn"), gw)
+                mm([(X("ps7", 0, C), [(X("idh"), X("md8")), (X("idh"), X("gn"))])])
+                diag(X("gd"), X("ps7", 0, C))
+            else:
+                tt(X("gn"), gw, X("md8"), A.add)
+                diag(X("gd"), X("gn"))
             ts(X("eb", 0, 12), D16("gd", C), col("s8k"), A.subtract)
         if t == 0:
             act(X("en0", 0, 12), D16("gd", C), bias=col("s8z"))
@@ -460,7 +490,7 @@ def _ops(g, T, topo, core):
 
     def final():
         n = X("ts", 24, 36)
-        ts(X("bb", 12, 24), X("rm", 0, 12), -1.0, A.mult, float(L), A.add)
+        ts(X("bb", 12, 24), X("tp", 24, 36), -1.0, A.mult, float(L), A.add)
         tt(X("bb", 0, 12), X("bb", 12, 24), n, A.add)
         cp(X("bbi"), X("bb"))
         ts(X("bbi"), X("bbi"), 15, A.bitwise_and)
@@ -471,23 +501,26 @@ def _ops(g, T, topo, core):
         tt(X("oo"), X("bb"), X("zo"), A.add)
         tt(X("oo"), X("oo"), X("dum"), A.min)
         cp(X("ou"), X("oo"))
-        ts(X("msk"), X("ps6", 0, 384), col("sc"), A.is_le)
+        act(X("msk"), X("ps6", 0, 384), AF.Sign, scale=-1.0, bias=col("sh"))
         tt(IND(X("xx1"), X("ou")), X("vrep"), X("msk"), A.mult)
         scan(X("yy1", C, C + L), X("xx1", 0, L), X("on"), 0.0, A.max, A.add)
         lq = X("lq", 0, 12)
         tt(lq, n, X("ts", 12, 24), A.add)
-        mm([(X("ps3", 0, 12), [(X("blk"), lq)])])
-        add("v", lambda: V.tensor_reduce(col("tot")[0], X("ps3", 0, 12)[0], AxisListType.X, A.add),
-            X("ps3", 0, 12)[1], col("tot")[1], 114.0)
+        act(X("lh", 0, 12), lq)
+        act(X("t4", 0, 12), X("lh", 0, 12), scale=-1.0)
+        mm([(X("ps3", 0, 12), [(X("idh"), lq), (X("idh"), X("t4", 0, 12))])])
+        act(X("lh", 12, 24), X("ps3", 0, 12))
+        mm([(X("ps4", s, C, 16), [(X("selt", 128 * s, 128 * s + 128), X("lh", 0, 12)),
+                                  (X("selt", 128 * s, 128 * s + 128), X("lh", 12, 24))]) for s in range(16)])
+        add("a", lambda: S.activation(X("ynr")[0], X("ps4", 0, C)[0], AF.Identity, accum_out=col("tot")[0]),
+            X("ps4", 0, C)[1], X("ynr")[1] + col("tot")[1], 300.0)
         act(X("tot", 1, 2), col("tot"), scale=-BIG, bias=col("g15"))
         act(X("jadj"), X("jd"), AF.Relu, scale=BIG, bias=X("tot", 1, 2))
         act(X("ps7", 0, C), X("jadj"), bias=col("sm15"))
-        tt(X("el"), IND(lq, X("ex", 0, 12)), X("mk", 0, C), A.mult)
-        mm([(X("ps4", 0, C), [(X("blks"), X("el"))])])
-        act(X("ynr"), X("ps4", 0, C))
         o = POOL["ynr"][1]
         dma("s", T.yn[:], T.pf[0:128:16, o:o + C], X("ynr")[1], [], "dn", 6144)
-        mm([(X("ps5", 0, C), [(X("blk"), X("ones", 0, C)), (X("p15"), X("yy1", C - 1, C - 1 + L, 16))])])
+        mm([(X("ps5", 0, C), [(X("blk"), X("ones", 0, C))])], stop=False)
+        mm([(X("ps5", 0, C), [(X("p15"), X("yy1", C - 1, C - 1 + L, 16))])], start=False)
         tt(X("nn"), X("ps5", 0, C), X("yy1", C + 15, C + L, 16), A.max)
         ts(X("nn"), X("nn"), 8191, A.bitwise_and)
         tt(X("npad", 16, 208), X("nn"), X("ps7", 0, C), A.add)
@@ -547,7 +580,7 @@ def _place(ops, edges, order, rel):
     return fin
 
 
-def _schedule(ops, tries=1200):
+def _schedule(ops, tries=1500, seed=5):
     deps = _deps(ops)
     n = len(ops)
     fw, bw = [[] for _ in ops], [[] for _ in ops]
@@ -557,7 +590,7 @@ def _schedule(ops, tries=1200):
             fw[i].append((j, lag))
             bw[j].append((i, lag))
     zero, tail = [0.0] * n, [o[5] for o in ops]
-    best, cur, seed, warm = None, None, 12345, max(1, tries // 10)
+    best, cur, warm = None, None, max(1, tries // 10)
     for it in range(tries):
         rank = [0.0] * n
         if it < warm:
@@ -584,7 +617,7 @@ def _schedule(ops, tries=1200):
                     rank[j] = max(rank[j], rank[i] + 1e-3)
         order = sorted(range(n), key=lambda k: (-rank[k], k))
         for _ in range(4 if it < warm else 2):
-            fin = _place(ops, fw, order, zero)
+            fin = _place(ops, fw, list(range(8)) + [k for k in order if k >= 8], zero)
             span = max(fin[i] + tail[i] for i in range(n))
             got = (span, [fin[i] - ops[i][4] for i in range(n)])
             if best is None or span < best[0]:

@@ -1,25 +1,31 @@
-from concourse.mybir import AluOpType as A, AxisListType, ActivationFunctionType as AF
+import math
+from concourse.mybir import AluOpType as A, ActivationFunctionType as AF
 
 W, L, C = 4096, 3072, 192
 BIG = 16384.0
+KEY = 8192.0
 XB = 8 + L
 ZN = XB + 3 * C
 NULLC = ZN + 7
-TB = ZN + 8
 NREL = 320
-NTW = TB + 6 * NREL
+TI = 512
+TW = TI + NREL + 64
+NTW = ZN + 8 + NREL
+Y1 = Y2 = C
 
-F_T = dict(pc=8, g16=8, sc=8, g15=8, p16=8, s15=8, s8k=8, s8z=8, e1=8, sm15=8, i143=144, j16=128, blk=128, blks=128, trl=128,
-           trg=128, p15=128, rep=128, mk=384, md=384, md8=192, ones=320, l8f=208, b8=208, bd1=208, bd2=192, cd=16, len=16,
-           t1=24, t2=24, t3=24, dum=24, negg=192, sg=192, stc=24, sv=24, c3=16, ks=16, kd=192, k0=24, k1=24, k2=24,
-           ts=48, tp=48, cap=48, kq=48, mx=48, ns=48, nsc=48, pa=24, pb=16, th0=192, th1=192, u1=192, ff=24, yy=24, rx2=24,
-           ro=24, cr=16, zo=24, oo=24, vv=24, ee=384, v1=320, v2=320, rr=8, rm=24, isin=16, aw=8, t4=24, sv0=16, sm4k=8, idh=128, sh=8,
-           gi0=16, g1=16, xo=16, gg=192, gn=192, gd=192, en0=16, ea=16, ms0=8, ms1=8, ms2=8, vrep=384, msk=384, jd=192, jadj=192,
-           npad=224, tt=416, lq=16, tot=8, el=192, ynr=192, ta=192, tb=192, z16=16, bb=24)
-H_T = dict(big=144, hp=128, hn=128, trlh=128, trgh=128, nid=128, ss=16, idb=128, aa=192, ab=192, lh=24, zb=208, km=208, m512=192, gz=192, hl=384, fd=200, cx=200,
-           h1=208, h2=208, fa=384, fs=192, cs=16, b15=24)
-U_T = dict(so=192, kb=16, sto=16, ex=24, pd=16, ou=24, rp=24, gi=16, xu=16, eb=16, eau=16, fo=192, tg=16)
-I_T = dict(pi=8, pj=8, l8=192, sp=192, gu=192, hli=384, bi=208, kbi=16, exi=24, rpi=24, bbi=24, nn=192)
+F_T = dict(bl=16, z24=24, cr=32, ts=24, cap0=24,
+           pc=8, g16=8, sc=8, g15=8, s8k=8, e1=8, sm15=8, s192=8, skey=8, sh=8, i143=144, j16=128, blk=128,
+           nblk=128, trl=128, ntrg=128, p15=128, idh=128, i11=128, i22=128, ikey=128, mk=384, md=384, md8=192,
+           ones=320, ed=16, ln=16, bd=16, qf=16, mf=16, t1=24, t2=24, t3=24, t4=24, t5=16, dum=24, c24=24, ng=192,
+           sg=192, stc=24, sv=24, e3=16, ks=16, kd=192, cap1=24, cap2=24, tp=32, kept=24, j11=128, kq=32, mx=32,
+           pa=24, pb=16, th1=192, th2=192, u1=192, ff=16, f2=16, nf2=16, pre=24, uu=16, gv=16, xq=16, xp=16, ro=24,
+           zo=24, oo=24, vv=24, ee=384, v1=320, v2=320, rr=8, sq=32, sk=32, isin=16, q0=16, q1=16, sv0=16,
+           xo=16, gg=192, gn=192, gd=192, en0=16, ea=16, ms0=8, ms1=8, ms2=8, vrep=384, eb1=384, eb2=384, msk=384, jd=192,
+           jadj=192, np0=128, np1=128, tt0=224, tt1=224, lq=16, lq2=16, tot=8, tq=8, ta=192, tb=192, bb=24)
+H_T = dict(ss=24, cs=32, zb=192, cx=200, big=144, big2=144, hp=128, hn=128, trlh=128, eq=208, lt=208, m512=192, gz=192,
+           hl=384, fd=192, h1=208, h2=208, fa=192, fs=192, b15=24, b16=24, q192=16, mh=16)
+U_T = dict(so=192, mb=16, sto=16, stg=16, ex=24, pm=16, pe=16, pd=16, ou=24, rp=24, gi=16, xu=16, eb=16, eau=16, fo=192, tg=16)
+I_T = dict(pi=8, pj=8, li=16, sp=192, gu=192, qi=16, exi=24, rpi=24, bbi=24, nn=192)
 
 
 def _alloc(d):
@@ -39,29 +45,33 @@ for _n, _d, _t in (("pf", F_T, "float32"), ("ph", H_T, "bfloat16"), ("pu", U_T, 
         POOL[_k] = (_n, _v[0], _v[1])
 for _t in range(3):
     SCRATCH["au%d" % _t] = ("sbuf", [128, W + 16], "bfloat16")
-    SCRATCH["yy%d" % _t] = ("sbuf", [128, C + L], "float32")
     SCRATCH["mi%d" % _t] = ("sbuf", [128, 4], "float32")
 for _t in range(2):
     SCRATCH["xx%d" % _t] = ("sbuf", [128, L + 2 * C], "float32")
     SCRATCH["fl%d" % _t] = ("sbuf", [128, L], "bfloat16")
-SCRATCH["mm"] = ("sbuf", [128, L + C], "bfloat16")
-SCRATCH["on"] = ("sbuf", [128, L], "bfloat16")
+for _n, _t in (("y0", "bfloat16"), ("y1", "bfloat16"), ("y2", "float32")):
+    SCRATCH[_n] = ("sbuf", [128, C + L], _t)
+SCRATCH["fz"] = ("sbuf", [128, 8 + L // 2], "float32")
+SCRATCH["mm"] = ("sbuf", [128, L + 2 * C], "bfloat16")
 SCRATCH["selt"] = ("sbuf", [128, 2048], "bfloat16")
 SCRATCH["nt"] = ("sbuf", [128, NTW], "float32")
-SCRATCH["wr"] = ("sbuf", [128, 2 * NREL + L + 2 * C], "float32")
+SCRATCH["tab"] = ("sbuf", [128, 3 * TW], "float32")
+SCRATCH["wr"] = ("sbuf", [128, 2 * NREL + 2 * L + 2 * C + 16], "float32")
 for _t in range(8):
     SCRATCH["ps%d" % _t] = ("psum", [128, 512], "float32")
 
-SEMAPHORES = (["qv", "qa", "qp", "qg", "sent", "dl", "dsp", "dg", "da0", "da1", "do", "dn", "ra1", "ra2", "rb1", "dh0", "dh1", "dh2"]
+SEMAPHORES = (["qv", "qa", "qp", "qg", "sent", "dl", "dsp", "dg", "da0", "da1", "do0", "do1", "dn", "ra1", "ra2", "rb1"]
               + ["rr%d" % t for t in range(3)] + ["rm%d" % t for t in range(3)])
 
-GCH = 512
-SCH = 1024
-DVE_G = {0: (0, 1, 2), 1: (0, 1, 2, 3), 2: ()}
-FIN_V = (0, 1, 2)
+GCH = 768
+DVE_G = {0: (0,), 1: (), 2: ()}
+PIECES = {0: (("y0", ((5, "v"), (5, "v"), (6, "v"))),), 1: (("y1", ((5, "v"), (5, "v"), (6, "v"))),),
+          2: (("y2", ((4, "a"),)),) * 4}
+H = C // 2
+FIN = ((("a", 0, H),), (("v", 0, 64), ("a", 64, H)))
 LAG_SAME, LAG_CROSS = 60.0, 140.0
-MV = 1088
-OPT = dict(k=0, zo=0, fs=0, gn=0, late=4500, pe=0.62, af=90)
+MV = 1024
+OPT = dict(zo=1, sq=1, kq=1, late=2500, pe=0.62, af=90, tries=1500, moves=100000, seed=5)
 PLAN = {}
 
 
@@ -101,7 +111,7 @@ def _ops(g, T, topo, core):
             return 50 + 3.8 * n
         if ins and ins[0][4] == "ind":
             return 50 + 1.56 * n
-        f = 2.0 if two else (0.5 if all(x[3] == "bfloat16" for x in [out] + ins) else 1.0)
+        f = 2.0 if two else (0.5 if all(x[3] in ("bfloat16", "uint16") for x in [out] + ins) else 1.0)
         return 20 + max(64, f * n)
 
     def ap(x):
@@ -133,10 +143,14 @@ def _ops(g, T, topo, core):
     def tr(out, i):
         add("v", lambda: V.transpose(out[0], i[0]), i[1], out[1], vcost(out, [i]))
 
-    def act(out, i, fn=AF.Identity, bias=0.0, scale=1.0):
+    def act(out, i, fn=AF.Identity, bias=0.0, scale=1.0, acc=None):
         rd, wr = split(out, [i, bias, scale])
         c = 65 + 1.56 * out[2] if i[4] == "ind" else OPT["af"] + max(64, out[2])
-        add("a", lambda: S.activation(out[0], i[0], fn, bias=ap(bias), scale=ap(scale)), rd, wr, c)
+        if acc is None:
+            add("a", lambda: S.activation(out[0], i[0], fn, bias=ap(bias), scale=ap(scale)), rd, wr, c)
+        else:
+            add("a", lambda: S.activation(out[0], i[0], fn, bias=ap(bias), scale=ap(scale), accum_out=acc[0]), rd,
+                wr + acc[1], c + 25)
 
     def gat(eng, out, i):
         if eng == "v":
@@ -190,15 +204,21 @@ def _ops(g, T, topo, core):
     def D16(name, n):
         return X(name, 15, n, 16)
 
-    def sel(s):
-        return X("big", 15 - s, 143 - s)
+    def sel(s, name="big"):
+        return X(name, 15 - s, 143 - s)
 
-    def count(out, name, a, b):
-        mm([(out, [(sel(s), X(name, a + s, b, 16)) for s in range(16)])])
+    def count(out, name, a, b, start=True):
+        mm([(out, [(sel(s), X(name, a + s, b, 16)) for s in range(16)])], start=start)
 
-    col = lambda n: X(n, 0, 1)
+    def spread(bank, width, step, parts):
+        mm([(X(bank, s, width, step), [(X("selt", 128 * s, 128 * s + 128), q) for q in parts]) for s in range(16)])
 
-    dma("s", T.pi32[0:8, POOL["l8"][1]:POOL["l8"][1] + C], T.lens[:], [], X("l8")[1], "dl", 6144)
+    col = lambda n, k=0: X(n, k, k + 1)
+    ev = lambda n: X(n, 0, 24, 2)
+    od = lambda n: X(n, 1, 24, 2)
+    t12 = lambda n: X(n, 0, 12)
+
+    dma("s", X("li", 0, 12)[0], T.lens[:], [], X("li", 0, 12)[1], "dl", 6144)
     dma("s", X("sp")[0], T.spots[:], [], X("sp")[1], "dsp", 98304)
     dma("a", X("au0", 0, W // 2)[0], T.aud[:, 0:W // 2], [], X("au0", 0, W // 2)[1], "da0", 524288, 500)
     dma("s", X("gu")[0], T.gua[:], [], X("gu")[1], "dg", 98304, 300)
@@ -210,104 +230,107 @@ def _ops(g, T, topo, core):
     iota(X("pi", 0, 1), [[0, 1]], 0, 1)
     iota(X("i143"), [[1, 144]], 0, 0)
     iota(X("j16"), [[16, 8], [0, 16]], 0, 0)
-    iota(X("md"), [[0, 24], [1, 16]], 0, 0)
+    iota(X("md", 0, 16), [[1, 16]], 0, 0)
+    iota(X("md", 16, 384), [[0, 23], [1, 16]], 0, 0)
+    ms(X("pf", 0, POOL["pc"][1]), 0.0)
+    ms(X("ph", 0, POOL["big"][1]), 0.0)
     cp(col("pc"), X("pi", 0, 1))
     ts(X("pj", 0, 1), X("pi", 0, 1), 15, A.bitwise_and)
     cp(col("sc"), X("pj", 0, 1))
-    ts(X("rep"), X("j16"), 0.0625, A.mult, col("pc"), A.is_equal)
     tt(col("g16"), col("pc"), col("sc"), A.subtract)
-    ts(X("mk"), X("md"), col("sc"), A.is_equal, 16777216.0, A.mult)
-    ms(X("l8f"), 0.0)
+    ts(X("mk", 0, 16), X("md", 0, 16), col("sc"), A.is_equal, 16777216.0, A.mult)
+    ts(X("mk", 16, 384), X("md", 16, 384), col("sc"), A.is_equal, 16777216.0, A.mult)
     ms(X("mm", 0, MV), 1.0)
-    for a in range(MV, L + C, MV):
-        b = min(a + MV, L + C)
+    for a in range(MV, L, MV):
+        b = min(a + MV, L)
         act(X("mm", a, b), X("mm", 0, b - a))
-    ms(X("zb"), 0.0)
     ts(X("big"), X("i143"), -15.0, A.add, col("g16"), A.is_equal)
+    act(X("big2"), X("big"), scale=2.0)
     ts(X("blk"), X("j16"), col("g16"), A.is_equal)
-    act(X("blks"), X("blk"), scale=1.0 / 16777216.0)
+    act(X("nblk"), X("blk"), scale=-1.0)
     act(X("hp"), X("blk"), scale=0.5)
     act(X("hn"), X("blk"), scale=-0.5)
     asel(X("trl"), X("blk"), [[1, 128]], A.is_gt, 0, -1)
-    asel(X("trg"), X("blk"), [[-1, 128]], A.is_ge, 0, 1)
-    act(X("trlh"), X("trl"))
-    act(X("trgh"), X("trg"))
+    asel(X("ntrg"), X("nblk"), [[-1, 128]], A.is_ge, 0, 1)
+    asel(X("trlh"), X("hp"), [[1, 128]], A.is_gt, 0, -1)
     asel(X("p15"), X("blk"), [[-16, 8], [0, 16]], A.is_equal, -15, 1)
     asel(X("idh"), X("blk"), [[-1, 128]], A.is_equal, 0, 1)
-    act(X("nid"), X("idh"), scale=-BIG)
+    for nm, c in (("i11", -11), ("j11", 11), ("i22", -22), ("ikey", int(KEY))):
+        fill(X(nm), c)
+        asel(X(nm), X(nm), [[-1, 128]], A.is_equal, 0, 1)
     act(col("s8k"), col("sc"), scale=8192.0)
-    act(col("s8z"), col("sc"), scale=-8192.0, bias=-4096.0)
     act(col("g15"), col("g16"), scale=-BIG, bias=BIG)
-    act(col("sm15"), col("sc"), bias=-15.0)
     act(col("sh"), col("sc"), bias=0.5)
-    if OPT["fs"]:
-        act(X("idb"), X("idh"))
-    act(col("sm4k"), col("sc"), scale=-4096.0)
+    act(col("s192"), col("sc"), scale=192.0)
+    act(col("skey"), col("sc"), scale=24.0)
     iota(X("md8"), [[0, 12], [8192, 16]], 0, 0)
-    iota(X("m512"), [[0, 12], [512, 16]], 0, 0)
+    iota(X("m512"), [[0, 12], [1024, 16]], 0, 0)
     fill(X("ones"), 1)
-    for k in range(6):
-        fill(X("on", 512 * k, 512 * k + 512), 1)
-    for h in range(4):
-        asel(X("selt", 512 * h, 512 * h + 512), X("on", 0, 512), [[1, 4], [16, 8], [0, 16]], A.is_equal, 4 * h, -1)
+    for s in range(16):
+        ts(X("selt", 128 * s, 128 * s + 128), X("hp"), col("mk", s), A.mult, 2.0 / 16777216.0, A.mult)
     iota(X("jd"), [[16, C]], 0, 1)
-    ts(X("cd", 0, 12), X("jd", 0, 12), col("g16"), A.subtract)
     iota(X("exi"), [[1, 24]], 0, 0)
+    ed = t12("ed")
+    ts(ed, X("exi", 0, 12), 16.0, A.mult, col("sc"), A.add)
     cp(X("ex"), X("exi"))
-    act(X("dum", 0, 12), X("cd", 0, 12), bias=float(L))
-    act(X("dum", 12, 24), X("cd", 0, 12), bias=float(L + C))
-    act(X("c3", 0, 12), X("cd", 0, 12), scale=3.0)
-    for t in range(3):
-        fill(X("au%d" % t, W, W + 16), 0)
-    fill(X("xx0", L, L + C), 0)
-    fill(X("xx1", L, L + C), 0)
+    ts(X("c24"), X("exi"), col("skey"), A.add)
+    ts(t12("pm"), ev("c24"), 0.5, A.mult)
+    act(X("dum"), X("c24"), bias=float(L))
+    act(t12("e3"), ed, scale=3.0)
+    fill(X("au2", W, W + 16), 0)
+    fill(X("au1", W, W + 16), 0)
     for t in range(3):
         fill(X("wr", NREL * t, NREL * t + NREL), 0)
+        fill(X("tab", TW * t + TI + NREL, TW * t + TW), 0)
     fill(X("nt", 0, 8), 0)
     fill(X("nt", XB, ZN), 0)
-    fill(X("nt", ZN, ZN + 1), W)
-    fill(X("nt", ZN + 1, TB), -1)
-    for nm, a, b in (("fd", 192, 200), ("cx", 0, 1), ("cr", 0, 1), ("cs", 0, 1), ("z16", 0, 16), ("cap", 12, 24),
-                     ("npad", 0, 16), ("npad", 208, 224)):
+    fill(X("nt", ZN, NTW), -1)
+    for nm, a, b in (("np0", 0, 128), ("np1", 0, 128), ("fz", 0, 8)):
         fill(X(nm, a, b), 0)
 
     cp(X("so"), X("sp"))
-    cp(X("l8f", 1, 193, p=8), X("l8", p=8))
-    scan(X("b8", p=8), X("l8f", p=8), X("zb", p=8), 0.0, A.add, A.add)
-    mm([(X("ps6", 0, 208), [(X("rep", p=8), X("b8", p=8))])])
-    diag(X("bd1"), X("ps6", 0, 208))
-    diag(X("bd2"), X("ps6", 1, 193))
-    st, ln, cd = D16("bd1", C), X("len", 0, 12), X("cd", 0, 12)
-    tt(ln, D16("bd2", C), st, A.subtract)
-    ts(X("t1", 0, 12), ln, 1.0, A.is_lt, BIG, A.mult)
-    tt(X("t2", 0, 12), X("t1", 0, 12), st, A.add)
-    tt(X("t3", 0, 12), X("t2", 0, 12), X("dum", 0, 12), A.min)
-    cp(X("sto", 0, 12), X("t3", 0, 12))
-    cp(IND(X("mm"), X("sto", 0, 12)), X("zb", 0, C))
-    ts(X("negg"), X("gu"), -1.0, A.mult)
-    for t in range(3):
-        h = X("yy%d" % t, 0, C)
-        dma("s", h[0], X("negg")[0], X("negg")[1], h[1], "dh%d" % t, 98304, 1500)
-    cp(X("bi"), X("ps6", 0, 208))
-    ts(X("bi"), X("bi"), 15, A.bitwise_and)
-    ts(X("km"), X("bi"), col("sc"), A.is_gt)
-    cp(X("kbi", 0, 13), D16("bd1", 208))
-    ts(X("kbi", 0, 13), X("kbi", 0, 13), 4, A.logical_shift_right)
-    cp(X("kb", 0, 13), X("kbi", 0, 13))
-    act(X("gz"), X("negg"), AF.Sign, bias=-0.5, scale=-1.0)
-    count(X("ps2", 0, 12), "gz", 0, C)
-    ts(X("t1", 0, 12), X("ps2", 0, 12), 5.0, A.is_gt)
-    act(X("t4", 0, 12), ln, scale=0.5, bias=col("sm4k"))
-    tt(X("ks", 0, 12), X("t1", 0, 12), X("t4", 0, 12), A.add)
-    act(X("stc", 0, 12), st, bias=191.0)
-    act(X("stc", 12, 24), cd, scale=1.0 / 8192.0)
-    act(X("sv", 0, 12), cd, scale=16387.0, bias=16384.0 + XB - 1)
-    act(X("t4", 12, 24), cd, scale=16384.0, bias=8192.0 + 7)
-    tt(X("sv", 12, 24), X("t4", 12, 24), st, A.add)
-    act(X("sv0", 0, 12), st, bias=7.0)
-    for u in range(2):
-        act(X("ts", 24 + 12 * u, 36 + 12 * u), ln)
-        act(X("rm", 12 * u, 12 * u + 12), st, scale=-1.0, bias=float(L))
+    ln, st = t12("ln"), X("bd", 0, 12)
+    cp(ln, X("li", 0, 12))
+    scan(X("bl", 1, 13), ln, t12("z24"), 0.0, A.add, A.add)
+    mm([(col("ps6"), [(X("trl"), col("bl", 12))])])
+    ts(X("bd", 0, 13), X("bl", 0, 13), col("ps6"), A.add)
+    ts(t12("t1"), ln, 1.0, A.is_lt, BIG, A.mult)
+    tt(t12("t2"), t12("t1"), st, A.add)
+    tt(t12("t5"), t12("t2"), ev("dum"), A.min)
+    cp(t12("sto"), t12("t5"))
+    ts(t12("stg"), st, float(L - 1), A.min)
+    cp(IND(X("mm"), t12("sto")), X("zb", 0, C))
+    ts(X("ng"), IND(X("gu"), t12("pm")), -1.0, A.mult, 255.0, A.add)
+    act(X("y1", 0, C), X("ng"))
+    act(X("y2", 0, C), X("ng"))
+    ts(X("qf", 0, 13), X("bd", 0, 13), 1.0 / C, A.mult, 0.5 / C - 0.5, A.add)
+    cp(X("qi", 0, 13), X("qf", 0, 13))
+    ts(X("q192", 0, 13), X("qi", 0, 13), float(C), A.mult)
+    tt(X("mf", 0, 13), X("bd", 0, 13), X("q192", 0, 13), A.subtract)
+    cp(X("mb", 0, 13), X("mf", 0, 13))
+    act(X("mh", 0, 13), X("mf", 0, 13))
+    spread("ps2", 208, 16, [X("q192", 0, 13)])
+    ts(X("eq"), X("ps2", 0, 208), col("s192"), A.is_equal)
+    ts(X("lt"), X("ps2", 0, 208), col("s192"), A.is_gt)
+    act(X("gz"), X("ng"), AF.Sign, bias=254.5, scale=-1.0)
+    count(X("ps3", 0, 12), "gz", 0, C)
+    ts(t12("t1"), X("ps3", 0, 12), 5.0, A.is_gt)
+    ts(t12("t4"), ln, 0.5, A.mult, col("s8k"), A.subtract)
+    tt(t12("ks"), t12("t1"), t12("t4"), A.add)
+    act(X("stc", 0, 12), st, bias=float(Y2 - 1))
+    act(X("t4", 12, 24), ev("c24"), scale=KEY, bias=7.0)
+    tt(ev("sv"), X("t4", 12, 24), st, A.add)
+    act(X("t2", 12, 24), od("c24"), scale=KEY, bias=float(XB - 1))
+    tt(od("sv"), X("t2", 12, 24), t12("e3"), A.add)
+    act(t12("sv0"), st, bias=7.0)
+    act(ev("ts"), ln)
+    act(X("tp", 0, 25, 2), X("bd", 0, 13), scale=-1.0, bias=float(L))
+    act(od("tp"), X("bd", 1, 13), scale=-1.0, bias=float(L))
+    ts(t12("t3"), ln, 8192.0, A.mult)
+    tt(t12("t3"), t12("t3"), ed, A.add)
+    act(X("t3", 12, 24), X("bd", 1, 13), bias=float(Y1 - 1))
+    tt(t12("t3"), t12("t3"), X("t3", 12, 24), A.min)
+    cp(t12("pe"), t12("t3"))
     tag[0] = 1
     cp(X("ta"), X("sp"))
     act(X("hl", 0, C), X("ta"))
@@ -322,219 +345,223 @@ def _ops(g, T, topo, core):
         act(X("nt", 8 + s, 8 + L, 16), X(pb, o, o + C))
 
     def wide(t):
-        xx, yy, fl, au = "xx%d" % (t % 2), "yy%d" % t, "fl%d" % (t % 2), "au%d" % t
+        xx, fl, au = "xx%d" % (t % 2), "fl%d" % (t % 2), "au%d" % t
+        cap = "cap%d" % t
         for k in range(L // GCH):
             gat("v" if k in DVE_G[t] else "a", X(xx, GCH * k, GCH * k + GCH),
                 IND(X(au), X("so", GCH // 16 * k, GCH // 16 * (k + 1))))
-        act(X("sg"), IND(X(xx, 0, L + C), X("sto", 0, 12)))
-        tt(IND(X(xx, 0, L + C), X("sto", 0, 12)), X("sg"), X("negg"), A.add)
-        for k in range(L // SCH):
-            a, b = SCH * k, SCH * k + SCH
-            scan(X(yy, C + a, C + b), X("mm", a, b), X(xx, a, b), 0.0 if k == 0 else X(yy, C + a - 1, C + a), A.mult, A.add)
-            act(X(fl, a, b), X(yy, C + a, C + b), AF.Sign, bias=-0.5, scale=-1.0)
-            count(X("ps0", a // 16, b // 16), fl, a, b)
-        act(X("fd", 0, C), X("ps0", 0, C), AF.Sign, bias=-5.0)
-        scan(X("cx", 1, 193), X("fd", 0, C), X("zb", 0, C), 0.0, A.add, A.add)
-        act(X("h1"), IND(X("cx", 0, 193), X("kb", 0, 13)))
-        tt(X("h2"), IND(X("fd", 0, 193), X("kb", 0, 13)), X("km"), A.mult)
-        mm([(X("ps1", 0, C), [(X("hp"), X("m512")), (X("hp"), X("h2", 1, 193)), (X("hn"), X("h2", 0, C)),
-                              (X("hp"), X("h1", 1, 193)), (X("hn"), X("h1", 0, C))])])
+        act(X("sg"), IND(X(xx, 0, L), t12("stg")))
+        tt(IND(X(xx), t12("sto")), X("sg"), X("ng"), A.add)
+        mm([(X("ps1", 0, C), [(X("hp"), X("m512"))])], stop=False)
+        q, last = 0, 0.0
+        for buf, parts in PIECES[t]:
+            a, b = C * q, C * (q + sum(n for n, _ in parts))
+            scan(X(buf, C + a, C + b), X("mm", a, b), X(xx, a, b), last, A.mult, A.add)
+            last = X(buf, C + b - 1, C + b)
+            for n, e in parts:
+                a, b = C * q, C * (q + n)
+                if e == "a":
+                    act(X(fl, a, b), X(buf, C + a, C + b), AF.Sign, bias=254.5, scale=-1.0)
+                else:
+                    ts(X(fl, a, b), X(buf, C + a, C + b), 254.5, A.is_lt, 0.5, A.subtract)
+                mm([(X("ps0", 0, C), [(sel(u, "big" if e == "a" else "big2"), X(fl, C * u, C * u + C)) for u in range(q, q + n)])],
+                   start=q == 0, stop=q + n == 16)
+                q += n
+        act(X("fd"), X("ps0", 0, C), AF.Sign, bias=-5.0, acc=col("tq"))
+        scan(X("cx", 1, 193), X("fd"), X("zb", 0, C), 0.0, A.add, A.add)
+        act(X("h2"), X("lt"), scale=col("tq"))
+        tt(X("h1"), IND(X("cx", 0, 193), X("mb", 0, 13)), X("eq"), A.mult)
+        mm([(X("ps1", 0, C), [(X("hp"), X("h2", 16, 208)), (X("hn"), X("h2", 0, C))])], start=False, stop=False)
+        mm([(X("ps1", 0, C), [(X("hp"), X("h1", 16, 208)), (X("hn"), X("h1", 0, C))])], start=False)
         diag(X("kd"), X("ps1", 0, C))
-        tt(X("k%d" % t, 0, 12), D16("kd", C), X("ks", 0, 12), A.add)
-        if OPT["k"] and t > 0:
-            act(X("k%d" % t, 12, 24), X("k%d" % t, 0, 12))
-        else:
-            tt(X("k%d" % t, 12, 24), D16("kd", C), X("ks", 0, 12), A.add)
+        tt(ev(cap), D16("kd", C), t12("ks"), A.add)
+        if t == 1:
+            tt(od(cap), ln, ev(cap), A.is_lt)
+            act(X("th1"), IND(X("y1"), t12("pe")), scale=-1.0, bias=255.0)
+
+    def second():
+        tt(X("pa", 0, 12), ev("ts"), X("stc", 0, 12), A.add)
+        mm([(X("ps6", 0, 12), [(X("ikey"), ev("ts")), (X("idh"), ed)])])
+        tt(t12("pb"), X("pa", 0, 12), X("ps6", 0, 12), A.min)
+        cp(t12("pd"), t12("pb"))
+        tt(t12("ea"), t12("en0"), od("ts"), A.mult)
+        ts(t12("eau"), t12("ea"), float(W), A.add)
+        act(t12("xq"), ev("ts"))
+
+    def second_b():
+        act(X("th2"), IND(X("y2"), t12("pd")), scale=-1.0, bias=255.0)
+        tt(X("u1"), IND(X("au2"), t12("eau")), X("th2"), A.subtract)
+        act(X("fa"), X("u1"), AF.Sign, bias=-0.5, scale=-1.0)
+        act(X("th2"), X("u1"), scale=-1.0)
+        count(X("ps1", 256, 268), "fa", 0, C)
+        ts(t12("f2"), X("ps1", 256, 268), 5.0, A.is_gt)
+        act(t12("nf2"), t12("f2"), scale=-1.0, bias=1.0)
+        tt(t12("ff"), t12("xq"), ev("cap2"), A.is_lt)
+        tt(od("cap2"), t12("ff"), t12("f2"), A.add)
 
     def visit(t):
-        yy, au, mi = "yy%d" % t, "au%d" % t, "mi%d" % t
-        rel, inn = TB + 2 * NREL * t, TB + 2 * NREL * t + NREL
-        n, y, m = X("ts", 24, 36), X("cap", 12, 24), X("cap", 24, 36)
-        ro, rx, s = X("ro", 12, 24), X("ro", 0, 12), X("ss", 0, 12)
-        tt(X("pa"), X("ts", 24, 48), X("stc"), A.add)
-        ts(X("pb", 0, 12), X("pa", 12, 24), 8192.0, A.mult)
-        tt(X("pb", 0, 12), X("pa", 0, 12), X("pb", 0, 12), A.min)
-        cp(X("pd", 0, 12), X("pb", 0, 12))
-        yd = IND(X(yy), X("pd", 0, 12))
-        act(X("fa", C, 2 * C), yd, AF.Sign, bias=-0.5, scale=-1.0)
-        if t > 0:
-            act(X("th0"), yd, scale=1.0 if OPT["fs"] else -1.0)
-        tt(X("cap", 24, 48), X("ts", 24, 48), X("k%d" % t), A.min)
+        au, mi, cap = "au%d" % t, "mi%d" % t, "cap%d" % t
+        rel, inn = TW * t, TW * t + TI
+        m, y, s = ev("kept"), od("kept"), od("ss")
         if t == 0:
-            count(X("ps2", 0, 12), "fa", C, 2 * C)
-            ts(s, X("ps2", 0, 12), 5.0, A.is_gt)
-        elif t == 1:
-            count(X("ps2", 0, 12), "fa", C, 2 * C)
-            ts(X("ff", 0, 12), X("ps2", 0, 12), 5.0, A.is_gt)
-            tt(y, X("ts", 12, 24), X("ff", 0, 12), A.mult)
+            tt(s, ln, ev(cap), A.is_lt)
         else:
-            tt(X("ea", 0, 12), X("en0", 0, 12), X("ts", 12, 24), A.mult)
-            ts(X("eau", 0, 12), X("ea", 0, 12), float(W), A.add)
-            if OPT["fs"]:
-                act(X("aa"), IND(X(au), X("eau", 0, 12)))
-                mm([(X("ps6", 0, C), [(X("idh"), X("th0")), (X("idb"), X("aa"))])])
-                act(X("fa", 0, C), X("ps6", 0, C), AF.Sign, bias=-0.5, scale=-1.0)
+            tt(t12("uu"), ev("ts"), ev(cap), A.is_ge)
+            if t == 1:
+                mm([(X("ps2", 0, 12), [(X("i11"), od("ts")), (X("i22"), t12("uu"))])], stop=False)
             else:
-                tt(X("u1"), IND(X(au), X("eau", 0, 12)), X("th0"), A.subtract)
-                act(X("fa", 0, C), X("u1"), AF.Sign, bias=-0.5, scale=-1.0)
-                act(X("th1"), X("u1"), scale=-1.0)
-            count(X("ps2", 0, 24), "fa", 0, 2 * C)
-            ts(X("ff"), X("ps2", 0, 24), 5.0, A.is_gt)
-            tt(X("yy"), X("ts", 0, 24), X("ff"), A.mult)
-            tt(X("ts", 12, 24), X("ts", 0, 12), X("ts", 12, 24), A.add)
-            tt(y, X("yy", 0, 12), X("yy", 12, 24), A.add)
-        a0 = 12 if t == 0 else 0
-        tt(X("ro", a0, 24), X("ts", 12 + a0, 36), X("cap", 12 + a0, 36), A.subtract)
-        scan(X("cr", 1, 13), ro, X("z16", 0, 12) if t == 0 else rx, 0.0, A.add, A.add)
-        mm([(X("ps3", 12 * u, 12 * u + 12), [(X("trl"), X("cr", 1, 13)), (X("trg"), X("cr", 0, 12))]) for u in range(2)]
-           + [(X("ps3", 24, 25), [(X("blk"), X("cr", 12, 13))])])
+                tt(t12("gv"), od("ts"), y, A.min)
+                tt(t12("xp"), t12("gv"), t12("nf2"), A.min)
+                mm([(X("ps2", 0, 12), [(X("i11"), od("ts")), (X("j11"), t12("gv")), (X("i22"), t12("uu")),
+                                       (X("i22"), t12("xp"))])], stop=False)
+        tt(X("kept"), X("ts"), X(cap), A.min)
+        tt(X("ro"), X("ts"), X("kept"), A.subtract)
+        scan(X("cr", 1, 25), X("ro"), X("z24"), 0.0, A.add, A.add)
+        c24 = col("cr", 24)
+        mm([(col("ps5"), [(X("trl"), c24)])])
+        mm([(col("ps4", 0), [(X("ntrg"), c24)]), (col("ps4", 1), [(X("blk"), c24)])])
+        mm([(col("ps3"), [(X("blk"), c24)])], stop=False)
         if OPT["zo"]:
-            act(X("zo", a0, 24), X("ro", a0, 24), AF.Relu, scale=-BIG, bias=BIG)
+            act(X("zo"), X("ro"), AF.Relu, scale=-BIG, bias=BIG)
         else:
-            ts(X("zo", a0, 24), X("ro", a0, 24), 1.0, A.is_lt, BIG, A.mult)
-        q = 16 * (24 - a0)
+            ts(X("zo"), X("ro"), 1.0, A.is_lt, BIG, A.mult)
+        tt(X("pre"), X("zo"), X("cr", 0, 24), A.add)
+        tt(X("pre"), X("pre"), X("dum"), A.min)
+        k = 12 if t == 0 else 24
         if t > 0:
-            tt(X("zo", 0, 12), X("zo", 0, 12), ro, A.add)
-            tt(X("vv"), X("cap", 12, 36), X("sv"), A.add)
-            act(X("ee"), IND(X("vv"), X("ex")))
+            tt(X("vv"), X("kept"), X("sv"), A.add)
+            ts(X("ou"), X("pre"), col("ps5"), A.add)
         else:
-            tt(X("vv", 0, 12), m, X("sv0", 0, 12), A.add)
-            act(X("ee", 0, q), IND(X("vv", 0, 12), X("ex", 0, 12)))
-        tt(X("oo", a0, 24), X("ps3", a0, 24), X("zo", a0, 24), A.add)
-        tt(X("oo", a0, 24), X("oo", a0, 24), X("dum", a0, 24), A.min)
-        cp(X("ou", a0, 24), X("oo", a0, 24))
+            tt(t12("vv"), m, t12("sv0"), A.add)
+            ts(t12("ou"), ev("pre"), col("ps5"), A.add)
+        act(X("ee", 0, 16 * k), IND(X("vv", 0, k), X("ex", 0, k)), scale=1.0 / 16777216.0)
         w0 = NREL * (2 - t)
-        tt(IND(X("wr", w0, w0 + L + 2 * C), X("ou", a0, 24)), X("ee", 0, q), X("mk", 0, q), A.mult)
-        mm([(X("ps5", 0, NREL), [(X("blks"), X("wr", w0, w0 + NREL))])])
-        act(col("rr"), X("ps3", 24, 25))
-        act(X("rr", 1, 2), X("ps3", 24, 25), scale=-0.5, bias=NREL / 2.0)
-        tt(X("kq", 24, 48), X("ps3", 0, 24), X("rm"), A.add)
+        tt(IND(X("wr", w0, w0 + 2 * L + 2 * C + 16), X("ou", 0, k)), X("ee", 0, 16 * k), X("mk", 0, 16 * k), A.mult)
+        mm([(X("ps5", 0, NREL), [(X("blk"), X("wr", w0, w0 + NREL))])])
+        if OPT["kq"]:
+            mm([(X("ps4", 16, 41), [(X("idh"), X("tp", 0, 25)), (X("idh"), X("cr", 0, 25))])])
+            ts(X("kq", 0, 25), X("ps4", 16, 41), col("ps4", 0), A.add)
+        else:
+            tt(X("kq", 0, 25), X("tp", 0, 25), X("cr", 0, 25), A.add)
+            ts(X("kq", 0, 25), X("kq", 0, 25), col("ps4", 0), A.add)
+        mm([(col("ps4", 2), [(X("nblk"), c24)])], stop=False)
         scan(X("v1"), X("ps5", 0, NREL), X("ones"), 0.0, A.max, A.add)
         diag(X("v2"), X("v1"))
         if t == 0:
-            ts(X("rp", 0, 20), D16("v2", NREL), float(NULLC), A.min)
+            cp(X("rp", 0, 20), D16("v2", NREL))
         else:
             cp(X("rpi", 0, 20), D16("v2", NREL))
             ts(X("rpi", 0, 20), X("rpi", 0, 20), 8191, A.bitwise_and)
-            ts(X("rp", 0, 20), X("rpi", 0, 20), float(NULLC), A.min)
-        act(X("nt", rel, rel + NREL), IND(X("nt", 0, TB), X("rp", 0, 20)))
-        remote(r + 1, X("nt", inn, inn + NREL), X("nt", rel, rel + NREL), "rr%d" % t, 163840)
-        if t > 0 and OPT["fs"]:
-            act(X("ab"), IND(X(au), X("eb", 0, 12)))
-            mm([(X("ps6", 0, C), [(X("idh"), X("th0"))] + ([(X("idb"), X("aa"))] if t == 2 else []) + [(X("idb"), X("ab"))])])
-            act(X("fs"), X("ps6", 0, C), AF.Sign, bias=-0.5, scale=-1.0)
-            count(X("ps2", 32, 44), "fs", 0, C)
-            ts(s, X("ps2", 32, 44), 5.0, A.is_gt)
-        elif t > 0:
-            tt(X("fs"), IND(X(au), X("eb", 0, 12)), X("th0" if t == 1 else "th1"), A.is_lt)
-            count(X("ps2", 32, 44), "fs", 0, C)
-            ts(s, X("ps2", 32, 44), 10.5, A.is_gt)
-        scan(X("cs", 1, 13), s, X("z16", 0, 12), 0.0, A.add, A.add)
-        c12 = X("cs", 12, 13)
-        mm([(X("ps4", 256, 257), [(X("blk"), X("cr", 12, 13)), (X("hn"), c12), (X("hn"), c12)]),
-            (X("ps4", 257, 258), [(X("hp"), c12)])])
-        mo = "ms%d" % t
-        ts(X(mo, 0, 2), X("ps4", 256, 258), 0.0, A.max, 128.0, A.min)
-        remote(r + 1, X(mi, 0, 2), X(mo, 0, 2), "rm%d" % t, 1024)
-        pre = [(X("trlh"), X("cs", 1, 13)), (X("trgh"), X("cs", 0, 12))]
-        mm([(X("ps4", 12 * u, 12 * u + 12), pre) for u in range(a0 // 12, 4)] + [(X("ps4", 48, 60), pre + [(X("nid"), s)])])
-        sg = X("ps4", 12, 24)
-        ts(X("isin", 0, 12), sg, col("rr"), A.is_ge, 2.0, A.mult)
-        tt(X("kq", 12, 24), X("kq", 36, 48), m, A.subtract)
+            cp(X("rp", 0, 20), X("rpi", 0, 20))
+        act(X("tab", rel, rel + NREL), IND(X("nt"), X("rp", 0, 20)))
+        remote(r + 1, X("tab", inn, inn + NREL), X("tab", rel, rel + NREL), "rr%d" % t, 163840)
         if t > 0:
-            tt(X("kq", 0, 12), X("kq", 12, 24), y, A.subtract)
-            tt(X("xo", 0, 12), y, X("c3", 0, 12), A.add)
-            cp(X("xu", 0, 12), X("xo", 0, 12))
-        tt(X("aw", 0, 2), X(mi, 0, 2), X("rr", 0, 2), A.add)
-        ts(X("mx", a0, 48), X("ps4", a0, 48), col("aw"), A.min)
-        ts(X("cap", a0, a0 + 12), X("ps4", 48, 60), BIG, A.add, col("aw"), A.is_lt)
-        tt(X("tp", a0, 48), X("kq", a0, 48), X("mx", a0, 48), A.subtract)
-        tt(X("ts", a0, 48), X("tp", a0, 48), X("cap", a0, 48), A.min)
-        ts(X("ts", a0, 48), X("ts", a0, 48), 0.0, A.max)
+            tt(X("fs"), IND(X(au), t12("eb")), X("th%d" % t), A.is_lt)
+            count(X("ps2", 0, 12), "fs", 0, C, start=False)
+            ts(s, X("ps2", 0, 12), -0.5, A.is_gt)
+        scan(X("cs", 1, 25), X("ss"), X("z24"), 0.0, A.add, A.add)
+        s24 = col("cs", 24)
+        mm([(col("ps3"), [(X("hn"), s24), (X("hn"), s24)])], start=False)
+        mm([(col("ps3", 1), [(X("hp"), s24)])])
+        mo = "ms%d" % t
+        ts(X(mo, 0, 2), X("ps3", 0, 2), 0.0, A.max, 128.0, A.min)
+        remote(r + 1, X(mi, 0, 2), X(mo, 0, 2), "rm%d" % t, 1024)
+        mm([(col("ps4", 2), [(X("trlh"), s24), (X("trlh"), s24)])], start=False)
+        if OPT["sq"]:
+            act(col("rr", 3), col("ps4", 2))
+            act(X("sq", 0, 25), X("cs", 0, 25), bias=col("rr", 3))
+        else:
+            ts(X("sq", 0, 25), X("cs", 0, 25), col("ps4", 2), A.add)
+        tt(X("sk", 0, 25), X("sq", 0, 25), X("kq", 0, 25), A.min)
+        ts(t12("isin"), od("sq"), 0.0, A.is_ge, float(TI), A.mult)
+        ts(t12("q0"), t12("isin"), col("ps4", 1), A.max)
+        tt(t12("q0"), t12("q0"), od("sq"), A.add)
+        if t > 0:
+            mm([(X("ps4", 48, 60), [(X("idh"), y), (X("idh"), t12("e3"))])])
+            cp(t12("xu"), X("ps4", 48, 60))
+        ts(t12("q1"), t12("isin"), col(mi, 1), A.mult, 2.0 / TI, A.mult)
+        tt(t12("q1"), t12("q1"), t12("q0"), A.add)
+        cp(t12("gi"), t12("q1"))
+        ts(X("mx", 0, 25), X("sk", 0, 25), col(mi), A.min)
+        tt(X("tp", 0, 25), X("kq", 0, 25), X("mx", 0, 25), A.subtract)
+        tt(X("ts"), X("tp", 0, 24), X("tp", 1, 25), A.subtract)
+        gw = IND(X("tab", rel, rel + TW), t12("gi"))
         if t < 2:
-            act(X("rm"), X("tp", 24, 48), AF.Relu)
-        ts(X("g1", 0, 12), X("isin", 0, 12), X("aw", 1, 2), A.mult, float(rel - ZN), A.add)
-        tt(X("g1", 0, 12), X("g1", 0, 12), sg, A.add)
-        tt(X("g1", 0, 12), X("g1", 0, 12), X("ts", a0, a0 + 12), A.mult)
-        cp(X("gi", 0, 12), X("g1", 0, 12))
-        gw = IND(X("nt", ZN, inn + NREL), X("gi", 0, 12))
-        if t < 2:
-            if OPT["gn"]:
-                act(X("gn"), gw)
-                mm([(X("ps7", 0, C), [(X("idh"), X("md8")), (X("idh"), X("gn"))])])
-                diag(X("gd"), X("ps7", 0, C))
-            else:
-                tt(X("gn"), gw, X("md8"), A.add)
-                diag(X("gd"), X("gn"))
-            ts(X("eb", 0, 12), D16("gd", C), col("s8k"), A.subtract)
+            tt(X("gn"), gw, X("md8"), A.add)
+            diag(X("gd"), X("gn"))
+            ts(t12("eb"), D16("gd", C), col("s8k"), A.subtract)
         if t == 0:
-            act(X("en0", 0, 12), D16("gd", C), bias=col("s8z"))
+            ts(t12("en0"), D16("gd", C), col("s8k"), A.subtract, float(W), A.subtract)
             act(X("nt", XB, ZN, 3), gw)
+            second()
         else:
             act(X("gg"), gw)
-            cp(IND(X("nt", XB, ZN), X("xu", 0, 12)), X("gg"))
+            cp(IND(X("nt", XB, ZN), t12("xu")), X("gg"))
 
     def final_static():
-        iota(X("vrep", 0, C), [[16387, C]], 16384 + XB - 1, 0)
-        iota(X("el"), [[16384, C]], 8192 + 7, 0)
-        mm([(X("ps7", 0, C), [(X("idh"), X("el")), (X("rep", p=8), X("b8", 0, C, p=8))])])
-        act(X("vrep", C, 2 * C), X("ps7", 0, C))
-        iota(X("ta"), [[1, 16], [32, 6], [224, 2]], 0, 0)
-        iota(X("tb"), [[0, 16], [0, 6], [-416, 2]], 208, 0)
+        iota(X("eb1"), [[2, 12], [1, 2], [24, 16]], 0, 0)
+        iota(X("eb2"), [[48, 12], [0, 2], [3, 16]], XB - 8, 0)
+        asel(X("eb2"), X("eb2"), [[0, 12], [1, 2], [0, 16]], A.is_gt, 0, 0)
+        mm([(X("ps7", 0, 2 * C), [(X("ikey"), X("eb1")), (X("idh"), X("eb2"))])], stop=False)
+        mm([(X("ps7", s, 2 * C, 32), [(X("selt", 128 * s, 128 * s + 128), q) for q in (t12("q192"), t12("mh"))])
+            for s in range(16)], start=False, stop=False)
+        mm([(X("ps7", 0, 16), [(X("hp"), X("zb", 0, 16))])], start=False)
+        act(X("vrep"), X("ps7", 0, 2 * C), bias=KEY + 8.0 + L)
+        iota(X("ta", 0, H), [[1, 16], [32, 3], [128, 2]], 0, 0)
+        iota(X("tb", 0, H), [[0, 16], [0, 3], [-224, 2]], 112, 0)
         ts(X("pj", 1, 2), X("pi", 0, 1), 4, A.logical_shift_right, 1, A.bitwise_and)
         cp(col("e1"), X("pj", 1, 2))
-        act(X("tb"), X("tb"), scale=col("e1"))
-        mm([(X("ps7", 0, C), [(X("idh"), X("ta")), (X("idh"), X("tb")), (X("idh"), X("md8"))])])
-        diag(X("ta"), X("ps7", 0, C))
-        ts(X("tg", 0, 12), D16("ta", C), col("s8k"), A.subtract)
+        act(X("tb", 0, H), X("tb", 0, H), scale=col("e1"))
+        mm([(X("ps7", 0, H), [(X("idh"), X("ta", 0, H)), (X("idh"), X("tb", 0, H)), (X("idh"), X("md8", 0, H))])])
+        diag(X("ta", 0, H), X("ps7", 0, H))
+        ts(X("tg", 0, 6), D16("ta", H), col("s8k"), A.subtract)
+        act(col("sm15"), col("g16"), scale=-1.0, bias=-float(L))
+        mm([(X("ps0", 0, C), [(X("idh"), X("jd"))])], stop=False)
 
     def final():
-        n = X("ts", 24, 36)
-        ts(X("bb", 12, 24), X("tp", 24, 36), -1.0, A.mult, float(L), A.add)
-        tt(X("bb", 0, 12), X("bb", 12, 24), n, A.add)
-        cp(X("bbi"), X("bb"))
+        ts(X("bbi"), X("tp", 0, 24), -1.0, A.mult, float(L), A.add)
         ts(X("bbi"), X("bbi"), 15, A.bitwise_and)
         cp(X("b15"), X("bbi"))
-        mm([(X("ps6", s, 384, 16), [(X("selt", 128 * s, 128 * s + 128), X("b15"))]) for s in range(16)])
-        tt(X("ts", 12, 24), X("ts", 0, 12), X("ts", 12, 24), A.add)
-        ts(X("zo"), X("ts", 12, 36), 1.0, A.is_lt, BIG, A.mult)
+        spread("ps7", 2 * C, 16, [X("b15")])
+        act(X("bb"), X("tp", 0, 24), scale=-1.0, bias=float(L))
+        tt(X("b16"), X("bb"), X("b15"), A.subtract)
+        spread("ps6", 2 * C, 16, [X("b16")])
+        act(X("zo"), X("ts"), AF.Relu, scale=-BIG, bias=BIG)
         tt(X("oo"), X("bb"), X("zo"), A.add)
         tt(X("oo"), X("oo"), X("dum"), A.min)
         cp(X("ou"), X("oo"))
-        act(X("msk"), X("ps6", 0, 384), AF.Sign, scale=-1.0, bias=col("sh"))
-        tt(IND(X("xx1"), X("ou")), X("vrep"), X("msk"), A.mult)
-        scan(X("yy1", C, C + L), X("xx1", 0, L), X("on"), 0.0, A.max, A.add)
-        lq = X("lq", 0, 12)
-        tt(lq, n, X("ts", 12, 24), A.add)
-        act(X("lh", 0, 12), lq)
-        act(X("t4", 0, 12), X("lh", 0, 12), scale=-1.0)
-        mm([(X("ps3", 0, 12), [(X("idh"), lq), (X("idh"), X("t4", 0, 12))])])
-        act(X("lh", 12, 24), X("ps3", 0, 12))
-        mm([(X("ps4", s, C, 16), [(X("selt", 128 * s, 128 * s + 128), X("lh", 0, 12)),
-                                  (X("selt", 128 * s, 128 * s + 128), X("lh", 12, 24))]) for s in range(16)])
-        add("a", lambda: S.activation(X("ynr")[0], X("ps4", 0, C)[0], AF.Identity, accum_out=col("tot")[0]),
-            X("ps4", 0, C)[1], X("ynr")[1] + col("tot")[1], 300.0)
-        act(X("tot", 1, 2), col("tot"), scale=-BIG, bias=col("g15"))
-        act(X("jadj"), X("jd"), AF.Relu, scale=BIG, bias=X("tot", 1, 2))
-        act(X("ps7", 0, C), X("jadj"), bias=col("sm15"))
-        o = POOL["ynr"][1]
-        dma("s", T.yn[:], T.pf[0:128:16, o:o + C], X("ynr")[1], [], "dn", 6144)
-        mm([(X("ps5", 0, C), [(X("blk"), X("ones", 0, C))])], stop=False)
-        mm([(X("ps5", 0, C), [(X("p15"), X("yy1", C - 1, C - 1 + L, 16))])], start=False)
-        tt(X("nn"), X("ps5", 0, C), X("yy1", C + 15, C + L, 16), A.max)
-        ts(X("nn"), X("nn"), 8191, A.bitwise_and)
-        tt(X("npad", 16, 208), X("nn"), X("ps7", 0, C), A.add)
-        tr(X("tt", 0, C), X("npad", 16, 208))
-        tr(X("tt", C, C + 224), X("npad"))
-        ts(X("fo"), IND(X("tt"), X("tg", 0, 12)), float(NULLC), A.min)
-        h = L // 2
-        for k in range(2):
-            gat("va"[k], X("xx0", h * k, h * k + h), IND(X("nt", 0, TB), X("fo", h // 16 * k, h // 16 * (k + 1))))
-        dma("s", T.yo[:], T.xx0[0:128:16, 0:L], X("xx0", 0, L)[1], [], "do", 98304)
+        tt(X("eb1"), X("vrep"), X("ps7", 0, 2 * C), A.subtract)
+        act(X("msk"), X("ps7", 0, 2 * C), AF.Sign, scale=-1.0, bias=col("sh"))
+        tt(X("eb2"), X("eb1"), X("ps6", 0, 2 * C), A.subtract)
+        tt(IND(X("xx1"), X("ou")), X("eb2"), X("msk"), A.mult)
+        lq = t12("lq")
+        tt(lq, ev("ts"), od("ts"), A.add)
+        act(t12("lq2"), lq, acc=col("tot"))
+        mm([(col("ps3"), [(X("blk"), col("tot"))])])
+        act(col("tot", 1), col("ps3"), scale=-BIG, bias=col("g15"))
+        act(X("jadj"), X("jd"), AF.Relu, scale=BIG, bias=col("tot", 1))
+        mm([(X("ps0", 0, C), [(X("idh"), X("jadj"))])], start=False)
+        dma("s", T.yn[:], lq[0], lq[1], [], "dn", 6144)
+        for h in range(2):
+            a, z, pb, pad, tw = 16 * H * h, 8 + 8 * H * h, ("ps5", "ps1")[h], "np%d" % h, "tt%d" % h
+            scan(X("fz", z, z + 8 * H), X("xx1", a, a + 16 * H, 2), X("xx1", a + 1, a + 16 * H, 2),
+                 col("fz", z - 1) if h else 0.0, A.max, A.max)
+            mm([(X(pb, 0, H), [(X("p15"), X("fz", z - 1, z - 1 + 8 * H, 8))])])
+            nn = X("nn", H * h, H * h + H)
+            tt(nn, X(pb, 0, H), X("fz", z + 7, z + 8 * H, 8), A.max)
+            ts(nn, nn, 8191, A.bitwise_and)
+            tt(X(pad, 16, 16 + H), nn, X("ps0", H * h, H * h + H), A.add)
+            tr(X(tw, 0, H), X(pad, 16, 16 + H))
+            tr(X(tw, H, 2 * H + 32), X(pad))
+            ts(X("fo", H * h, H * h + H), IND(X(tw), X("tg", 0, 6)), col("sm15"), A.add, float(NULLC), A.min)
+            for e, u, w in FIN[h]:
+                gat(e, X("xx0", a + 16 * u, a + 16 * w), IND(X("nt"), X("fo", H * h + u, H * h + w)))
+            dma("s", T.yo[:, H * h:H * h + H], T.xx0[0:128:16, a:a + 16 * H], X("xx0", a, a + 16 * H)[1], [], "do%d" % h, 49152, 300)
 
-    for k, (f, t) in enumerate(((wide, 0), (wide, 1), (visit, 0), (wide, 2), (final_static, 0), (visit, 1), (visit, 2), (final, 0))):
+    for k, (f, t) in enumerate(((wide, 0), (wide, 1), (visit, 0), (wide, 2), (second_b, None), (visit, 1), (final_static, None),
+                                (visit, 2), (final, None))):
         tag[0] = 2 + k
-        if f is final or f is final_static:
+        if t is None:
             f()
         else:
             f(t)
@@ -550,7 +577,9 @@ def _deps(ops):
                 ps = SCRATCH[buf][0] == "psum"
                 for j, a2, b2, w2 in hist.get(buf, []):
                     over = a < b2 and a2 < b
-                    if over and (w or w2) and not (w and w2 and buf == "nt" and o[8] == 1 and ops[j][8] == 1):
+                    if ps and o[0] == "p" and ops[j][0] == "p":
+                        d.setdefault(j, False)
+                    elif over and (w or w2) and not (w and w2 and buf == "nt" and o[8] == 1 and ops[j][8] == 1):
                         d[j] = True
                     elif (over and (w or w2)) or (ps and ops[j][0] != o[0]):
                         d.setdefault(j, False)
@@ -580,12 +609,105 @@ def _place(ops, edges, order, rel):
     return fin
 
 
-def _schedule(ops, tries=1500, seed=5):
+def _anneal(ops, fw, bw, start, tries, seed, hot=250.0, cold=10.0, reach=8):
+    n = len(ops)
+    cost, tail = [o[4] for o in ops], [o[5] for o in ops]
+    seqs = {}
+    for i in sorted(range(n), key=lambda k: (start[k], k)):
+        seqs.setdefault(ops[i][0], []).append(i)
+    npre = [len(f) for f in fw]
+
+    def times():
+        prev, nxt, left = [-1] * n, [-1] * n, list(npre)
+        for s in seqs.values():
+            for a, b in zip(s, s[1:]):
+                prev[b], nxt[a] = a, b
+                left[b] += 1
+        todo = [i for i in range(n) if left[i] == 0]
+        fin, why, done = [0.0] * n, [-1] * n, 0
+        while todo:
+            i = todo.pop()
+            done += 1
+            t, w = 0.0, -1
+            for j, lag in fw[i]:
+                if fin[j] + lag > t:
+                    t, w = fin[j] + lag, j
+            if prev[i] >= 0 and fin[prev[i]] >= t:
+                t, w = fin[prev[i]], -2 - prev[i]
+            fin[i], why[i] = t + cost[i], w
+            for j, _ in bw[i]:
+                left[j] -= 1
+                if left[j] == 0:
+                    todo.append(j)
+            j = nxt[i]
+            if j >= 0:
+                left[j] -= 1
+                if left[j] == 0:
+                    todo.append(j)
+        if done < n:
+            return None
+        last = max(range(n), key=lambda k: fin[k] + tail[k])
+        return fin[last] + tail[last], fin, why, last
+
+    st = [seed]
+
+    def rnd():
+        st[0] = (st[0] * 1103515245 + 12345) % 2147483648
+        return st[0] / 2147483648.0
+
+    best = cur = times()
+    links = None
+    for it in range(tries):
+        if links is None:
+            links, i = [], cur[3]
+            while i >= 0:
+                w = cur[2][i]
+                if w <= -2:
+                    w = -2 - w
+                    if w >= 8:
+                        links.append((w, i))
+                i = w
+            if not links:
+                break
+        u, v = links[int(rnd() * len(links))]
+        s = seqs[ops[u][0]]
+        a, k = s.index(u), int(rnd() ** 2 * reach)
+        if rnd() < 0.5:
+            lo = max(a - k, 0)
+            while s[lo] < 8:
+                lo += 1
+            old = s[lo:a + 2]
+            s[lo:a + 2] = [v] + old[:-1]
+        else:
+            lo = a
+            old = s[a:a + 2 + k]
+            s[a:a + 2 + k] = old[1:] + [u]
+        got = times()
+        if got is not None and (got[0] <= cur[0] or rnd() < math.exp((cur[0] - got[0]) / (hot * (cold / hot) ** (it / tries)))):
+            cur, links = got, None
+            if got[0] < best[0]:
+                best = got
+        else:
+            s[lo:lo + len(old)] = old
+    return best[0], [best[1][i] - cost[i] for i in range(n)]
+
+
+def _schedule(ops, tries, seed):
     deps = _deps(ops)
     n = len(ops)
     fw, bw = [[] for _ in ops], [[] for _ in ops]
+    anc = []
     for i in range(n):
+        far = 0
+        for j in deps[i]:
+            far |= anc[j]
+        near = far
+        for j in deps[i]:
+            near |= 1 << j
+        anc.append(near)
         for j, raw in deps[i].items():
+            if far >> j & 1 and ops[j][6] is None:
+                continue
             lag = (LAG_SAME if raw else 0.0) if (ops[j][0] == ops[i][0] and ops[j][6] is None) else ops[j][5] + LAG_CROSS
             fw[i].append((j, lag))
             bw[j].append((i, lag))
@@ -595,25 +717,25 @@ def _schedule(ops, tries=1500, seed=5):
         rank = [0.0] * n
         if it < warm:
             fac = []
-            for _ in range(10):
+            for _ in range(12):
                 seed = (seed * 1103515245 + 12345) % 2147483648
                 fac.append(0.05 + 2.0 * (seed / 2147483648.0) ** 2)
             for i in range(n - 1, -1, -1):
                 seed = (seed * 1103515245 + 12345) % 2147483648
                 rank[i] += ((ops[i][4] + 70) * (1.0 + 0.3 * seed / 2147483648.0) + ops[i][5]) * fac[ops[i][8]]
-                for j in deps[i]:
+                for j, _ in fw[i]:
                     rank[j] = max(rank[j], rank[i] + 1e-3)
         else:
             rnd = []
             for _ in range(6):
                 seed = (seed * 1103515245 + 12345) % 2147483648
                 rnd.append(seed / 2147483648.0)
-            mid, wid, sh, tg = rnd[0] * cur[0], 500 + 6000 * rnd[1], (rnd[2] - 0.5) * 8000, int(rnd[3] * 10)
+            mid, wid, sh, tg = rnd[0] * cur[0], 500 + 6000 * rnd[1], (rnd[2] - 0.5) * 8000, int(rnd[3] * 12)
             rank = [-1e9] * n
             for i in range(n - 1, -1, -1):
                 hit = abs(cur[1][i] - mid) < wid and (ops[i][8] == tg or (rnd[4] < 0.3 and (i * 7 + it) % 5 == 0))
                 rank[i] = max(rank[i], -cur[1][i] + (sh if hit else 0.0))
-                for j in deps[i]:
+                for j, _ in fw[i]:
                     rank[j] = max(rank[j], rank[i] + 1e-3)
         order = sorted(range(n), key=lambda k: (-rank[k], k))
         for _ in range(4 if it < warm else 2):
@@ -628,6 +750,7 @@ def _schedule(ops, tries=1500, seed=5):
                 cur = got
             back = _place(ops, bw, sorted(range(n), key=lambda k: (-fin[k] - tail[k], -k)), tail)
             order = sorted(range(n), key=lambda k: (-back[k], k))
+    best = _anneal(ops, fw, bw, best[1], OPT["moves"], seed)
     order = sorted(range(n), key=lambda k: (best[1][k], k))
     need, waits, know, seen, pos, cnt = set(), {}, {}, {}, {}, {}
     for i in order:
@@ -660,7 +783,7 @@ def rank_program(g, core, T, topo):
         return
     ops = _ops(g, T, topo, core)
     if "p" not in PLAN:
-        PLAN["p"] = _schedule(ops)
+        PLAN["p"] = _schedule(ops, OPT["tries"], OPT["seed"])
     p = PLAN["p"]
     Q = dict(v=g.vector, a=g.scalar, p=g.tensor, g=g, s=g.sync)
     sent = 0

@@ -14,17 +14,17 @@ NTW = ZN + 8 + NREL
 Y1 = Y2 = C
 
 F_T = dict(bl=16, z24=24, cr=32, ts=24, cap0=24,
-           pc=8, g16=8, sc=8, g15=8, s8k=8, e1=8, sm15=8, s192=8, skey=8, sh=8, i143=144, j16=128, blk=128,
-           nblk=128, trl=128, ntrg=128, p15=128, idh=128, i11=128, i22=128, ikey=128, mk=384, md=384, md8=192,
+           pc=8, g16=8, sc=8, g15=8, s8k=8, s8z=8, s6=8, lk=24, za=24, z2=192, g0=16, e1=8, sm15=8, s192=8, skey=8, sh=8, i143=144, j16=128, blk=128,
+           nblk=128, trl=128, ntrg=128, p15=128, idh=128, i11=128, i22=128, ikey=128, mk=384, md=16, md8=192,
            ones=320, ed=16, ln=16, bd=16, qf=16, mf=16, t1=24, t2=24, t3=24, t4=24, t5=16, dum=24, c24=24, ng=192,
            sg=192, stc=24, sv=24, e3=16, ks=16, kd=192, cap1=24, cap2=24, tp=32, kept=24, j11=128, kq=32, mx=32,
            pa=24, pb=16, th1=192, th2=192, u1=192, ff=16, f2=16, nf2=16, pre=24, uu=16, gv=16, xq=16, xp=16, ro=24,
            zo=24, oo=24, vv=24, ee=384, v1=320, v2=320, rr=8, sq=32, sk=32, isin=16, q0=16, q1=16, sv0=16,
            xo=16, gg=192, gn=192, gd=192, en0=16, ea=16, ms0=8, ms1=8, ms2=8, vrep=384, eb1=384, eb2=384, msk=384, jd=192,
            jadj=192, np0=128, np1=128, tt0=224, tt1=224, lq=16, lq2=16, tot=8, tq=8, ta=192, tb=192, bb=24)
-H_T = dict(ss=24, cs=32, zb=192, cx=200, big=144, big2=144, hp=128, hn=128, trlh=128, eq=208, lt=208, m512=192, gz=192,
+H_T = dict(ss=24, cs=32, zb=192, cx=200, big=144, on=512, big2=144, hp=128, hn=128, trlh=128, eq=208, lt=208, m512=192, gz=192,
            hl=384, fd=192, h1=208, h2=208, fa=192, fs=192, b15=24, b16=24, q192=16, mh=16)
-U_T = dict(so=192, mb=16, sto=16, stg=16, ex=24, pm=16, pe=16, pd=16, ou=24, rp=24, gi=16, xu=16, eb=16, eau=16, fo=192, tg=16)
+U_T = dict(so=192, zu=16, zw=16, mb=16, sto=16, stg=16, ex=24, pm=16, pe=16, pd=16, ou=24, rp=24, gi=16, xu=16, eb=16, eau=16, fo=192, tg=16)
 I_T = dict(pi=8, pj=8, li=16, sp=192, gu=192, qi=16, exi=24, rpi=24, bbi=24, nn=192)
 
 
@@ -49,29 +49,36 @@ for _t in range(3):
 for _t in range(2):
     SCRATCH["xx%d" % _t] = ("sbuf", [128, L + 2 * C], "float32")
     SCRATCH["fl%d" % _t] = ("sbuf", [128, L], "bfloat16")
-for _n, _t in (("y0", "bfloat16"), ("y1", "bfloat16"), ("y2", "float32")):
+for _n, _t in (("y0", "float32"), ("yb", "bfloat16"), ("y1", "bfloat16"), ("y2", "float32")):
     SCRATCH[_n] = ("sbuf", [128, C + L], _t)
 SCRATCH["fz"] = ("sbuf", [128, 8 + L // 2], "float32")
 SCRATCH["mm"] = ("sbuf", [128, L + 2 * C], "bfloat16")
 SCRATCH["selt"] = ("sbuf", [128, 2048], "bfloat16")
 SCRATCH["nt"] = ("sbuf", [128, NTW], "float32")
+SCRATCH["nd"] = ("dram", [8, L], "float32")
 SCRATCH["tab"] = ("sbuf", [128, 3 * TW], "float32")
 SCRATCH["wr"] = ("sbuf", [128, 2 * NREL + 2 * L + 2 * C + 16], "float32")
 for _t in range(8):
     SCRATCH["ps%d" % _t] = ("psum", [128, 512], "float32")
 
-SEMAPHORES = (["qv", "qa", "qp", "qg", "sent", "dl", "dsp", "dg", "da0", "da1", "do0", "do1", "dn", "ra1", "ra2", "rb1"]
+SEMAPHORES = (["qv", "qa", "qp", "qg", "sent", "dl", "dsp", "dg", "da0", "da1", "da2", "do0", "do1", "dn", "dz", "dt", "dm0", "dm1", "dm2", "dm3", "dm4", "ra0", "ra1", "ra2", "rb"]
               + ["rr%d" % t for t in range(3)] + ["rm%d" % t for t in range(3)])
 
-GCH = 768
-DVE_G = {0: (0,), 1: (), 2: ()}
-PIECES = {0: (("y0", ((5, "v"), (5, "v"), (6, "v"))),), 1: (("y1", ((5, "v"), (5, "v"), (6, "v"))),),
+GCH = 512
+DVE_G = {0: (0, 1, 2), 1: (0, 1), 2: ()}
+PIECES = {0: (("y0", ((6, "a"),)), ("y0", ((6, "a"),)), ("yb", ((4, "v"),))), 1: (("y1", ((5, "a"), (5, "a"), (6, "v"))),),
           2: (("y2", ((4, "a"),)),) * 4}
 H = C // 2
 FIN = ((("a", 0, H),), (("v", 0, 64), ("a", 64, H)))
 LAG_SAME, LAG_CROSS = 60.0, 140.0
 MV = 1024
-OPT = dict(zo=1, sq=1, kq=1, late=2500, pe=0.62, af=90, tries=1500, moves=100000, seed=5)
+NF = 10
+OPT = dict(mu=0.06, mu2=0.03, cuts=(0, 512, 2048, W), au1=12000, au2=18000, ntd=9000, dma=1400, rem=1900, zo=(1, 2), sq=(1, 2),
+           kq=(1, 2), qa=(1, 2), selg=4, fb=0, pe=0.62, af=90, tries=3000, moves=20000, seed=2)
+OPT.update(ga=1.56, sc=3.8)
+CASES = ((dict(rem=2600, dma=1900, au1=14500, au2=21500, ntd=11000), 60.0, 180.0),
+         (dict(ga=2.0, sc=5.5, pe=0.7), 80.0, 140.0),
+         (dict(ga=1.15, sc=2.0, rem=1500, au1=11000, au2=16500, af=70), 40.0, 110.0))
 PLAN = {}
 
 
@@ -108,9 +115,9 @@ def _ops(g, T, topo, core):
     def vcost(out, ins, two=False):
         n = out[2]
         if out[4] == "ind":
-            return 50 + 3.8 * n
+            return 50 + OPT["sc"] * n
         if ins and ins[0][4] == "ind":
-            return 50 + 1.56 * n
+            return 50 + OPT["ga"] * n
         f = 2.0 if two else (0.5 if all(x[3] in ("bfloat16", "uint16") for x in [out] + ins) else 1.0)
         return 20 + max(64, f * n)
 
@@ -145,7 +152,7 @@ def _ops(g, T, topo, core):
 
     def act(out, i, fn=AF.Identity, bias=0.0, scale=1.0, acc=None):
         rd, wr = split(out, [i, bias, scale])
-        c = 65 + 1.56 * out[2] if i[4] == "ind" else OPT["af"] + max(64, out[2])
+        c = 65 + OPT["ga"] * out[2] if i[4] == "ind" else OPT["af"] + max(64, out[2])
         if acc is None:
             add("a", lambda: S.activation(out[0], i[0], fn, bias=ap(bias), scale=ap(scale)), rd, wr, c)
         else:
@@ -188,7 +195,14 @@ def _ops(g, T, topo, core):
 
     def dma(q, out, i, rd, wr, sem, nbytes, extra=0.0):
         e = g.sync if q == "s" else g.scalar
-        add(q, lambda: e.dma_start(out, i), rd, wr, 60.0, 1700 + extra + nbytes / 300.0, sem, 16)
+        add(q, lambda: e.dma_start(out, i), rd, wr, 60.0, OPT["dma"] + extra + nbytes / 300.0, sem, 16)
+
+    def dmas(q, pairs, rd, wr, sem, lat):
+        def emit():
+            for out, i in pairs[:-1]:
+                g.sync.dma_start(out, i).then_inc(T.sem[sem], 16)
+            return g.sync.dma_start(*pairs[-1])
+        add(q, emit, rd, wr, 60.0 * len(pairs), lat, sem, 16 * len(pairs))
 
     def remote(dst_rank, out, i, sem, nbytes, extra=0.0):
         d = T.cores[dst_rank % N]
@@ -196,7 +210,7 @@ def _ops(g, T, topo, core):
         m = topo.mask(core, d)
         k = len(topo.engines(core, d))
         add("g", lambda: g.remote_dma(out[0], i[0], T.sem[sem], T.sem.sent, pid, rid, m), i[1], out[1], 400.0,
-            2400 + extra + nbytes / 250.0, sem, k)
+            OPT["rem"] + extra + nbytes / 250.0, sem, k)
 
     def diag(out, src):
         scan(out, X("mk", 0, src[2]), src, 0.0, A.add, A.min)
@@ -220,26 +234,29 @@ def _ops(g, T, topo, core):
 
     dma("s", X("li", 0, 12)[0], T.lens[:], [], X("li", 0, 12)[1], "dl", 6144)
     dma("s", X("sp")[0], T.spots[:], [], X("sp")[1], "dsp", 98304)
-    dma("a", X("au0", 0, W // 2)[0], T.aud[:, 0:W // 2], [], X("au0", 0, W // 2)[1], "da0", 524288, 500)
+    cuts = OPT["cuts"]
+    for k in range(3):
+        a, b = cuts[k], cuts[k + 1]
+        dma("a", X("au0", a, b)[0], T.aud[:, a:b], [], X("au0", a, b)[1], "da%d" % k, 256 * b, (300, 500, 550)[k])
     dma("s", X("gu")[0], T.gua[:], [], X("gu")[1], "dg", 98304, 300)
-    dma("a", X("au0", W // 2, W)[0], T.aud[:, W // 2:W], [], X("au0", W // 2, W)[1], "da1", 524288, 2300)
-    remote(r - 1, X("au1", 0, W // 2), X("au0", 0, W // 2), "ra1", 1 << 19, OPT["late"] + 2300)
-    remote(r - 1, X("au1", W // 2, W), X("au0", W // 2, W), "rb1", 1 << 19, OPT["late"])
-    remote(r - 2, X("au2", 0, W), X("au0", 0, W), "ra2", 1 << 20, OPT["late"] + 5000)
+    for k in range(3):
+        a, b = cuts[k], cuts[k + 1]
+        remote(r - 1, X("au1", a, b), X("au0", a, b), "ra%d" % k, 0, OPT["au1"] - 6100 - OPT["rem"])
+    remote(r - 2, X("au2", 0, W), X("au0", 0, W), "rb", 0, OPT["au2"] - 6500 - OPT["rem"])
 
     iota(X("pi", 0, 1), [[0, 1]], 0, 1)
     iota(X("i143"), [[1, 144]], 0, 0)
     iota(X("j16"), [[16, 8], [0, 16]], 0, 0)
     iota(X("md", 0, 16), [[1, 16]], 0, 0)
-    iota(X("md", 16, 384), [[0, 23], [1, 16]], 0, 0)
     ms(X("pf", 0, POOL["pc"][1]), 0.0)
-    ms(X("ph", 0, POOL["big"][1]), 0.0)
+    ms(X("ph", 0, POOL["cx"][1] + 16), 0.0)
     cp(col("pc"), X("pi", 0, 1))
     ts(X("pj", 0, 1), X("pi", 0, 1), 15, A.bitwise_and)
     cp(col("sc"), X("pj", 0, 1))
     tt(col("g16"), col("pc"), col("sc"), A.subtract)
     ts(X("mk", 0, 16), X("md", 0, 16), col("sc"), A.is_equal, 16777216.0, A.mult)
-    ts(X("mk", 16, 384), X("md", 16, 384), col("sc"), A.is_equal, 16777216.0, A.mult)
+    for k, (a, b) in enumerate(((16, 32), (32, 64), (64, 128), (128, 256), (256, 384))):
+        dma("s", X("mk", a, b)[0], X("mk", 0, b - a)[0], X("mk", 0, b - a)[1], X("mk", a, b)[1], "dm%d" % k, 0, 500)
     ms(X("mm", 0, MV), 1.0)
     for a in range(MV, L, MV):
         b = min(a + MV, L)
@@ -266,8 +283,15 @@ def _ops(g, T, topo, core):
     iota(X("md8"), [[0, 12], [8192, 16]], 0, 0)
     iota(X("m512"), [[0, 12], [1024, 16]], 0, 0)
     fill(X("ones"), 1)
-    for s in range(16):
-        ts(X("selt", 128 * s, 128 * s + 128), X("hp"), col("mk", s), A.mult, 2.0 / 16777216.0, A.mult)
+    if OPT["selg"]:
+        fill(X("on"), 1)
+    for h in range(4):
+        if h < OPT["selg"]:
+            asel(X("selt", 512 * h, 512 * h + 512), X("on"), [[1, 4], [16, 8], [0, 16]], A.is_equal, 4 * h, -1)
+        else:
+            for s in range(4 * h, 4 * h + 4):
+                ts(X("selt", 128 * s, 128 * s + 128), X("hp"), col("mk", s), A.mult, 2.0 / 16777216.0, A.mult)
+    act(col("s8z"), col("sc"), scale=-8192.0, bias=-float(W))
     iota(X("jd"), [[16, C]], 0, 1)
     iota(X("exi"), [[1, 24]], 0, 0)
     ed = t12("ed")
@@ -294,7 +318,7 @@ def _ops(g, T, topo, core):
     scan(X("bl", 1, 13), ln, t12("z24"), 0.0, A.add, A.add)
     mm([(col("ps6"), [(X("trl"), col("bl", 12))])])
     ts(X("bd", 0, 13), X("bl", 0, 13), col("ps6"), A.add)
-    ts(t12("t1"), ln, 1.0, A.is_lt, BIG, A.mult)
+    act(t12("t1"), ln, AF.Relu, scale=-BIG, bias=BIG)
     tt(t12("t2"), t12("t1"), st, A.add)
     tt(t12("t5"), t12("t2"), ev("dum"), A.min)
     cp(t12("sto"), t12("t5"))
@@ -318,31 +342,31 @@ def _ops(g, T, topo, core):
     ts(t12("t4"), ln, 0.5, A.mult, col("s8k"), A.subtract)
     tt(t12("ks"), t12("t1"), t12("t4"), A.add)
     act(X("stc", 0, 12), st, bias=float(Y2 - 1))
-    act(X("t4", 12, 24), ev("c24"), scale=KEY, bias=7.0)
-    tt(ev("sv"), X("t4", 12, 24), st, A.add)
-    act(X("t2", 12, 24), od("c24"), scale=KEY, bias=float(XB - 1))
-    tt(od("sv"), X("t2", 12, 24), t12("e3"), A.add)
+    mm([(X("ps3", 16, 28), [(X("ikey"), ev("c24")), (X("idh"), st)]),
+        (X("ps3", 28, 40), [(X("ikey"), od("c24")), (X("idh"), t12("e3"))]),
+        (X("ps3", 40, 52), [(X("ikey"), ln), (X("idh"), ed)])])
+    act(ev("sv"), X("ps3", 16, 28), bias=7.0)
+    act(od("sv"), X("ps3", 28, 40), bias=float(XB - 1))
     act(t12("sv0"), st, bias=7.0)
     act(ev("ts"), ln)
     act(X("tp", 0, 25, 2), X("bd", 0, 13), scale=-1.0, bias=float(L))
     act(od("tp"), X("bd", 1, 13), scale=-1.0, bias=float(L))
-    ts(t12("t3"), ln, 8192.0, A.mult)
-    tt(t12("t3"), t12("t3"), ed, A.add)
     act(X("t3", 12, 24), X("bd", 1, 13), bias=float(Y1 - 1))
-    tt(t12("t3"), t12("t3"), X("t3", 12, 24), A.min)
+    tt(t12("t3"), X("ps3", 40, 52), X("t3", 12, 24), A.min)
     cp(t12("pe"), t12("t3"))
     tag[0] = 1
-    cp(X("ta"), X("sp"))
-    act(X("hl", 0, C), X("ta"))
-    act(X("tb"), X("hl", 0, C), scale=-1.0)
-    mm([(X("ps7", 0, C), [(X("idh"), X("ta")), (X("idh"), X("tb"))])])
-    act(X("hl", C, 2 * C), X("ps7", 0, C))
-    for s in range(16):
-        pb, o = "ps%d" % (6 + (s // 2) % 2), C * (s % 2)
-        if s % 2 == 0:
-            mm([(X(pb, C * u, C * u + C), [(X("selt", 128 * (s + u), 128 * (s + u) + 128), X("hl", 0, C)),
-                                           (X("selt", 128 * (s + u), 128 * (s + u) + 128), X("hl", C, 2 * C))]) for u in range(2)])
-        act(X("nt", 8 + s, 8 + L, 16), X(pb, o, o + C))
+    iota(X("za", 0, 12), [[1, 6], [96, 2]], 0, 0)
+    iota(X("za", 12, 24), [[16, 2], [32, 6]], 0, 0)
+    act(col("s6"), col("sc"), scale=6.0)
+    ts(t12("zu"), X("za", 0, 12), col("s6"), A.add)
+    ts(t12("zw"), X("za", 12, 24), col("sc"), A.add)
+    cp(X("z2"), X("sp"))
+    act(X("ta"), IND(X("z2"), t12("zu")))
+    tr(X("tb"), X("ta"))
+    act(X("z2"), IND(X("tb"), t12("zw")))
+    dmas("s", [(T.nd[u:8:2, :], X("z2", H * u, H * u + H)[0]) for u in range(2)], X("z2")[1], [("nd", 0, L)], "dz", OPT["dma"] + 600)
+    dmas("s", [(T.nt[i:128:16, 8:8 + L], T.nd[:]) for i in range(16)], [("nd", 0, L)] + X("au1", 0, W)[1], X("nt", 8, 8 + L)[1],
+         "dt", OPT["ntd"])
 
     def wide(t):
         xx, fl, au = "xx%d" % (t % 2), "fl%d" % (t % 2), "au%d" % t
@@ -381,27 +405,29 @@ def _ops(g, T, topo, core):
 
     def second():
         tt(X("pa", 0, 12), ev("ts"), X("stc", 0, 12), A.add)
-        mm([(X("ps6", 0, 12), [(X("ikey"), ev("ts")), (X("idh"), ed)])])
-        tt(t12("pb"), X("pa", 0, 12), X("ps6", 0, 12), A.min)
+        mm([(X("ps7", 0, 12), [(X("ikey"), ev("ts")), (X("idh"), ed)])])
+        tt(t12("pb"), X("pa", 0, 12), X("ps7", 0, 12), A.min)
         cp(t12("pd"), t12("pb"))
         tt(t12("ea"), t12("en0"), od("ts"), A.mult)
         ts(t12("eau"), t12("ea"), float(W), A.add)
         act(t12("xq"), ev("ts"))
 
     def second_b():
-        act(X("th2"), IND(X("y2"), t12("pd")), scale=-1.0, bias=255.0)
-        tt(X("u1"), IND(X("au2"), t12("eau")), X("th2"), A.subtract)
-        act(X("fa"), X("u1"), AF.Sign, bias=-0.5, scale=-1.0)
-        act(X("th2"), X("u1"), scale=-1.0)
-        count(X("ps1", 256, 268), "fa", 0, C)
-        ts(t12("f2"), X("ps1", 256, 268), 5.0, A.is_gt)
+        act(X("th2"), IND(X("y2"), t12("pd")), bias=-255.0)
+        act(X("u1"), IND(X("au2"), t12("eau")))
+        mm([(X("ps7", 0, C), [(X("idh"), X("u1")), (X("idh"), X("th2"))])])
+        act(X("fa"), X("ps7", 0, C), AF.Sign, bias=-0.5, scale=-1.0)
+        act(X("th2"), X("ps7", 0, C), scale=-1.0)
+        count(X("ps7", 256, 268), "fa", 0, C)
+        ts(t12("f2"), X("ps7", 256, 268), 5.0, A.is_gt)
         act(t12("nf2"), t12("f2"), scale=-1.0, bias=1.0)
         tt(t12("ff"), t12("xq"), ev("cap2"), A.is_lt)
         tt(od("cap2"), t12("ff"), t12("f2"), A.add)
 
     def visit(t):
         au, mi, cap = "au%d" % t, "mi%d" % t, "cap%d" % t
-        rel, inn = TW * t, TW * t + TI
+        rel = TW * (1, 0, 2)[t]
+        inn = rel + TI
         m, y, s = ev("kept"), od("kept"), od("ss")
         if t == 0:
             tt(s, ln, ev(cap), A.is_lt)
@@ -421,7 +447,7 @@ def _ops(g, T, topo, core):
         mm([(col("ps5"), [(X("trl"), c24)])])
         mm([(col("ps4", 0), [(X("ntrg"), c24)]), (col("ps4", 1), [(X("blk"), c24)])])
         mm([(col("ps3"), [(X("blk"), c24)])], stop=False)
-        if OPT["zo"]:
+        if t in OPT["zo"]:
             act(X("zo"), X("ro"), AF.Relu, scale=-BIG, bias=BIG)
         else:
             ts(X("zo"), X("ro"), 1.0, A.is_lt, BIG, A.mult)
@@ -438,12 +464,15 @@ def _ops(g, T, topo, core):
         w0 = NREL * (2 - t)
         tt(IND(X("wr", w0, w0 + 2 * L + 2 * C + 16), X("ou", 0, k)), X("ee", 0, 16 * k), X("mk", 0, 16 * k), A.mult)
         mm([(X("ps5", 0, NREL), [(X("blk"), X("wr", w0, w0 + NREL))])])
-        if OPT["kq"]:
-            mm([(X("ps4", 16, 41), [(X("idh"), X("tp", 0, 25)), (X("idh"), X("cr", 0, 25))])])
-            ts(X("kq", 0, 25), X("ps4", 16, 41), col("ps4", 0), A.add)
+        mm([(X("ps4", 16, 41), [(X("idh"), X("tp", 0, 25)), (X("idh"), X("cr", 0, 25))])])
+        if t in OPT["kq"]:
+            act(col("rr", 0), col("ps4", 0))
+            act(X("kq", 0, 25), X("ps4", 16, 41), bias=col("rr", 0))
         else:
-            tt(X("kq", 0, 25), X("tp", 0, 25), X("cr", 0, 25), A.add)
-            ts(X("kq", 0, 25), X("kq", 0, 25), col("ps4", 0), A.add)
+            ts(X("kq", 0, 25), X("ps4", 16, 41), col("ps4", 0), A.add)
+        if t in OPT["qa"]:
+            act(col("rr", 1), col("ps4", 1), scale=-0.5, bias=TI / 2.0)
+            act(col("rr", 2), col("ps4", 1), scale=0.5, bias=TI / 2.0)
         mm([(col("ps4", 2), [(X("nblk"), c24)])], stop=False)
         scan(X("v1"), X("ps5", 0, NREL), X("ones"), 0.0, A.max, A.add)
         diag(X("v2"), X("v1"))
@@ -467,19 +496,28 @@ def _ops(g, T, topo, core):
         ts(X(mo, 0, 2), X("ps3", 0, 2), 0.0, A.max, 128.0, A.min)
         remote(r + 1, X(mi, 0, 2), X(mo, 0, 2), "rm%d" % t, 1024)
         mm([(col("ps4", 2), [(X("trlh"), s24), (X("trlh"), s24)])], start=False)
-        if OPT["sq"]:
+        if t in OPT["sq"]:
             act(col("rr", 3), col("ps4", 2))
             act(X("sq", 0, 25), X("cs", 0, 25), bias=col("rr", 3))
         else:
             ts(X("sq", 0, 25), X("cs", 0, 25), col("ps4", 2), A.add)
         tt(X("sk", 0, 25), X("sq", 0, 25), X("kq", 0, 25), A.min)
-        ts(t12("isin"), od("sq"), 0.0, A.is_ge, float(TI), A.mult)
-        ts(t12("q0"), t12("isin"), col("ps4", 1), A.max)
+        if t in OPT["qa"]:
+            act(t12("isin"), od("sq"), AF.Sign, bias=0.5)
+            act(t12("q0"), t12("isin"), scale=col("rr", 1), bias=col("rr", 2))
+        else:
+            ts(t12("isin"), od("sq"), 0.0, A.is_ge, float(TI), A.mult)
+            ts(t12("q0"), t12("isin"), col("ps4", 1), A.max)
         tt(t12("q0"), t12("q0"), od("sq"), A.add)
-        if t > 0:
+        if t == 1:
+            tt(t12("xo"), y, t12("g0"), A.mult)
+        if t == 2:
             mm([(X("ps4", 48, 60), [(X("idh"), y), (X("idh"), t12("e3"))])])
             cp(t12("xu"), X("ps4", 48, 60))
-        ts(t12("q1"), t12("isin"), col(mi, 1), A.mult, 2.0 / TI, A.mult)
+        if t in OPT["qa"]:
+            ts(t12("q1"), t12("isin"), col(mi, 1), A.mult, col(mi, 1), A.add)
+        else:
+            ts(t12("q1"), t12("isin"), col(mi, 1), A.mult, 2.0 / TI, A.mult)
         tt(t12("q1"), t12("q1"), t12("q0"), A.add)
         cp(t12("gi"), t12("q1"))
         ts(X("mx", 0, 25), X("sk", 0, 25), col(mi), A.min)
@@ -491,9 +529,15 @@ def _ops(g, T, topo, core):
             diag(X("gd"), X("gn"))
             ts(t12("eb"), D16("gd", C), col("s8k"), A.subtract)
         if t == 0:
-            ts(t12("en0"), D16("gd", C), col("s8k"), A.subtract, float(W), A.subtract)
+            act(t12("en0"), D16("gd", C), bias=col("s8z"))
+            act(t12("g0"), t12("q1"), bias=float(TW))
             act(X("nt", XB, ZN, 3), gw)
             second()
+        elif t == 1:
+            tt(t12("xo"), t12("xo"), t12("q1"), A.max)
+            cp(t12("xu"), t12("xo"))
+            act(X("nt", XB + 1, ZN, 3), gw)
+            act(X("nt", XB, ZN, 3), IND(X("tab", 0, 2 * TW), t12("xu")))
         else:
             act(X("gg"), gw)
             cp(IND(X("nt", XB, ZN), t12("xu")), X("gg"))
@@ -506,7 +550,11 @@ def _ops(g, T, topo, core):
         mm([(X("ps7", s, 2 * C, 32), [(X("selt", 128 * s, 128 * s + 128), q) for q in (t12("q192"), t12("mh"))])
             for s in range(16)], start=False, stop=False)
         mm([(X("ps7", 0, 16), [(X("hp"), X("zb", 0, 16))])], start=False)
-        act(X("vrep"), X("ps7", 0, 2 * C), bias=KEY + 8.0 + L)
+        if OPT["fb"]:
+            act(X("vrep"), X("ps7", 0, 2 * C), scale=-1.0, bias=-(KEY + 8.0 + L))
+            mm([(X("ps6", 0, 2 * C), [(X("idh"), X("vrep"))])], stop=False)
+        else:
+            act(X("vrep"), X("ps7", 0, 2 * C), bias=KEY + 8.0 + L)
         iota(X("ta", 0, H), [[1, 16], [32, 3], [128, 2]], 0, 0)
         iota(X("tb", 0, H), [[0, 16], [0, 3], [-224, 2]], 112, 0)
         ts(X("pj", 1, 2), X("pi", 0, 1), 4, A.logical_shift_right, 1, A.bitwise_and)
@@ -516,23 +564,33 @@ def _ops(g, T, topo, core):
         diag(X("ta", 0, H), X("ps7", 0, H))
         ts(X("tg", 0, 6), D16("ta", H), col("s8k"), A.subtract)
         act(col("sm15"), col("g16"), scale=-1.0, bias=-float(L))
-        mm([(X("ps0", 0, C), [(X("idh"), X("jd"))])], stop=False)
 
     def final():
-        ts(X("bbi"), X("tp", 0, 24), -1.0, A.mult, float(L), A.add)
+        mm([(X("ps0", 0, C), [(X("idh"), X("jd"))])], stop=False)
+        act(X("lk"), X("kq", 0, 24), scale=-1.0, bias=float(L))
+        tt(X("bbi"), X("mx", 0, 24), X("lk"), A.add)
         ts(X("bbi"), X("bbi"), 15, A.bitwise_and)
         cp(X("b15"), X("bbi"))
         spread("ps7", 2 * C, 16, [X("b15")])
         act(X("bb"), X("tp", 0, 24), scale=-1.0, bias=float(L))
         tt(X("b16"), X("bb"), X("b15"), A.subtract)
-        spread("ps6", 2 * C, 16, [X("b16")])
+        if OPT["fb"]:
+            mm([(X("ps6", s, 2 * C, 16), [(X("selt", 128 * s, 128 * s + 128), q) for q in (X("b15"), X("b16"))])
+                for s in range(16)], start=False, stop=False)
+            mm([(X("ps6", 0, 16), [(X("hp"), X("zb", 0, 16))])], start=False)
+        else:
+            spread("ps6", 2 * C, 16, [X("b16")])
         act(X("zo"), X("ts"), AF.Relu, scale=-BIG, bias=BIG)
         tt(X("oo"), X("bb"), X("zo"), A.add)
         tt(X("oo"), X("oo"), X("dum"), A.min)
         cp(X("ou"), X("oo"))
-        tt(X("eb1"), X("vrep"), X("ps7", 0, 2 * C), A.subtract)
+        if not OPT["fb"]:
+            tt(X("eb1"), X("vrep"), X("ps7", 0, 2 * C), A.subtract)
         act(X("msk"), X("ps7", 0, 2 * C), AF.Sign, scale=-1.0, bias=col("sh"))
-        tt(X("eb2"), X("eb1"), X("ps6", 0, 2 * C), A.subtract)
+        if OPT["fb"]:
+            act(X("eb2"), X("ps6", 0, 2 * C), scale=-1.0)
+        else:
+            tt(X("eb2"), X("eb1"), X("ps6", 0, 2 * C), A.subtract)
         tt(IND(X("xx1"), X("ou")), X("eb2"), X("msk"), A.mult)
         lq = t12("lq")
         tt(lq, ev("ts"), od("ts"), A.add)
@@ -558,7 +616,7 @@ def _ops(g, T, topo, core):
                 gat(e, X("xx0", a + 16 * u, a + 16 * w), IND(X("nt"), X("fo", H * h + u, H * h + w)))
             dma("s", T.yo[:, H * h:H * h + H], T.xx0[0:128:16, a:a + 16 * H], X("xx0", a, a + 16 * H)[1], [], "do%d" % h, 49152, 300)
 
-    for k, (f, t) in enumerate(((wide, 0), (wide, 1), (visit, 0), (wide, 2), (second_b, None), (visit, 1), (final_static, None),
+    for k, (f, t) in enumerate(((wide, 0), (wide, 1), (final_static, None), (visit, 0), (wide, 2), (second_b, None), (visit, 1),
                                 (visit, 2), (final, None))):
         tag[0] = 2 + k
         if t is None:
@@ -598,20 +656,34 @@ def _place(ops, edges, order, rel):
         for j, lag in edges[i]:
             t = max(t, fin[j] + lag)
         lst = busy.setdefault(ops[i][0], [(1e18, 1e18)])
-        k = 0
-        for k, (a, b) in enumerate(lst):
-            if t + c <= a:
-                break
-            if b > t:
-                t = b
+        k, hi = 0, len(lst) - 1
+        while k < hi:
+            m = (k + hi) >> 1
+            if lst[m][1] > t:
+                hi = m
+            else:
+                k = m + 1
+        while t + c > lst[k][0]:
+            t = lst[k][1]
+            k += 1
         lst.insert(k, (t, t + c))
         fin[i] = t + c
     return fin
 
 
-def _anneal(ops, fw, bw, start, tries, seed, hot=250.0, cold=10.0, reach=8):
+def _random(seed):
+    st = [seed]
+
+    def rnd():
+        st[0] = (st[0] * 1103515245 + 12345) % 2147483648
+        return st[0] / 2147483648.0
+    return rnd
+
+
+def _anneal(ops, fw, bw, cases, start, tries, rnd, marks, hot=50.0, cold=4.0, reach=8):
     n = len(ops)
-    cost, tail = [o[4] for o in ops], [o[5] for o in ops]
+    after = [[j for j, _ in b] for b in bw]
+    ends = [i for i in range(n) if not bw[i]]
     seqs = {}
     for i in sorted(range(n), key=lambda k: (start[k], k)):
         seqs.setdefault(ops[i][0], []).append(i)
@@ -624,18 +696,8 @@ def _anneal(ops, fw, bw, start, tries, seed, hot=250.0, cold=10.0, reach=8):
                 prev[b], nxt[a] = a, b
                 left[b] += 1
         todo = [i for i in range(n) if left[i] == 0]
-        fin, why, done = [0.0] * n, [-1] * n, 0
-        while todo:
-            i = todo.pop()
-            done += 1
-            t, w = 0.0, -1
-            for j, lag in fw[i]:
-                if fin[j] + lag > t:
-                    t, w = fin[j] + lag, j
-            if prev[i] >= 0 and fin[prev[i]] >= t:
-                t, w = fin[prev[i]], -2 - prev[i]
-            fin[i], why[i] = t + cost[i], w
-            for j, _ in bw[i]:
+        for i in todo:
+            for j in after[i]:
                 left[j] -= 1
                 if left[j] == 0:
                     todo.append(j)
@@ -644,37 +706,45 @@ def _anneal(ops, fw, bw, start, tries, seed, hot=250.0, cold=10.0, reach=8):
                 left[j] -= 1
                 if left[j] == 0:
                     todo.append(j)
-        if done < n:
+        if len(todo) < n:
             return None
-        last = max(range(n), key=lambda k: fin[k] + tail[k])
-        return fin[last] + tail[last], fin, why, last
-
-    st = [seed]
-
-    def rnd():
-        st[0] = (st[0] * 1103515245 + 12345) % 2147483648
-        return st[0] / 2147483648.0
+        res, total = [], 0.0
+        for cost, edges, tail, weight in cases:
+            fin, why = [0.0] * n, [-1] * n
+            for i in todo:
+                t, w = 0.0, -1
+                for j, lag in edges[i]:
+                    if fin[j] + lag > t:
+                        t, w = fin[j] + lag, j
+                if prev[i] >= 0 and fin[prev[i]] >= t:
+                    t, w = fin[prev[i]], -2 - prev[i]
+                fin[i], why[i] = t + cost[i], w
+            span, last = max((fin[i] + tail[i], i) for i in ends)
+            total += weight * span
+            res.append((fin, why, last, span))
+        return total + OPT["mu2"] * sum(res[0][0][i] for i in marks), res, total
 
     best = cur = times()
-    links = None
     for it in range(tries):
-        if links is None:
-            links, i = [], cur[3]
-            while i >= 0:
-                w = cur[2][i]
-                if w <= -2:
-                    w = -2 - w
-                    if w >= 8:
-                        links.append((w, i))
-                i = w
-            if not links:
-                break
+        _, why, i, _ = cur[1][int(rnd() * len(cases))]
+        links = []
+        if rnd() < 0.3:
+            i = marks[int(rnd() * len(marks))]
+        while i >= 0:
+            w = why[i]
+            if w <= -2:
+                w = -2 - w
+                if w >= NF:
+                    links.append((w, i))
+            i = w
+        if not links:
+            continue
         u, v = links[int(rnd() * len(links))]
         s = seqs[ops[u][0]]
         a, k = s.index(u), int(rnd() ** 2 * reach)
         if rnd() < 0.5:
             lo = max(a - k, 0)
-            while s[lo] < 8:
+            while s[lo] < NF:
                 lo += 1
             old = s[lo:a + 2]
             s[lo:a + 2] = [v] + old[:-1]
@@ -684,15 +754,15 @@ def _anneal(ops, fw, bw, start, tries, seed, hot=250.0, cold=10.0, reach=8):
             s[a:a + 2 + k] = old[1:] + [u]
         got = times()
         if got is not None and (got[0] <= cur[0] or rnd() < math.exp((cur[0] - got[0]) / (hot * (cold / hot) ** (it / tries)))):
-            cur, links = got, None
-            if got[0] < best[0]:
+            cur = got
+            if got[2] < best[2]:
                 best = got
         else:
             s[lo:lo + len(old)] = old
-    return best[0], [best[1][i] - cost[i] for i in range(n)]
+    return [x[3] for x in best[1]], [best[1][0][0][i] - cases[0][0][i] for i in range(n)]
 
 
-def _schedule(ops, tries, seed):
+def _schedule(ops, tries, seed, others=()):
     deps = _deps(ops)
     n = len(ops)
     fw, bw = [[] for _ in ops], [[] for _ in ops]
@@ -711,46 +781,57 @@ def _schedule(ops, tries, seed):
             lag = (LAG_SAME if raw else 0.0) if (ops[j][0] == ops[i][0] and ops[j][6] is None) else ops[j][5] + LAG_CROSS
             fw[i].append((j, lag))
             bw[j].append((i, lag))
-    zero, tail = [0.0] * n, [o[5] for o in ops]
-    best, cur, warm = None, None, max(1, tries // 10)
+    cost, tail = [o[4] for o in ops], [o[5] for o in ops]
+    rnd = _random(seed)
+    caps = [POOL["cap%d" % t][:2] for t in range(3)]
+    marks = [i for i in range(NF, n) if (ops[i][0] == "g" and ops[i][6]) or any(w[:2] in caps for w in ops[i][3])]
+
+    def forward(rank):
+        for i in range(n - 1, -1, -1):
+            for j, _ in fw[i]:
+                if rank[j] <= rank[i]:
+                    rank[j] = rank[i] + 1e-3
+        fin = _place(ops, fw, list(range(NF)) + sorted(range(NF, n), key=lambda k: (-rank[k], k)), [0.0] * n)
+        span = max(f + t for f, t in zip(fin, tail))
+        return span + OPT["mu"] * sum(fin[i] for i in marks), [f - c for f, c in zip(fin, cost)], span
+
+    def backward(st):
+        return _place(ops, bw, sorted(range(n), key=lambda k: (-st[k] - cost[k] - tail[k], -k)), tail)
+
+    rank = [0.0] * n
+    for i in range(n - 1, -1, -1):
+        rank[i] = cost[i] + max([tail[i]] + [rank[j] + lag for j, lag in bw[i]])
+    cur = forward(rank)
+    for _ in range(4):
+        cur = min(cur, forward(backward(cur[1])))
+    best = cur
     for it in range(tries):
-        rank = [0.0] * n
-        if it < warm:
-            fac = []
-            for _ in range(12):
-                seed = (seed * 1103515245 + 12345) % 2147483648
-                fac.append(0.05 + 2.0 * (seed / 2147483648.0) ** 2)
-            for i in range(n - 1, -1, -1):
-                seed = (seed * 1103515245 + 12345) % 2147483648
-                rank[i] += ((ops[i][4] + 70) * (1.0 + 0.3 * seed / 2147483648.0) + ops[i][5]) * fac[ops[i][8]]
-                for j, _ in fw[i]:
-                    rank[j] = max(rank[j], rank[i] + 1e-3)
-        else:
-            rnd = []
-            for _ in range(6):
-                seed = (seed * 1103515245 + 12345) % 2147483648
-                rnd.append(seed / 2147483648.0)
-            mid, wid, sh, tg = rnd[0] * cur[0], 500 + 6000 * rnd[1], (rnd[2] - 0.5) * 8000, int(rnd[3] * 12)
-            rank = [-1e9] * n
-            for i in range(n - 1, -1, -1):
-                hit = abs(cur[1][i] - mid) < wid and (ops[i][8] == tg or (rnd[4] < 0.3 and (i * 7 + it) % 5 == 0))
-                rank[i] = max(rank[i], -cur[1][i] + (sh if hit else 0.0))
-                for j, _ in fw[i]:
-                    rank[j] = max(rank[j], rank[i] + 1e-3)
-        order = sorted(range(n), key=lambda k: (-rank[k], k))
-        for _ in range(4 if it < warm else 2):
-            fin = _place(ops, fw, list(range(8)) + [k for k in order if k >= 8], zero)
-            span = max(fin[i] + tail[i] for i in range(n))
-            got = (span, [fin[i] - ops[i][4] for i in range(n)])
-            if best is None or span < best[0]:
-                best = got
-            if it < warm:
-                cur = best
-            elif span < cur[0] + 400.0 * (1.0 - it / tries):
-                cur = got
-            back = _place(ops, bw, sorted(range(n), key=lambda k: (-fin[k] - tail[k], -k)), tail)
-            order = sorted(range(n), key=lambda k: (-back[k], k))
-    best = _anneal(ops, fw, bw, best[1], OPT["moves"], seed)
+        st = cur[1]
+        back = backward(st)
+        end = max(back)
+        a = rnd() * cur[2]
+        b = a + 2000 + 25000 * rnd() ** 2
+        w, amp = rnd(), 3000 * rnd() ** 2
+        far = 2000 + 20000 * rnd() ** 2
+        shift = [(rnd() - 0.5) * far * (rnd() < 0.4) for _ in range(12)]
+        rank = [-(w * (end - back[i]) + (1 - w) * st[i] + shift[ops[i][8]] + amp * rnd() * (cost[i] > 300)) if a <= st[i] < b
+                else -st[i] for i in range(n)]
+        for k in range(n):
+            for j, _ in fw[k]:
+                if rank[k] >= rank[j] and not (a <= st[j] < b and rnd() < 0.5):
+                    rank[k] = rank[j] - 1e-3
+        got = forward(rank)
+        if rnd() < 0.5:
+            got = min(got, forward(backward(got[1])))
+        if got[0] < cur[0] + 600.0 * (1 - it / tries) * rnd():
+            cur = got
+        best = min(best, got)
+    cases = [(cost, fw, tail, 1.0 / (1 + len(others)))]
+    for o, same, cross in others:
+        edges = [[(j, (same if deps[i][j] else 0.0) if (o[j][0] == o[i][0] and o[j][6] is None) else o[j][5] + cross)
+                  for j, _ in fw[i]] for i in range(n)]
+        cases.append(([x[4] for x in o], edges, [x[5] for x in o], sum(cost) / sum(x[4] for x in o) / (1 + len(others))))
+    best = _anneal(ops, fw, bw, cases, best[1], OPT["moves"], rnd, marks)
     order = sorted(range(n), key=lambda k: (best[1][k], k))
     need, waits, know, seen, pos, cnt = set(), {}, {}, {}, {}, {}
     for i in order:
@@ -778,12 +859,21 @@ def _schedule(ops, tries, seed):
     return dict(order=order, waits=waits, val=val, cnt=cnt, need=need, span=best[0], start=best[1])
 
 
+def _cases(g, T, topo, core):
+    out, keep = [], dict(OPT)
+    for change, same, cross in CASES:
+        OPT.update(change)
+        out.append((_ops(g, T, topo, core), same, cross))
+        OPT.update(keep)
+    return out
+
+
 def rank_program(g, core, T, topo):
     if T.rank_of(core) is None:
         return
     ops = _ops(g, T, topo, core)
     if "p" not in PLAN:
-        PLAN["p"] = _schedule(ops, OPT["tries"], OPT["seed"])
+        PLAN["p"] = _schedule(ops, OPT["tries"], OPT["seed"], _cases(g, T, topo, core))
     p = PLAN["p"]
     Q = dict(v=g.vector, a=g.scalar, p=g.tensor, g=g, s=g.sync)
     sent = 0

import math
from concourse.mybir import AluOpType as A, ActivationFunctionType as AF

W, L, C = 4096, 3072, 192
BIG = 16384.0
KEY = 8192.0
XB = 8 + L
ZN = XB + 3 * C
NULLC = ZN + 7
NREL = 320
TI = 512
TW = TI + NREL + 64
NTW = ZN + 8 + NREL
Y1 = Y2 = C

F_T = dict(bl=16, z24=24, cr=32, ts=24, cap0=24,
           pc=8, g16=8, sc=8, g15=8, s8k=8, s8z=8, s6=8, lk=24, za=24, z2=192, g0=16, e1=8, sm15=8, s192=8, skey=8, sh=8, i143=144, j16=128, blk=128,
           nblk=128, trl=128, ntrg=128, p15=128, idh=128, i11=128, i22=128, ikey=128, mk=384, md=16, md8=192,
           ones=320, ed=16, ln=16, bd=16, qf=16, mf=16, t1=24, t2=24, t3=24, t4=24, t5=16, dum=24, c24=24, ng=192,
           sg=192, stc=24, sv=24, e3=16, ks=16, kd=192, cap1=24, cap2=24, tp=32, kept=24, j11=128, kq=32, mx=32,
           pa=24, pb=16, th1=192, th2=192, u1=192, ff=16, f2=16, nf2=16, pre=24, uu=16, gv=16, xq=16, xp=16, ro=24,
           zo=24, oo=24, vv=24, ee=384, v1=320, v2=320, rr=8, sq=32, sk=32, isin=16, q0=16, q1=16, sv0=16,
           xo=16, gg=192, gn=192, gd=192, en0=16, ea=16, ms0=8, ms1=8, ms2=8, vrep=384, eb1=384, eb2=384, msk=384, jd=192,
           jadj=192, np0=128, np1=128, tt0=224, tt1=224, lq=16, lq2=16, tot=8, tq=8, ta=192, tb=192, bb=24)
H_T = dict(ss=24, cs=32, zb=192, cx=200, big=144, on=512, big2=144, hp=128, hn=128, trlh=128, eq=208, lt=208, m512=192, gz=192,
           hl=384, fd=192, h1=208, h2=208, fa=192, fs=192, b15=24, b16=24, q192=16, mh=16)
U_T = dict(so=192, zu=16, zw=16, mb=16, sto=16, stg=16, ex=24, pm=16, pe=16, pd=16, ou=24, rp=24, gi=16, xu=16, eb=16, eau=16, fo=192, tg=16)
I_T = dict(pi=8, pj=8, li=16, sp=192, gu=192, qi=16, exi=24, rpi=24, bbi=24, nn=192)


def _alloc(d):
    pos, at = {}, 0
    for k, n in d.items():
        pos[k] = (at, n)
        at += (n + 15) // 16 * 16
    return pos, at


POOL = {}
SCRATCH = {}
for _n, _d, _t in (("pf", F_T, "float32"), ("ph", H_T, "bfloat16"), ("pu", U_T, "uint16"), ("pi32", I_T, "int32")):
    _p, _w = _alloc(_d)
    SCRATCH[_n] = ("sbuf", [128, _w], _t)
    for _k, _v in _p.items():
        POOL[_k] = (_n, _v[0], _v[1])
for _t in range(3):
    SCRATCH["au%d" % _t] = ("sbuf", [128, W + 16], "bfloat16")
    SCRATCH["mi%d" % _t] = ("sbuf", [128, 4], "float32")
for _t in range(2):
    SCRATCH["xx%d" % _t] = ("sbuf", [128, L + 2 * C], "float32")
    SCRATCH["fl%d" % _t] = ("sbuf", [128, L], "bfloat16")
for _n, _t in (("y0", "float32"), ("yb", "bfloat16"), ("y1", "bfloat16"), ("y2", "float32")):
    SCRATCH[_n] = ("sbuf", [128, C + L], _t)
SCRATCH["fz"] = ("sbuf", [128, 8 + L // 2], "float32")
SCRATCH["mm"] = ("sbuf", [128, L + 2 * C], "bfloat16")
SCRATCH["selt"] = ("sbuf", [128, 2048], "bfloat16")
SCRATCH["nt"] = ("sbuf", [128, NTW], "float32")
SCRATCH["nd"] = ("dram", [8, L], "float32")
SCRATCH["tab"] = ("sbuf", [128, 3 * TW], "float32")
SCRATCH["wr"] = ("sbuf", [128, 2 * NREL + 2 * L + 2 * C + 16], "float32")
for _t in range(8):
    SCRATCH["ps%d" % _t] = ("psum", [128, 512], "float32")

SEMAPHORES = (["qv", "qa", "qp", "qg", "sent", "dl", "dsp", "dg", "da0", "da1", "da2", "do0", "do1", "dn", "dz", "dt", "dm0", "dm1", "dm2", "dm3", "dm4", "ra0", "ra1", "ra2", "rb"]
              + ["rr%d" % t for t in range(3)] + ["rm%d" % t for t in range(3)])

GCH = 512
DVE_G = {0: (0, 1, 2), 1: (0, 1), 2: ()}
PIECES = {0: (("y0", ((6, "a"),)), ("y0", ((6, "a"),)), ("yb", ((4, "v"),))), 1: (("y1", ((5, "a"), (5, "a"), (6, "v"))),),
          2: (("y2", ((4, "a"),)),) * 4}
H = C // 2
FIN = ((("a", 0, H),), (("v", 0, 64), ("a", 64, H)))
LAG_SAME, LAG_CROSS = 60.0, 140.0
MV = 1024
NF = 10
OPT = dict(mu=0.06, mu2=0.03, cuts=(0, 512, 2048, W), au1=12000, au2=18000, ntd=9000, dma=1400, rem=1900, zo=(1, 2), sq=(1, 2),
           kq=(1, 2), qa=(1, 2), selg=4, fb=0, pe=0.62, af=90, tries=3000, moves=20000, seed=2)
OPT.update(ga=1.56, sc=3.8)
CASES = ((dict(rem=2600, dma=1900, au1=14500, au2=21500, ntd=11000), 60.0, 180.0),
         (dict(ga=2.0, sc=5.5, pe=0.7), 80.0, 140.0),
         (dict(ga=1.15, sc=2.0, rem=1500, au1=11000, au2=16500, af=70), 40.0, 110.0))
PLAN = {}


def _ops(g, T, topo, core):
    ops, tag = [], [0]
    V, S, P = g.vector, g.scalar, g.tensor
    N = len(T.cores)
    r = T.rank_of(core)

    def X(name, a=0, b=None, st=1, p=128):
        if name in POOL:
            buf, o, n = POOL[name]
        else:
            buf, o, n = name, 0, SCRATCH[name][1][1]
        b = n if b is None else b
        ap = T[buf][0:p, o + a:o + b:st] if st != 1 else T[buf][0:p, o + a:o + b]
        return (ap, [(buf, o + a, o + b)], (b - a + st - 1) // st, SCRATCH[buf][2], SCRATCH[buf][0])

    def IND(win, off):
        return (win[0].indirect(off[0]), win[1] + off[1], 16 * off[2], win[3], "ind", win[1], off[1])

    def add(q, emit, rd, wr, cost, lat=0.0, sem=None, cnt=1):
        ops.append((q, emit, rd, wr, cost, lat, sem, cnt, tag[0]))

    def split(out, ins):
        rd = []
        for i in ins:
            if isinstance(i, tuple):
                rd += i[1]
        if out[4] == "ind":
            return rd + out[6], out[5]
        return rd, out[1]

    def vcost(out, ins, two=False):
        n = out[2]
        if out[4] == "ind":
            return 50 + OPT["sc"] * n
        if ins and ins[0][4] == "ind":
            return 50 + OPT["ga"] * n
        f = 2.0 if two else (0.5 if all(x[3] in ("bfloat16", "uint16") for x in [out] + ins) else 1.0)
        return 20 + max(64, f * n)

    def ap(x):
        return x[0] if isinstance(x, tuple) else x

    def cp(out, i):
        rd, wr = split(out, [i])
        add("v", lambda: V.tensor_copy(out[0], i[0]), rd, wr, vcost(out, [i]))

    def tt(out, a, b, op):
        rd, wr = split(out, [a, b])
        add("v", lambda: V.tensor_tensor(out[0], a[0], b[0], op), rd, wr,
            vcost(out, [a, b], a[4] != "psum" and b[4] != "psum"))

    def ts(out, a, s1, op0, s2=None, op1=None):
        rd, wr = split(out, [a, s1, s2])
        if op1 is None:
            add("v", lambda: V.tensor_scalar(out[0], a[0], ap(s1), None, op0), rd, wr, vcost(out, [a]))
        else:
            add("v", lambda: V.tensor_scalar(out[0], a[0], ap(s1), ap(s2), op0, op1), rd, wr, vcost(out, [a]))

    def scan(out, d0, d1, init, op0, op1):
        rd, wr = split(out, [d0, d1, init])
        add("v", lambda: V.tensor_tensor_scan(out[0], d0[0], d1[0], ap(init), op0, op1), rd, wr, vcost(out, [d0, d1]))

    def ms(out, c):
        add("v", lambda: V.memset(out[0], c), [], out[1], vcost(out, []))

    def tr(out, i):
        add("v", lambda: V.transpose(out[0], i[0]), i[1], out[1], vcost(out, [i]))

    def act(out, i, fn=AF.Identity, bias=0.0, scale=1.0, acc=None):
        rd, wr = split(out, [i, bias, scale])
        c = 65 + OPT["ga"] * out[2] if i[4] == "ind" else OPT["af"] + max(64, out[2])
        if acc is None:
            add("a", lambda: S.activation(out[0], i[0], fn, bias=ap(bias), scale=ap(scale)), rd, wr, c)
        else:
            add("a", lambda: S.activation(out[0], i[0], fn, bias=ap(bias), scale=ap(scale), accum_out=acc[0]), rd,
                wr + acc[1], c + 25)

    def gat(eng, out, i):
        if eng == "v":
            cp(out, i)
        else:
            act(out, i)

    def mm(groups, start=True, stop=True):
        rd, wr, c = [], [], 60.0
        for out, l in groups:
            wr += out[1]
            for a, b in l:
                rd += a[1] + b[1]
                c += OPT["pe"] * max(64, b[2]) * (4 if b[3] == "float32" else 1)

        def emit():
            ins = None
            for out, l in groups:
                for k, (a, b) in enumerate(l):
                    ins = P.matmul(out[0], a[0], b[0], start and k == 0, stop and k == len(l) - 1)
            return ins
        add("p", emit, rd, wr, c)

    def iota(out, pat, base, cm):
        if out[3] == "int32":
            add("g", lambda: g.iota(out[0], pat, base, cm), [], out[1], 130 + 2 * out[2])
        else:
            add("g", lambda: g.iota(out[0], pat, base, cm, allow_small_or_imprecise_dtypes=True), [], out[1], 130 + 2 * out[2])

    def fill(out, c):
        iota(out, [[0, out[2]]], c, 0)

    def asel(out, i, pat, op, base, cm):
        add("g", lambda: g.affine_select(out[0], i[0], pat, op, 0.0, base, cm), i[1], out[1], 170 + 2 * out[2])

    def dma(q, out, i, rd, wr, sem, nbytes, extra=0.0):
        e = g.sync if q == "s" else g.scalar
        add(q, lambda: e.dma_start(out, i), rd, wr, 60.0, OPT["dma"] + extra + nbytes / 300.0, sem, 16)

    def dmas(q, pairs, rd, wr, sem, lat):
        def emit():
            for out, i in pairs[:-1]:
                g.sync.dma_start(out, i).then_inc(T.sem[sem], 16)
            return g.sync.dma_start(*pairs[-1])
        add(q, emit, rd, wr, 60.0 * len(pairs), lat, sem, 16 * len(pairs))

    def remote(dst_rank, out, i, sem, nbytes, extra=0.0):
        d = T.cores[dst_rank % N]
        rid, pid, _ = topo.addr(d)
        m = topo.mask(core, d)
        k = len(topo.engines(core, d))
        add("g", lambda: g.remote_dma(out[0], i[0], T.sem[sem], T.sem.sent, pid, rid, m), i[1], out[1], 400.0,
            OPT["rem"] + extra + nbytes / 250.0, sem, k)

    def diag(out, src):
        scan(out, X("mk", 0, src[2]), src, 0.0, A.add, A.min)

    def D16(name, n):
        return X(name, 15, n, 16)

    def sel(s, name="big"):
        return X(name, 15 - s, 143 - s)

    def count(out, name, a, b, start=True):
        mm([(out, [(sel(s), X(name, a + s, b, 16)) for s in range(16)])], start=start)

    def spread(bank, width, step, parts):
        mm([(X(bank, s, width, step), [(X("selt", 128 * s, 128 * s + 128), q) for q in parts]) for s in range(16)])

    col = lambda n, k=0: X(n, k, k + 1)
    ev = lambda n: X(n, 0, 24, 2)
    od = lambda n: X(n, 1, 24, 2)
    t12 = lambda n: X(n, 0, 12)

    dma("s", X("li", 0, 12)[0], T.lens[:], [], X("li", 0, 12)[1], "dl", 6144)
    dma("s", X("sp")[0], T.spots[:], [], X("sp")[1], "dsp", 98304)
    cuts = OPT["cuts"]
    for k in range(3):
        a, b = cuts[k], cuts[k + 1]
        dma("a", X("au0", a, b)[0], T.aud[:, a:b], [], X("au0", a, b)[1], "da%d" % k, 256 * b, (300, 500, 550)[k])
    dma("s", X("gu")[0], T.gua[:], [], X("gu")[1], "dg", 98304, 300)
    for k in range(3):
        a, b = cuts[k], cuts[k + 1]
        remote(r - 1, X("au1", a, b), X("au0", a, b), "ra%d" % k, 0, OPT["au1"] - 6100 - OPT["rem"])
    remote(r - 2, X("au2", 0, W), X("au0", 0, W), "rb", 0, OPT["au2"] - 6500 - OPT["rem"])

    iota(X("pi", 0, 1), [[0, 1]], 0, 1)
    iota(X("i143"), [[1, 144]], 0, 0)
    iota(X("j16"), [[16, 8], [0, 16]], 0, 0)
    iota(X("md", 0, 16), [[1, 16]], 0, 0)
    ms(X("pf", 0, POOL["pc"][1]), 0.0)
    ms(X("ph", 0, POOL["cx"][1] + 16), 0.0)
    cp(col("pc"), X("pi", 0, 1))
    ts(X("pj", 0, 1), X("pi", 0, 1), 15, A.bitwise_and)
    cp(col("sc"), X("pj", 0, 1))
    tt(col("g16"), col("pc"), col("sc"), A.subtract)
    ts(X("mk", 0, 16), X("md", 0, 16), col("sc"), A.is_equal, 16777216.0, A.mult)
    for k, (a, b) in enumerate(((16, 32), (32, 64), (64, 128), (128, 256), (256, 384))):
        dma("s", X("mk", a, b)[0], X("mk", 0, b - a)[0], X("mk", 0, b - a)[1], X("mk", a, b)[1], "dm%d" % k, 0, 500)
    ms(X("mm", 0, MV), 1.0)
    for a in range(MV, L, MV):
        b = min(a + MV, L)
        act(X("mm", a, b), X("mm", 0, b - a))
    ts(X("big"), X("i143"), -15.0, A.add, col("g16"), A.is_equal)
    act(X("big2"), X("big"), scale=2.0)
    ts(X("blk"), X("j16"), col("g16"), A.is_equal)
    act(X("nblk"), X("blk"), scale=-1.0)
    act(X("hp"), X("blk"), scale=0.5)
    act(X("hn"), X("blk"), scale=-0.5)
    asel(X("trl"), X("blk"), [[1, 128]], A.is_gt, 0, -1)
    asel(X("ntrg"), X("nblk"), [[-1, 128]], A.is_ge, 0, 1)
    asel(X("trlh"), X("hp"), [[1, 128]], A.is_gt, 0, -1)
    asel(X("p15"), X("blk"), [[-16, 8], [0, 16]], A.is_equal, -15, 1)
    asel(X("idh"), X("blk"), [[-1, 128]], A.is_equal, 0, 1)
    for nm, c in (("i11", -11), ("j11", 11), ("i22", -22), ("ikey", int(KEY))):
        fill(X(nm), c)
        asel(X(nm), X(nm), [[-1, 128]], A.is_equal, 0, 1)
    act(col("s8k"), col("sc"), scale=8192.0)
    act(col("g15"), col("g16"), scale=-BIG, bias=BIG)
    act(col("sh"), col("sc"), bias=0.5)
    act(col("s192"), col("sc"), scale=192.0)
    act(col("skey"), col("sc"), scale=24.0)
    iota(X("md8"), [[0, 12], [8192, 16]], 0, 0)
    iota(X("m512"), [[0, 12], [1024, 16]], 0, 0)
    fill(X("ones"), 1)
    if OPT["selg"]:
        fill(X("on"), 1)
    for h in range(4):
        if h < OPT["selg"]:
            asel(X("selt", 512 * h, 512 * h + 512), X("on"), [[1, 4], [16, 8], [0, 16]], A.is_equal, 4 * h, -1)
        else:
            for s in range(4 * h, 4 * h + 4):
                ts(X("selt", 128 * s, 128 * s + 128), X("hp"), col("mk", s), A.mult, 2.0 / 16777216.0, A.mult)
    act(col("s8z"), col("sc"), scale=-8192.0, bias=-float(W))
    iota(X("jd"), [[16, C]], 0, 1)
    iota(X("exi"), [[1, 24]], 0, 0)
    ed = t12("ed")
    ts(ed, X("exi", 0, 12), 16.0, A.mult, col("sc"), A.add)
    cp(X("ex"), X("exi"))
    ts(X("c24"), X("exi"), col("skey"), A.add)
    ts(t12("pm"), ev("c24"), 0.5, A.mult)
    act(X("dum"), X("c24"), bias=float(L))
    act(t12("e3"), ed, scale=3.0)
    fill(X("au2", W, W + 16), 0)
    fill(X("au1", W, W + 16), 0)
    for t in range(3):
        fill(X("wr", NREL * t, NREL * t + NREL), 0)
        fill(X("tab", TW * t + TI + NREL, TW * t + TW), 0)
    fill(X("nt", 0, 8), 0)
    fill(X("nt", XB, ZN), 0)
    fill(X("nt", ZN, NTW), -1)
    for nm, a, b in (("np0", 0, 128), ("np1", 0, 128), ("fz", 0, 8)):
        fill(X(nm, a, b), 0)

    cp(X("so"), X("sp"))
    ln, st = t12("ln"), X("bd", 0, 12)
    cp(ln, X("li", 0, 12))
    scan(X("bl", 1, 13), ln, t12("z24"), 0.0, A.add, A.add)
    mm([(col("ps6"), [(X("trl"), col("bl", 12))])])
    ts(X("bd", 0, 13), X("bl", 0, 13), col("ps6"), A.add)
    act(t12("t1"), ln, AF.Relu, scale=-BIG, bias=BIG)
    tt(t12("t2"), t12("t1"), st, A.add)
    tt(t12("t5"), t12("t2"), ev("dum"), A.min)
    cp(t12("sto"), t12("t5"))
    ts(t12("stg"), st, float(L - 1), A.min)
    cp(IND(X("mm"), t12("sto")), X("zb", 0, C))
    ts(X("ng"), IND(X("gu"), t12("pm")), -1.0, A.mult, 255.0, A.add)
    act(X("y1", 0, C), X("ng"))
    act(X("y2", 0, C), X("ng"))
    ts(X("qf", 0, 13), X("bd", 0, 13), 1.0 / C, A.mult, 0.5 / C - 0.5, A.add)
    cp(X("qi", 0, 13), X("qf", 0, 13))
    ts(X("q192", 0, 13), X("qi", 0, 13), float(C), A.mult)
    tt(X("mf", 0, 13), X("bd", 0, 13), X("q192", 0, 13), A.subtract)
    cp(X("mb", 0, 13), X("mf", 0, 13))
    act(X("mh", 0, 13), X("mf", 0, 13))
    spread("ps2", 208, 16, [X("q192", 0, 13)])
    ts(X("eq"), X("ps2", 0, 208), col("s192"), A.is_equal)
    ts(X("lt"), X("ps2", 0, 208), col("s192"), A.is_gt)
    act(X("gz"), X("ng"), AF.Sign, bias=254.5, scale=-1.0)
    count(X("ps3", 0, 12), "gz", 0, C)
    ts(t12("t1"), X("ps3", 0, 12), 5.0, A.is_gt)
    ts(t12("t4"), ln, 0.5, A.mult, col("s8k"), A.subtract)
    tt(t12("ks"), t12("t1"), t12("t4"), A.add)
    act(X("stc", 0, 12), st, bias=float(Y2 - 1))
    mm([(X("ps3", 16, 28), [(X("ikey"), ev("c24")), (X("idh"), st)]),
        (X("ps3", 28, 40), [(X("ikey"), od("c24")), (X("idh"), t12("e3"))]),
        (X("ps3", 40, 52), [(X("ikey"), ln), (X("idh"), ed)])])
    act(ev("sv"), X("ps3", 16, 28), bias=7.0)
    act(od("sv"), X("ps3", 28, 40), bias=float(XB - 1))
    act(t12("sv0"), st, bias=7.0)
    act(ev("ts"), ln)
    act(X("tp", 0, 25, 2), X("bd", 0, 13), scale=-1.0, bias=float(L))
    act(od("tp"), X("bd", 1, 13), scale=-1.0, bias=float(L))
    act(X("t3", 12, 24), X("bd", 1, 13), bias=float(Y1 - 1))
    tt(t12("t3"), X("ps3", 40, 52), X("t3", 12, 24), A.min)
    cp(t12("pe"), t12("t3"))
    tag[0] = 1
    iota(X("za", 0, 12), [[1, 6], [96, 2]], 0, 0)
    iota(X("za", 12, 24), [[16, 2], [32, 6]], 0, 0)
    act(col("s6"), col("sc"), scale=6.0)
    ts(t12("zu"), X("za", 0, 12), col("s6"), A.add)
    ts(t12("zw"), X("za", 12, 24), col("sc"), A.add)
    cp(X("z2"), X("sp"))
    act(X("ta"), IND(X("z2"), t12("zu")))
    tr(X("tb"), X("ta"))
    act(X("z2"), IND(X("tb"), t12("zw")))
    dmas("s", [(T.nd[u:8:2, :], X("z2", H * u, H * u + H)[0]) for u in range(2)], X("z2")[1], [("nd", 0, L)], "dz", OPT["dma"] + 600)
    dmas("s", [(T.nt[i:128:16, 8:8 + L], T.nd[:]) for i in range(16)], [("nd", 0, L)] + X("au1", 0, W)[1], X("nt", 8, 8 + L)[1],
         "dt", OPT["ntd"])

    def wide(t):
        xx, fl, au = "xx%d" % (t % 2), "fl%d" % (t % 2), "au%d" % t
        cap = "cap%d" % t
        for k in range(L // GCH):
            gat("v" if k in DVE_G[t] else "a", X(xx, GCH * k, GCH * k + GCH),
                IND(X(au), X("so", GCH // 16 * k, GCH // 16 * (k + 1))))
        act(X("sg"), IND(X(xx, 0, L), t12("stg")))
        tt(IND(X(xx), t12("sto")), X("sg"), X("ng"), A.add)
        mm([(X("ps1", 0, C), [(X("hp"), X("m512"))])], stop=False)
        q, last = 0, 0.0
        for buf, parts in PIECES[t]:
            a, b = C * q, C * (q + sum(n for n, _ in parts))
            scan(X(buf, C + a, C + b), X("mm", a, b), X(xx, a, b), last, A.mult, A.add)
            last = X(buf, C + b - 1, C + b)
            for n, e in parts:
                a, b = C * q, C * (q + n)
                if e == "a":
                    act(X(fl, a, b), X(buf, C + a, C + b), AF.Sign, bias=254.5, scale=-1.0)
                else:
                    ts(X(fl, a, b), X(buf, C + a, C + b), 254.5, A.is_lt, 0.5, A.subtract)
                mm([(X("ps0", 0, C), [(sel(u, "big" if e == "a" else "big2"), X(fl, C * u, C * u + C)) for u in range(q, q + n)])],
                   start=q == 0, stop=q + n == 16)
                q += n
        act(X("fd"), X("ps0", 0, C), AF.Sign, bias=-5.0, acc=col("tq"))
        scan(X("cx", 1, 193), X("fd"), X("zb", 0, C), 0.0, A.add, A.add)
        act(X("h2"), X("lt"), scale=col("tq"))
        tt(X("h1"), IND(X("cx", 0, 193), X("mb", 0, 13)), X("eq"), A.mult)
        mm([(X("ps1", 0, C), [(X("hp"), X("h2", 16, 208)), (X("hn"), X("h2", 0, C))])], start=False, stop=False)
        mm([(X("ps1", 0, C), [(X("hp"), X("h1", 16, 208)), (X("hn"), X("h1", 0, C))])], start=False)
        diag(X("kd"), X("ps1", 0, C))
        tt(ev(cap), D16("kd", C), t12("ks"), A.add)
        if t == 1:
            tt(od(cap), ln, ev(cap), A.is_lt)
            act(X("th1"), IND(X("y1"), t12("pe")), scale=-1.0, bias=255.0)

    def second():
        tt(X("pa", 0, 12), ev("ts"), X("stc", 0, 12), A.add)
        mm([(X("ps7", 0, 12), [(X("ikey"), ev("ts")), (X("idh"), ed)])])
        tt(t12("pb"), X("pa", 0, 12), X("ps7", 0, 12), A.min)
        cp(t12("pd"), t12("pb"))
        tt(t12("ea"), t12("en0"), od("ts"), A.mult)
        ts(t12("eau"), t12("ea"), float(W), A.add)
        act(t12("xq"), ev("ts"))

    def second_b():
        act(X("th2"), IND(X("y2"), t12("pd")), bias=-255.0)
        act(X("u1"), IND(X("au2"), t12("eau")))
        mm([(X("ps7", 0, C), [(X("idh"), X("u1")), (X("idh"), X("th2"))])])
        act(X("fa"), X("ps7", 0, C), AF.Sign, bias=-0.5, scale=-1.0)
        act(X("th2"), X("ps7", 0, C), scale=-1.0)
        count(X("ps7", 256, 268), "fa", 0, C)
        ts(t12("f2"), X("ps7", 256, 268), 5.0, A.is_gt)
        act(t12("nf2"), t12("f2"), scale=-1.0, bias=1.0)
        tt(t12("ff"), t12("xq"), ev("cap2"), A.is_lt)
        tt(od("cap2"), t12("ff"), t12("f2"), A.add)

    def visit(t):
        au, mi, cap = "au%d" % t, "mi%d" % t, "cap%d" % t
        rel = TW * (1, 0, 2)[t]
        inn = rel + TI
        m, y, s = ev("kept"), od("kept"), od("ss")
        if t == 0:
            tt(s, ln, ev(cap), A.is_lt)
        else:
            tt(t12("uu"), ev("ts"), ev(cap), A.is_ge)
            if t == 1:
                mm([(X("ps2", 0, 12), [(X("i11"), od("ts")), (X("i22"), t12("uu"))])], stop=False)
            else:
                tt(t12("gv"), od("ts"), y, A.min)
                tt(t12("xp"), t12("gv"), t12("nf2"), A.min)
                mm([(X("ps2", 0, 12), [(X("i11"), od("ts")), (X("j11"), t12("gv")), (X("i22"), t12("uu")),
                                       (X("i22"), t12("xp"))])], stop=False)
        tt(X("kept"), X("ts"), X(cap), A.min)
        tt(X("ro"), X("ts"), X("kept"), A.subtract)
        scan(X("cr", 1, 25), X("ro"), X("z24"), 0.0, A.add, A.add)
        c24 = col("cr", 24)
        mm([(col("ps5"), [(X("trl"), c24)])])
        mm([(col("ps4", 0), [(X("ntrg"), c24)]), (col("ps4", 1), [(X("blk"), c24)])])
        mm([(col("ps3"), [(X("blk"), c24)])], stop=False)
        if t in OPT["zo"]:
            act(X("zo"), X("ro"), AF.Relu, scale=-BIG, bias=BIG)
        else:
            ts(X("zo"), X("ro"), 1.0, A.is_lt, BIG, A.mult)
        tt(X("pre"), X("zo"), X("cr", 0, 24), A.add)
        tt(X("pre"), X("pre"), X("dum"), A.min)
        k = 12 if t == 0 else 24
        if t > 0:
            tt(X("vv"), X("kept"), X("sv"), A.add)
            ts(X("ou"), X("pre"), col("ps5"), A.add)
        else:
            tt(t12("vv"), m, t12("sv0"), A.add)
            ts(t12("ou"), ev("pre"), col("ps5"), A.add)
        act(X("ee", 0, 16 * k), IND(X("vv", 0, k), X("ex", 0, k)), scale=1.0 / 16777216.0)
        w0 = NREL * (2 - t)
        tt(IND(X("wr", w0, w0 + 2 * L + 2 * C + 16), X("ou", 0, k)), X("ee", 0, 16 * k), X("mk", 0, 16 * k), A.mult)
        mm([(X("ps5", 0, NREL), [(X("blk"), X("wr", w0, w0 + NREL))])])
        mm([(X("ps4", 16, 41), [(X("idh"), X("tp", 0, 25)), (X("idh"), X("cr", 0, 25))])])
        if t in OPT["kq"]:
            act(col("rr", 0), col("ps4", 0))
            act(X("kq", 0, 25), X("ps4", 16, 41), bias=col("rr", 0))
        else:
            ts(X("kq", 0, 25), X("ps4", 16, 41), col("ps4", 0), A.add)
        if t in OPT["qa"]:
            act(col("rr", 1), col("ps4", 1), scale=-0.5, bias=TI / 2.0)
            act(col("rr", 2), col("ps4", 1), scale=0.5, bias=TI / 2.0)
        mm([(col("ps4", 2), [(X("nblk"), c24)])], stop=False)
        scan(X("v1"), X("ps5", 0, NREL), X("ones"), 0.0, A.max, A.add)
        diag(X("v2"), X("v1"))
        if t == 0:
            cp(X("rp", 0, 20), D16("v2", NREL))
        else:
            cp(X("rpi", 0, 20), D16("v2", NREL))
            ts(X("rpi", 0, 20), X("rpi", 0, 20), 8191, A.bitwise_and)
            cp(X("rp", 0, 20), X("rpi", 0, 20))
        act(X("tab", rel, rel + NREL), IND(X("nt"), X("rp", 0, 20)))
        remote(r + 1, X("tab", inn, inn + NREL), X("tab", rel, rel + NREL), "rr%d" % t, 163840)
        if t > 0:
            tt(X("fs"), IND(X(au), t12("eb")), X("th%d" % t), A.is_lt)
            count(X("ps2", 0, 12), "fs", 0, C, start=False)
            ts(s, X("ps2", 0, 12), -0.5, A.is_gt)
        scan(X("cs", 1, 25), X("ss"), X("z24"), 0.0, A.add, A.add)
        s24 = col("cs", 24)
        mm([(col("ps3"), [(X("hn"), s24), (X("hn"), s24)])], start=False)
        mm([(col("ps3", 1), [(X("hp"), s24)])])
        mo = "ms%d" % t
        ts(X(mo, 0, 2), X("ps3", 0, 2), 0.0, A.max, 128.0, A.min)
        remote(r + 1, X(mi, 0, 2), X(mo, 0, 2), "rm%d" % t, 1024)
        mm([(col("ps4", 2), [(X("trlh"), s24), (X("trlh"), s24)])], start=False)
        if t in OPT["sq"]:
            act(col("rr", 3), col("ps4", 2))
            act(X("sq", 0, 25), X("cs", 0, 25), bias=col("rr", 3))
        else:
            ts(X("sq", 0, 25), X("cs", 0, 25), col("ps4", 2), A.add)
        tt(X("sk", 0, 25), X("sq", 0, 25), X("kq", 0, 25), A.min)
        if t in OPT["qa"]:
            act(t12("isin"), od("sq"), AF.Sign, bias=0.5)
            act(t12("q0"), t12("isin"), scale=col("rr", 1), bias=col("rr", 2))
        else:
            ts(t12("isin"), od("sq"), 0.0, A.is_ge, float(TI), A.mult)
            ts(t12("q0"), t12("isin"), col("ps4", 1), A.max)
        tt(t12("q0"), t12("q0"), od("sq"), A.add)
        if t == 1:
            tt(t12("xo"), y, t12("g0"), A.mult)
        if t == 2:
            mm([(X("ps4", 48, 60), [(X("idh"), y), (X("idh"), t12("e3"))])])
            cp(t12("xu"), X("ps4", 48, 60))
        if t in OPT["qa"]:
            ts(t12("q1"), t12("isin"), col(mi, 1), A.mult, col(mi, 1), A.add)
        else:
            ts(t12("q1"), t12("isin"), col(mi, 1), A.mult, 2.0 / TI, A.mult)
        tt(t12("q1"), t12("q1"), t12("q0"), A.add)
        cp(t12("gi"), t12("q1"))
        ts(X("mx", 0, 25), X("sk", 0, 25), col(mi), A.min)
        tt(X("tp", 0, 25), X("kq", 0, 25), X("mx", 0, 25), A.subtract)
        tt(X("ts"), X("tp", 0, 24), X("tp", 1, 25), A.subtract)
        gw = IND(X("tab", rel, rel + TW), t12("gi"))
        if t < 2:
            tt(X("gn"), gw, X("md8"), A.add)
            diag(X("gd"), X("gn"))
            ts(t12("eb"), D16("gd", C), col("s8k"), A.subtract)
        if t == 0:
            act(t12("en0"), D16("gd", C), bias=col("s8z"))
            act(t12("g0"), t12("q1"), bias=float(TW))
            act(X("nt", XB, ZN, 3), gw)
            second()
        elif t == 1:
            tt(t12("xo"), t12("xo"), t12("q1"), A.max)
            cp(t12("xu"), t12("xo"))
            act(X("nt", XB + 1, ZN, 3), gw)
            act(X("nt", XB, ZN, 3), IND(X("tab", 0, 2 * TW), t12("xu")))
        else:
            act(X("gg"), gw)
            cp(IND(X("nt", XB, ZN), t12("xu")), X("gg"))

    def final_static():
        iota(X("eb1"), [[2, 12], [1, 2], [24, 16]], 0, 0)
        iota(X("eb2"), [[48, 12], [0, 2], [3, 16]], XB - 8, 0)
        asel(X("eb2"), X("eb2"), [[0, 12], [1, 2], [0, 16]], A.is_gt, 0, 0)
        mm([(X("ps7", 0, 2 * C), [(X("ikey"), X("eb1")), (X("idh"), X("eb2"))])], stop=False)
        mm([(X("ps7", s, 2 * C, 32), [(X("selt", 128 * s, 128 * s + 128), q) for q in (t12("q192"), t12("mh"))])
            for s in range(16)], start=False, stop=False)
        mm([(X("ps7", 0, 16), [(X("hp"), X("zb", 0, 16))])], start=False)
        if OPT["fb"]:
            act(X("vrep"), X("ps7", 0, 2 * C), scale=-1.0, bias=-(KEY + 8.0 + L))
            mm([(X("ps6", 0, 2 * C), [(X("idh"), X("vrep"))])], stop=False)
        else:
            act(X("vrep"), X("ps7", 0, 2 * C), bias=KEY + 8.0 + L)
        iota(X("ta", 0, H), [[1, 16], [32, 3], [128, 2]], 0, 0)
        iota(X("tb", 0, H), [[0, 16], [0, 3], [-224, 2]], 112, 0)
        ts(X("pj", 1, 2), X("pi", 0, 1), 4, A.logical_shift_right, 1, A.bitwise_and)
        cp(col("e1"), X("pj", 1, 2))
        act(X("tb", 0, H), X("tb", 0, H), scale=col("e1"))
        mm([(X("ps7", 0, H), [(X("idh"), X("ta", 0, H)), (X("idh"), X("tb", 0, H)), (X("idh"), X("md8", 0, H))])])
        diag(X("ta", 0, H), X("ps7", 0, H))
        ts(X("tg", 0, 6), D16("ta", H), col("s8k"), A.subtract)
        act(col("sm15"), col("g16"), scale=-1.0, bias=-float(L))

    def final():
        mm([(X("ps0", 0, C), [(X("idh"), X("jd"))])], stop=False)
        act(X("lk"), X("kq", 0, 24), scale=-1.0, bias=float(L))
        tt(X("bbi"), X("mx", 0, 24), X("lk"), A.add)
        ts(X("bbi"), X("bbi"), 15, A.bitwise_and)
        cp(X("b15"), X("bbi"))
        spread("ps7", 2 * C, 16, [X("b15")])
        act(X("bb"), X("tp", 0, 24), scale=-1.0, bias=float(L))
        tt(X("b16"), X("bb"), X("b15"), A.subtract)
        if OPT["fb"]:
            mm([(X("ps6", s, 2 * C, 16), [(X("selt", 128 * s, 128 * s + 128), q) for q in (X("b15"), X("b16"))])
                for s in range(16)], start=False, stop=False)
            mm([(X("ps6", 0, 16), [(X("hp"), X("zb", 0, 16))])], start=False)
        else:
            spread("ps6", 2 * C, 16, [X("b16")])
        act(X("zo"), X("ts"), AF.Relu, scale=-BIG, bias=BIG)
        tt(X("oo"), X("bb"), X("zo"), A.add)
        tt(X("oo"), X("oo"), X("dum"), A.min)
        cp(X("ou"), X("oo"))
        if not OPT["fb"]:
            tt(X("eb1"), X("vrep"), X("ps7", 0, 2 * C), A.subtract)
        act(X("msk"), X("ps7", 0, 2 * C), AF.Sign, scale=-1.0, bias=col("sh"))
        if OPT["fb"]:
            act(X("eb2"), X("ps6", 0, 2 * C), scale=-1.0)
        else:
            tt(X("eb2"), X("eb1"), X("ps6", 0, 2 * C), A.subtract)
        tt(IND(X("xx1"), X("ou")), X("eb2"), X("msk"), A.mult)
        lq = t12("lq")
        tt(lq, ev("ts"), od("ts"), A.add)
        act(t12("lq2"), lq, acc=col("tot"))
        mm([(col("ps3"), [(X("blk"), col("tot"))])])
        act(col("tot", 1), col("ps3"), scale=-BIG, bias=col("g15"))
        act(X("jadj"), X("jd"), AF.Relu, scale=BIG, bias=col("tot", 1))
        mm([(X("ps0", 0, C), [(X("idh"), X("jadj"))])], start=False)
        dma("s", T.yn[:], lq[0], lq[1], [], "dn", 6144)
        for h in range(2):
            a, z, pb, pad, tw = 16 * H * h, 8 + 8 * H * h, ("ps5", "ps1")[h], "np%d" % h, "tt%d" % h
            scan(X("fz", z, z + 8 * H), X("xx1", a, a + 16 * H, 2), X("xx1", a + 1, a + 16 * H, 2),
                 col("fz", z - 1) if h else 0.0, A.max, A.max)
            mm([(X(pb, 0, H), [(X("p15"), X("fz", z - 1, z - 1 + 8 * H, 8))])])
            nn = X("nn", H * h, H * h + H)
            tt(nn, X(pb, 0, H), X("fz", z + 7, z + 8 * H, 8), A.max)
            ts(nn, nn, 8191, A.bitwise_and)
            tt(X(pad, 16, 16 + H), nn, X("ps0", H * h, H * h + H), A.add)
            tr(X(tw, 0, H), X(pad, 16, 16 + H))
            tr(X(tw, H, 2 * H + 32), X(pad))
            ts(X("fo", H * h, H * h + H), IND(X(tw), X("tg", 0, 6)), col("sm15"), A.add, float(NULLC), A.min)
            for e, u, w in FIN[h]:
                gat(e, X("xx0", a + 16 * u, a + 16 * w), IND(X("nt"), X("fo", H * h + u, H * h + w)))
            dma("s", T.yo[:, H * h:H * h + H], T.xx0[0:128:16, a:a + 16 * H], X("xx0", a, a + 16 * H)[1], [], "do%d" % h, 49152, 300)

    for k, (f, t) in enumerate(((wide, 0), (wide, 1), (final_static, None), (visit, 0), (wide, 2), (second_b, None), (visit, 1),
                                (visit, 2), (final, None))):
        tag[0] = 2 + k
        if t is None:
            f()
        else:
            f(t)
    return ops


def _deps(ops):
    hist, deps = {}, []
    for i, o in enumerate(ops):
        d = {}
        for regs, w in ((o[2], False), (o[3], True)):
            for buf, a, b in regs:
                ps = SCRATCH[buf][0] == "psum"
                for j, a2, b2, w2 in hist.get(buf, []):
                    over = a < b2 and a2 < b
                    if ps and o[0] == "p" and ops[j][0] == "p":
                        d.setdefault(j, False)
                    elif over and (w or w2) and not (w and w2 and buf == "nt" and o[8] == 1 and ops[j][8] == 1):
                        d[j] = True
                    elif (over and (w or w2)) or (ps and ops[j][0] != o[0]):
                        d.setdefault(j, False)
        for regs, w in ((o[2], False), (o[3], True)):
            for buf, a, b in regs:
                hist.setdefault(buf, []).append((i, a, b, w))
        deps.append(d)
    return deps


def _place(ops, edges, order, rel):
    n = len(ops)
    fin, busy = [0.0] * n, {}
    for i in order:
        c, t = ops[i][4], rel[i]
        for j, lag in edges[i]:
            t = max(t, fin[j] + lag)
        lst = busy.setdefault(ops[i][0], [(1e18, 1e18)])
        k, hi = 0, len(lst) - 1
        while k < hi:
            m = (k + hi) >> 1
            if lst[m][1] > t:
                hi = m
            else:
                k = m + 1
        while t + c > lst[k][0]:
            t = lst[k][1]
            k += 1
        lst.insert(k, (t, t + c))
        fin[i] = t + c
    return fin


def _random(seed):
    st = [seed]

    def rnd():
        st[0] = (st[0] * 1103515245 + 12345) % 2147483648
        return st[0] / 2147483648.0
    return rnd


def _anneal(ops, fw, bw, cases, start, tries, rnd, marks, hot=50.0, cold=4.0, reach=8):
    n = len(ops)
    after = [[j for j, _ in b] for b in bw]
    ends = [i for i in range(n) if not bw[i]]
    seqs = {}
    for i in sorted(range(n), key=lambda k: (start[k], k)):
        seqs.setdefault(ops[i][0], []).append(i)
    npre = [len(f) for f in fw]

    def times():
        prev, nxt, left = [-1] * n, [-1] * n, list(npre)
        for s in seqs.values():
            for a, b in zip(s, s[1:]):
                prev[b], nxt[a] = a, b
                left[b] += 1
        todo = [i for i in range(n) if left[i] == 0]
        for i in todo:
            for j in after[i]:
                left[j] -= 1
                if left[j] == 0:
                    todo.append(j)
            j = nxt[i]
            if j >= 0:
                left[j] -= 1
                if left[j] == 0:
                    todo.append(j)
        if len(todo) < n:
            return None
        res, total = [], 0.0
        for cost, edges, tail, weight in cases:
            fin, why = [0.0] * n, [-1] * n
            for i in todo:
                t, w = 0.0, -1
                for j, lag in edges[i]:
                    if fin[j] + lag > t:
                        t, w = fin[j] + lag, j
                if prev[i] >= 0 and fin[prev[i]] >= t:
                    t, w = fin[prev[i]], -2 - prev[i]
                fin[i], why[i] = t + cost[i], w
            span, last = max((fin[i] + tail[i], i) for i in ends)
            total += weight * span
            res.append((fin, why, last, span))
        return total + OPT["mu2"] * sum(res[0][0][i] for i in marks), res, total

    best = cur = times()
    for it in range(tries):
        _, why, i, _ = cur[1][int(rnd() * len(cases))]
        links = []
        if rnd() < 0.3:
            i = marks[int(rnd() * len(marks))]
        while i >= 0:
            w = why[i]
            if w <= -2:
                w = -2 - w
                if w >= NF:
                    links.append((w, i))
            i = w
        if not links:
            continue
        u, v = links[int(rnd() * len(links))]
        s = seqs[ops[u][0]]
        a, k = s.index(u), int(rnd() ** 2 * reach)
        if rnd() < 0.5:
            lo = max(a - k, 0)
            while s[lo] < NF:
                lo += 1
            old = s[lo:a + 2]
            s[lo:a + 2] = [v] + old[:-1]
        else:
            lo = a
            old = s[a:a + 2 + k]
            s[a:a + 2 + k] = old[1:] + [u]
        got = times()
        if got is not None and (got[0] <= cur[0] or rnd() < math.exp((cur[0] - got[0]) / (hot * (cold / hot) ** (it / tries)))):
            cur = got
            if got[2] < best[2]:
                best = got
        else:
            s[lo:lo + len(old)] = old
    return [x[3] for x in best[1]], [best[1][0][0][i] - cases[0][0][i] for i in range(n)]


def _schedule(ops, tries, seed, others=()):
    deps = _deps(ops)
    n = len(ops)
    fw, bw = [[] for _ in ops], [[] for _ in ops]
    anc = []
    for i in range(n):
        far = 0
        for j in deps[i]:
            far |= anc[j]
        near = far
        for j in deps[i]:
            near |= 1 << j
        anc.append(near)
        for j, raw in deps[i].items():
            if far >> j & 1 and ops[j][6] is None:
                continue
            lag = (LAG_SAME if raw else 0.0) if (ops[j][0] == ops[i][0] and ops[j][6] is None) else ops[j][5] + LAG_CROSS
            fw[i].append((j, lag))
            bw[j].append((i, lag))
    cost, tail = [o[4] for o in ops], [o[5] for o in ops]
    rnd = _random(seed)
    caps = [POOL["cap%d" % t][:2] for t in range(3)]
    marks = [i for i in range(NF, n) if (ops[i][0] == "g" and ops[i][6]) or any(w[:2] in caps for w in ops[i][3])]

    def forward(rank):
        for i in range(n - 1, -1, -1):
            for j, _ in fw[i]:
                if rank[j] <= rank[i]:
                    rank[j] = rank[i] + 1e-3
        fin = _place(ops, fw, list(range(NF)) + sorted(range(NF, n), key=lambda k: (-rank[k], k)), [0.0] * n)
        span = max(f + t for f, t in zip(fin, tail))
        return span + OPT["mu"] * sum(fin[i] for i in marks), [f - c for f, c in zip(fin, cost)], span

    def backward(st):
        return _place(ops, bw, sorted(range(n), key=lambda k: (-st[k] - cost[k] - tail[k], -k)), tail)

    rank = [0.0] * n
    for i in range(n - 1, -1, -1):
        rank[i] = cost[i] + max([tail[i]] + [rank[j] + lag for j, lag in bw[i]])
    cur = forward(rank)
    for _ in range(4):
        cur = min(cur, forward(backward(cur[1])))
    best = cur
    for it in range(tries):
        st = cur[1]
        back = backward(st)
        end = max(back)
        a = rnd() * cur[2]
        b = a + 2000 + 25000 * rnd() ** 2
        w, amp = rnd(), 3000 * rnd() ** 2
        far = 2000 + 20000 * rnd() ** 2
        shift = [(rnd() - 0.5) * far * (rnd() < 0.4) for _ in range(12)]
        rank = [-(w * (end - back[i]) + (1 - w) * st[i] + shift[ops[i][8]] + amp * rnd() * (cost[i] > 300)) if a <= st[i] < b
                else -st[i] for i in range(n)]
        for k in range(n):
            for j, _ in fw[k]:
                if rank[k] >= rank[j] and not (a <= st[j] < b and rnd() < 0.5):
                    rank[k] = rank[j] - 1e-3
        got = forward(rank)
        if rnd() < 0.5:
            got = min(got, forward(backward(got[1])))
        if got[0] < cur[0] + 600.0 * (1 - it / tries) * rnd():
            cur = got
        best = min(best, got)
    cases = [(cost, fw, tail, 1.0 / (1 + len(others)))]
    for o, same, cross in others:
        edges = [[(j, (same if deps[i][j] else 0.0) if (o[j][0] == o[i][0] and o[j][6] is None) else o[j][5] + cross)
                  for j, _ in fw[i]] for i in range(n)]
        cases.append(([x[4] for x in o], edges, [x[5] for x in o], sum(cost) / sum(x[4] for x in o) / (1 + len(others))))
    best = _anneal(ops, fw, bw, cases, best[1], OPT["moves"], rnd, marks)
    order = sorted(range(n), key=lambda k: (best[1][k], k))
    need, waits, know, seen, pos, cnt = set(), {}, {}, {}, {}, {}
    for i in order:
        q = ops[i][0]
        kn = know.setdefault(q, set())
        w = []
        for j in sorted(deps[i], key=lambda k: -best[1][k]):
            if j in kn or (ops[j][0] == q and ops[j][6] is None and not deps[i][j]):
                continue
            w.append(j)
            need.add(j)
            kn |= seen[j]
        waits[i] = w
        s = set() if (q == "g" and ops[i][6]) else set(kn)
        s.add(i)
        if ops[i][6] is None:
            s |= pos.get(q, set())
            pos[q] = s
        seen[i] = s
    val = {}
    for i in order:
        if ops[i][6] is None and i in need:
            cnt[ops[i][0]] = cnt.get(ops[i][0], 0) + 1
            val[i] = cnt[ops[i][0]]
    return dict(order=order, waits=waits, val=val, cnt=cnt, need=need, span=best[0], start=best[1])


def _cases(g, T, topo, core):
    out, keep = [], dict(OPT)
    for change, same, cross in CASES:
        OPT.update(change)
        out.append((_ops(g, T, topo, core), same, cross))
        OPT.update(keep)
    return out


def rank_program(g, core, T, topo):
    if T.rank_of(core) is None:
        return
    ops = _ops(g, T, topo, core)
    if "p" not in PLAN:
        PLAN["p"] = _schedule(ops, OPT["tries"], OPT["seed"], _cases(g, T, topo, core))
    p = PLAN["p"]
    Q = dict(v=g.vector, a=g.scalar, p=g.tensor, g=g, s=g.sync)
    sent = 0
    for i in p["order"]:
        q, emit, sem, k = ops[i][0], ops[i][1], ops[i][6], ops[i][7]
        top = {}
        for j in p["waits"][i]:
            name, v = (ops[j][6], ops[j][7]) if ops[j][6] else ("q" + ops[j][0], p["val"][j])
            top[name] = max(top.get(name, 0), v)
        for name, v in top.items():
            Q[q].wait_ge(T.sem[name], v)
        ins = emit()
        if sem is None:
            if i in p["val"]:
                ins.then_inc(T.sem["q" + q], 1)
        elif q == "g":
            sent += k
        else:
            ins.then_inc(T.sem[sem], 16)
    g.wait_ge(T.sem.sent, sent)
    for i in p["order"]:
        if ops[i][6] and i not in p["need"]:
            g.sync.wait_ge(T.sem[ops[i][6]], ops[i][7])
